import numpy as np
import ml_dtypes


def mxq(x, axis, fmt="e4m3"):
    dtype, down = {"e4m3": (ml_dtypes.float8_e4m3fn, 7), "e5m2": (ml_dtypes.float8_e5m2, 14)}[fmt]
    v = np.moveaxis(np.asarray(x, np.float32).astype(ml_dtypes.bfloat16).astype(np.float64), axis, -1)
    blocks = v.reshape(v.shape[:-1] + (-1, 32))
    amax = np.abs(blocks).max(-1, keepdims=True)
    byte = np.maximum(np.where(amax > 0, np.frexp(amax)[1] - 1 + 127, 0) - down, 1)
    scale = np.exp2(byte - 127.0)
    codes = (blocks / scale).astype(np.float32).astype(dtype).astype(np.float64)
    return np.moveaxis((codes * scale).reshape(v.shape), -1, axis)


WIDE = False


def mx_kscale(k):
    if not WIDE:
        return np.ones(k)
    levels = np.array([10, -10, 5, -5, 0])
    if k % 512:
        return np.exp2(np.random.permutation(np.resize(levels, k // 32))).repeat(32)
    a = np.empty((k // 512, 16))
    for p in range(k // 512):
        a[p, :8] = np.random.permutation(np.resize(levels, 8))
        for g in range(8):
            far = levels[np.abs(levels - a[p, g]) >= 10]
            a[p, g + 8] = far[np.random.randint(len(far))]
    return np.exp2(a.ravel()).repeat(32)


def f64(x):
    return np.asarray(x).astype(np.float64)


def striped(idx):
    return np.tile(idx.reshape(-1, 16).T, (8, 1)).astype(np.uint16)


def unstriped(offs):
    return offs[:16].T.reshape(-1).astype(np.int64)


E2M1 = np.array([0.0, 0.5, 1.0, 1.5, 2.0, 3.0, 4.0, 6.0, -0.0, -0.5, -1.0, -1.5, -2.0, -3.0, -4.0, -6.0])


def pack_weight(w, fmt):
    k, n = w.shape
    w = f64(np.asarray(w, np.float32).astype(ml_dtypes.bfloat16)).reshape(k // 32, 32, n)
    amax = np.abs(w).max(1)
    if fmt == "e4m3":
        byte = np.frexp(amax)[1] - 1 + 127 - 7
    else:
        mant, ex = np.frexp(amax / 6.0)
        byte = np.where(mant > 0.5, ex, ex - 1) + 127
    byte = np.clip(np.where(amax > 0, byte, 1), 1, 254)
    scaled = (w * np.exp2(127.0 - byte)[:, None, :]).reshape(k, n).astype(np.float32)
    by_word = np.ascontiguousarray(scaled.reshape(k // 512, 128, 4, n).transpose(0, 1, 3, 2))
    if fmt == "e4m3":
        words = by_word.astype(ml_dtypes.float8_e4m3fn).view(np.uint8)
    else:
        c = by_word.astype(ml_dtypes.float4_e2m1fn).view(np.uint8) & 0xF
        words = (c[..., 0::2] | (c[..., 1::2] << 4)).reshape(k // 512, 128, 2 * n)
    return np.ascontiguousarray(words), np.ascontiguousarray(byte.astype(np.uint8).reshape(k // 512, 16, n))


def unpack_weight(words, scales, fmt):
    g, _, n = scales.shape
    words = np.ascontiguousarray(words).reshape(g, 128, n, -1)
    if fmt == "e4m3":
        vals = words.view(ml_dtypes.float8_e4m3fn).astype(np.float64)
    else:
        nib = np.empty((g, 128, n, 4), np.uint8)
        nib[..., 0::2] = words & 0xF
        nib[..., 1::2] = words >> 4
        vals = E2M1[nib]
    vals = vals * np.repeat(np.exp2(scales.astype(np.float64) - 127.0), 8, axis=1)[..., None]
    return vals.transpose(0, 1, 3, 2).reshape(g * 512, n)


def gelu(v):
    return 0.5 * v * (1.0 + np.tanh(np.sqrt(2.0 / np.pi) * (v + 0.044715 * v**3)))


K, H, N, T, S = 512, 1024, 256, 4096, 1536

def setup_inputs():
    n = np.random.standard_normal
    s = mx_kscale(K)[:, None]
    u = mx_kscale(H)[:, None]
    tab_words, tab_scales = pack_weight(n((K, T)) * s, "e4m3")
    tab2_words, tab2_scales = pack_weight(n((K, T)) * s, "e4m3")
    w2_words, w2_scales = pack_weight(n((K, H)) / np.sqrt(K) / s, "e2m1")
    return {
        "tab_words": tab_words, "tab_scales": tab_scales,
        "tab2_words": tab2_words, "tab2_scales": tab2_scales,
        "offs": striped(np.random.permutation(T)[:S]),
        "offs2": striped(np.random.permutation(T)[:S]),
        "w1": (n((K, H)) / np.sqrt(K) / s).astype(np.float32),
        "w2_words": w2_words, "w2_scales": w2_scales,
        "gain": (np.exp(0.3 * n(H)) * u[:, 0]).astype(np.float32),
        "w3": (n((H, N)) / np.sqrt(H) / u).astype(np.float32),
    }

def reference(tab_words, tab_scales, tab2_words, tab2_scales, offs, offs2, w1, w2_words, w2_scales, gain, w3):
    v = unpack_weight(tab_words, tab_scales, "e4m3")[:, unstriped(offs)]
    v2 = unpack_weight(tab2_words, tab2_scales, "e4m3")[:, unstriped(offs2)]
    w1q = mxq(f64(w1), 0, "e4m3")
    w2 = unpack_weight(w2_words, w2_scales, "e2m1")
    d = (w1q.T @ v) - (w2.T @ v2)
    h = np.sqrt(1.0 + np.square(d)) * f64(gain)[:, None]
    hq = mxq(h, 0, "e4m3")
    w3q = mxq(f64(w3), 0, "e4m3")
    return w3q.T @ hq

@@ -1,0 +1,300 @@
+from contextlib import ExitStack
+
+import concourse.mybir as mybir
+from concourse.masks import make_identity
+
+K, H, N, T, S = 512, 1024, 256, 4096, 1536
+FLOPS = 2 * (2 * K * H * S + H * N * S)
+
+F32 = mybir.dt.float32
+BF16 = mybir.dt.bfloat16
+I32 = mybir.dt.int32
+U32 = mybir.dt.uint32
+U16 = mybir.dt.uint16
+U8 = mybir.dt.uint8
+FP8X4 = mybir.dt.float8_e4m3fn_x4
+FP4X4 = mybir.dt.float4_e2m1fn_x4
+ALU = mybir.AluOpType
+ACT = mybir.ActivationFunctionType
+
+P = 128
+PACK = 4
+CHUNK = 512
+CHUNKS = S // CHUNK
+HALVES = H // 512
+V_ROW = 4
+LAST_PIECES = [slice(0, 256), slice(256, 384), slice(384, 512)]
+
+
+def tile_list_flow_residual_refine_kernel(
+    tc, tab_words, tab_scales, tab2_words, tab2_scales, offs, offs2, w1, w2_words, w2_scales, gain, w3, out
+):
+    nc = tc.nc
+    with ExitStack() as ctx:
+        keep = ctx.enter_context(tc.tile_pool(name="keep", bufs=1))
+        ring = ctx.enter_context(tc.tile_pool(name="ring", bufs=2))
+        psum = ctx.enter_context(tc.psum_pool(name="psum", bufs=1))
+
+        list1 = keep.tile([P, S // 16], U16, name="list1")
+        list2 = keep.tile([P, S // 16], U16, name="list2")
+        nc.sync.dma_start(list1[:], offs)
+        nc.sync.dma_start(list2[:], offs2)
+
+        scale_win1 = keep.tile([P, T], U8, name="scale_win1", tag="win1_then_w1")
+        scale_win2 = keep.tile([P, T], U8, name="scale_win2")
+        w2_scale_raw = keep.tile([P, H], U8, name="w2_scale_raw", tag="w2_scales_then_grouped", align_bytes=64)
+        nc.vector.memset(scale_win1[:].bitcast(I32), 0)
+        nc.vector.memset(scale_win2[:].bitcast(I32), 0)
+        nc.vector.memset(w2_scale_raw[:].bitcast(I32), 0)
+
+        warm_in = keep.tile([P, 1], F32, name="warm_in")
+        warm_out = keep.tile([P, 1], F32, name="warm_out")
+        nc.gpsimd.memset(warm_in[:], 1.0)
+
+        def load_scale_rows(queue, plane, first_row, rows):
+            for quad in range(4):
+                row = 32 * quad + first_row
+                queue.dma_start(plane[row : row + 4, :].bitcast(I32), rows[0, 4 * quad : 4 * quad + 4, :].bitcast(I32))
+
+        load_scale_rows(nc.scalar, scale_win1, V_ROW, tab_scales)
+        nc.scalar.activation(warm_out[:], warm_in[:], ACT.Sqrt)
+
+        word_win1 = keep.tile([P, T], I32, name="word_win1")
+        word_win2 = keep.tile([P, T], I32, name="word_win2")
+        w1_rows = w1.rearrange("(p j) r -> p j r", j=PACK)
+        w1_raw0 = keep.tile([P, PACK, 512], F32, name="w1_raw0", tag="w1_then_w3")
+        w2_raw = keep.tile([P, H // 2], I32, name="w2_raw")
+        nc.sync.dma_start(word_win1[:], tab_words[0].rearrange("p t i -> p (t i)").bitcast(I32))
+        nc.sync.dma_start(w1_raw0[:], w1_rows[:, :, 0:512])
+        nc.sync.dma_start(w2_raw[:], w2_words[0].bitcast(I32))
+        nc.sync.dma_start(word_win2[:], tab2_words[0].rearrange("p t i -> p (t i)").bitcast(I32))
+
+        load_scale_rows(nc.gpsimd, scale_win2, 0, tab2_scales)
+        load_scale_rows(nc.gpsimd, w2_scale_raw, 0, w2_scales)
+        gain_sq = keep.tile([P, HALVES * PACK], F32, name="gain_sq")
+        gain_neg = keep.tile([P, HALVES * PACK], F32, name="gain_neg")
+        gain_sign = keep.tile([P, HALVES * PACK], F32, name="gain_sign")
+        identity = keep.tile([P, P], F32, name="identity")
+        make_identity(nc, identity[:])
+        gain_rows = keep.tile([P, P], F32, name="gain_rows")
+        nc.vector.memset(gain_rows[:], 0.0)
+        gain_by_slot = gain.rearrange("(b q t s) -> b t q s", b=HALVES, t=PACK, s=8)
+        for b in range(HALVES):
+            nc.scalar.dma_start(gain_rows[PACK * b : PACK * (b + 1), :], gain_by_slot[b])
+        gain_turned = psum.tile([P, CHUNK], F32, name="gain_turned", tag="d_acc", bufs=6)
+        nc.tensor.transpose(gain_turned[:, 0:P], gain_rows[:], identity[:])
+        gain_cols = keep.tile([P, HALVES * PACK], F32, name="gain_cols")
+        nc.scalar.copy(gain_cols[:], gain_turned[:, 0 : HALVES * PACK])
+        nc.gpsimd.tensor_tensor(gain_sq[:], gain_cols[:], gain_cols[:], ALU.mult)
+        nc.gpsimd.tensor_scalar(gain_neg[:], gain_cols[:], 0.0, -2.0, ALU.is_lt, ALU.mult)
+        nc.gpsimd.tensor_scalar(gain_sign[:], gain_neg[:], 1.0, 1.0, ALU.mult, ALU.add)
+
+        def list_cols(c):
+            return slice(c * CHUNK // 16, (c + 1) * CHUNK // 16)
+
+        def gather_scales(name, window, offsets, c):
+            picked = keep.tile([P, CHUNK], U8, name="%s%d" % (name, c), align_bytes=64)
+            nc.vector.tensor_copy(picked[:], window[:].indirect(offsets[:, list_cols(c)]))
+            return picked
+
+        def gather_words(name, window, offsets, c):
+            picked = keep.tile([P, CHUNK], U32, name="%s%d" % (name, c), tag="%s%d" % (name, c), align_bytes=64)
+            nc.vector.tensor_copy(picked[:], window[:].bitcast(U32).indirect(offsets[:, list_cols(c)]))
+            return picked
+
+        v_scales = [gather_scales("v_scales", scale_win1, list1, c) for c in range(CHUNKS)]
+        v2_scales = [gather_scales("v2_scales", scale_win2, list2, c) for c in range(CHUNKS)]
+        v_words = [gather_words("v_words", word_win1, list1, 0)]
+
+        w1_raw1 = keep.tile([P, PACK, 512], F32, name="w1_raw1", tag="win1_then_w1")
+        nc.sync.dma_start(w1_raw1[:], w1_rows[:, :, 512:1024])
+
+        w2_codes = keep.tile([P, 2 * H], U8, name="w2_codes", align_bytes=64)
+        w2_plane = keep.tile([P, H], U8, name="w2_plane", align_bytes=64)
+        nc.vector.tensor_copy(
+            w2_codes[:].bitcast(I32).rearrange("p (b t q w) -> p b t q w", b=HALVES, t=PACK, w=4),
+            w2_raw[:].rearrange("p (b q t w) -> p b t q w", b=HALVES, t=PACK, w=4),
+        )
+        nc.vector.tensor_copy(
+            w2_plane[:].bitcast(I32).rearrange("p (b t q w) -> p b t q w", b=HALVES, t=PACK, w=2),
+            w2_scale_raw[:].bitcast(I32).rearrange("p (b q t w) -> p b t q w", b=HALVES, t=PACK, w=2),
+        )
+
+        w1_codes = keep.tile([P, H], U32, name="w1_codes", align_bytes=64)
+        w1_plane = keep.tile([P, H], U8, name="w1_plane", align_bytes=64)
+
+        def w1_views(raw, grouped, t):
+            src = raw[:].rearrange("p j (q t s) -> p t q j s", t=PACK, s=8)[:, t]
+            dst = grouped[:, t * 512 : (t + 1) * 512].rearrange("p (q s j) -> p q j s", s=8, j=PACK)
+            return dst, src
+
+        grouped0 = keep.tile([P, PACK * 512], BF16, name="w1_grouped0", align_bytes=64)
+        for t in range(PACK):
+            dst, src = w1_views(w1_raw0, grouped0, t)
+            nc.scalar.activation(dst, src, ACT.Copy, scale=-1.0)
+        for t in range(PACK):
+            cols = slice(t * P, (t + 1) * P)
+            nc.vector.quantize_mx(w1_codes[:, cols].bitcast(FP8X4), w1_plane[:, cols], grouped0[:, t * 512 : (t + 1) * 512])
+
+        v2_words = [gather_words("v2_words", word_win2, list2, 0)]
+
+        w3_raw = keep.tile([P, HALVES, PACK, N], F32, name="w3_raw", tag="w1_then_w3")
+        w3_rows = w3.rearrange("(b q t s) n -> b t q s n", b=HALVES, t=PACK, s=8)
+        for b in range(HALVES):
+            for t in range(PACK):
+                nc.sync.dma_start(w3_raw[:, b, t, :], w3_rows[b, t])
+
+        def prepare_w1_second_half():
+            grouped1 = keep.tile([P, PACK * 512], BF16, name="w1_grouped1", tag="w2_scales_then_grouped", align_bytes=64)
+            for t in range(PACK):
+                dst, src = w1_views(w1_raw1, grouped1, t)
+                nc.vector.tensor_scalar(dst, src, -1.0, None, ALU.mult)
+            return grouped1
+
+        w3_codes = keep.tile([P, HALVES * N], U32, name="w3_codes", align_bytes=64)
+        w3_plane = keep.tile([P, HALVES * N], U8, name="w3_plane", align_bytes=64)
+
+        def prepare_w3():
+            grouped3 = keep.tile([P, HALVES * N * PACK], BF16, name="w3_grouped", tag="w2_scales_then_grouped", align_bytes=64)
+            for b in range(HALVES):
+                sign = gain_sign[:, PACK * b : PACK * (b + 1)].unsqueeze(1).unsqueeze(3).to_broadcast([P, N // 4, PACK, 4])
+                nc.vector.tensor_tensor(
+                    grouped3[:, b * N * PACK : (b + 1) * N * PACK].rearrange("p (c i t) -> p c t i", i=4, t=PACK),
+                    w3_raw[:, b].rearrange("p t (c i) -> p c t i", i=4),
+                    sign,
+                    ALU.mult,
+                )
+            return grouped3
+
+        def first_products(c, b, t):
+            acc = psum.tile([P, CHUNK], F32, name="d_acc", tag="d_acc", bufs=6)
+            cols = slice((PACK * b + t) * P, (PACK * b + t + 1) * P)
+            nc.tensor.matmul_mx(
+                acc[:], w1_codes[:, cols].bitcast(FP8X4), w1_plane[:, cols],
+                v_words[c][:].bitcast(FP8X4), v_scales[c][V_ROW:P, :], start=True, stop=False,
+            )
+            nc.tensor.matmul_mx(
+                acc[:], w2_codes[:, 2 * cols.start : 2 * cols.stop].bitcast(FP4X4), w2_plane[:, cols],
+                v2_words[c][:].bitcast(FP8X4), v2_scales[c][:], start=False, stop=True,
+            )
+            return acc
+
+        def square(acc, tag):
+            if tag is None:
+                sq = ring.tile([P, CHUNK], F32, name="sq", tag="sq", bufs=5)
+            else:
+                sq = keep.tile([P, CHUNK], F32, name="sq_" + tag, tag=tag, align_bytes=64)
+            nc.scalar.activation(sq[:], acc[:], ACT.Square)
+            return sq
+
+        def root(sq, planes, b, t, cols=slice(0, CHUNK)):
+            g2 = gain_sq[:, PACK * b + t : PACK * b + t + 1]
+            nc.scalar.activation(planes[:, t, cols], sq[:, cols], ACT.Sqrt, bias=g2, scale=g2)
+
+        def interleave(planes, cols=slice(0, CHUNK)):
+            width = cols.stop - cols.start
+            grouped = ring.tile([P, width * PACK], BF16, name="h_grouped", align_bytes=64)
+            nc.vector.tensor_copy(
+                grouped[:].rearrange("p (c i t) -> p c t i", i=4, t=PACK),
+                planes[:, :, cols].rearrange("p t (c i) -> p c t i", i=4),
+            )
+            return grouped
+
+        def quantize_h(grouped):
+            width = grouped.shape[1] // PACK
+            codes = ring.tile([P, width], U32, name="h_codes", align_bytes=64, bufs=4)
+            plane = ring.tile([P, width], U8, name="h_plane", align_bytes=64, bufs=4)
+            nc.vector.quantize_mx(codes[:].bitcast(FP8X4), plane[:], grouped[:])
+            return codes, plane
+
+        def last_product(accs, b, codes, plane):
+            for half in range(N // P):
+                cols = slice(b * N + half * P, b * N + (half + 1) * P)
+                nc.tensor.matmul_mx(
+                    accs[half][:], w3_codes[:, cols].bitcast(FP8X4), w3_plane[:, cols],
+                    codes[:].bitcast(FP8X4), plane[:], start=(b == 0), stop=(b == HALVES - 1),
+                )
+
+        def store(accs, c):
+            for half in range(N // P):
+                res = ring.tile([P, CHUNK], F32, name="res", bufs=4)
+                nc.vector.tensor_copy(res[:], accs[half][:])
+                nc.sync.dma_start(out[half * P : (half + 1) * P, c * CHUNK : (c + 1) * CHUNK], res[:])
+
+        units = [(c, b) for c in range(CHUNKS) for b in range(HALVES)]
+        steps = [(u, t) for u in range(len(units)) for t in range(PACK)]
+        planes = {}
+        quantized = {}
+        out_accs = {}
+        pending = None
+        last = len(units) - 1
+        last_squares = []
+        late_tags = ["v_words1", "v2_words1", "v_words2", "v2_words2"]
+
+        def finish_unit(u):
+            quantized[u] = quantize_h(interleave(planes[u]))
+
+        def multiply_unit(u):
+            c, b = units[u]
+            if b == 0:
+                out_accs[c] = [psum.tile([P, CHUNK], F32, name="o_acc%d" % h, tag="o_acc%d" % h) for h in range(N // P)]
+            last_product(out_accs[c], b, *quantized[u])
+            if b == HALVES - 1:
+                store(out_accs[c], c)
+
+        for u, t in steps:
+            c, b = units[u]
+            if t == 0:
+                planes[u] = ring.tile([P, PACK, CHUNK], BF16, name="h_planes", tag="h_planes", bufs=3)
+            sq = square(first_products(c, b, t), late_tags[t] if u == 0 else None)
+            if pending is not None:
+                root(*pending)
+            pending = (sq, planes[u], b, t)
+            if u == last:
+                pending = None
+                last_squares.append(sq)
+            if t == 0 and u >= 1:
+                finish_unit(u - 1)
+            if (u, t) == (0, 0):
+                grouped1 = prepare_w1_second_half()
+                nc.vector.quantize_mx(w1_codes[:, 512:1024].bitcast(FP8X4), w1_plane[:, 512:1024], grouped1[:])
+            if (u, t) == (0, 1):
+                v_words.append(gather_words("v_words", word_win1, list1, 1))
+            if (u, t) == (0, 2):
+                v2_words.append(gather_words("v2_words", word_win2, list2, 1))
+            if (u, t) == (1, 0):
+                grouped3 = prepare_w3()
+                v_words.append(gather_words("v_words", word_win1, list1, 2))
+                nc.vector.quantize_mx(w3_codes[:].bitcast(FP8X4), w3_plane[:], grouped3[:])
+            if (u, t) == (1, 1):
+                v2_words.append(gather_words("v2_words", word_win2, list2, 2))
+            if t == 3 and 1 <= u < last:
+                multiply_unit(u - 1)
+
+        out_halves = out.rearrange("(h p) j -> p h j", p=P)
+        first_col = (CHUNKS - 1) * CHUNK
+        for piece in LAST_PIECES:
+            width = piece.stop - piece.start
+            for t in range(PACK):
+                root(last_squares[t], planes[last], HALVES - 1, t, piece)
+            operands = [
+                (quantized[last - 1][0][:, piece], quantized[last - 1][1][:, piece]),
+                tuple(x[:] for x in quantize_h(interleave(planes[last], piece))),
+            ]
+            acc = psum.tile([P, CHUNK], F32, name="piece_acc", tag="o_acc%d" % (LAST_PIECES.index(piece) % 2))
+            for half in range(N // P):
+                for b in range(HALVES):
+                    cols = slice(b * N + half * P, b * N + (half + 1) * P)
+                    nc.tensor.matmul_mx(
+                        acc[:, half * width : (half + 1) * width], w3_codes[:, cols].bitcast(FP8X4), w3_plane[:, cols],
+                        operands[b][0].bitcast(FP8X4), operands[b][1], start=(b == 0), stop=(b == HALVES - 1),
+                    )
+            res = ring.tile([P, (N // P) * width], F32, name="res", bufs=4)
+            if piece.stop == CHUNK:
+                nc.scalar.copy(res[:], acc[:, 0 : (N // P) * width])
+            else:
+                nc.vector.tensor_copy(res[:], acc[:, 0 : (N // P) * width])
+            nc.sync.dma_start(
+                out_halves[:, :, first_col + piece.start : first_col + piece.stop],
+                res[:].rearrange("p (h j) -> p h j", j=width),
+            )

@@ -22,7 +22,7 @@ PACK = 4
 CHUNK = 512
 CHUNKS = S // CHUNK
 HALVES = H // 512
-V_ROW = 4
+VECTOR_SQUARE_UNITS = (3, 4)
 LAST_PIECES = [slice(0, 256), slice(256, 384), slice(384, 512)]
 
 
@@ -40,12 +40,17 @@ def tile_list_flow_residual_refine_kernel(
         nc.sync.dma_start(list1[:], offs)
         nc.sync.dma_start(list2[:], offs2)
 
-        scale_win1 = keep.tile([P, T], U8, name="scale_win1", tag="win1_then_w1")
-        scale_win2 = keep.tile([P, T], U8, name="scale_win2")
+        scale_win1 = keep.tile([P, T], U8, name="scale_win1")
+        scale_win2 = keep.tile([P, T], U8, name="scale_win2", tag="win1_then_w1")
         w2_scale_raw = keep.tile([P, H], U8, name="w2_scale_raw", tag="w2_scales_then_grouped", align_bytes=64)
-        nc.vector.memset(scale_win1[:].bitcast(I32), 0)
-        nc.vector.memset(scale_win2[:].bitcast(I32), 0)
-        nc.vector.memset(w2_scale_raw[:].bitcast(I32), 0)
+        picked_plane = keep.tile([P, 2 * S], U8, name="picked_plane", align_bytes=64)
+        nc.gpsimd.memset(w2_scale_raw[:].bitcast(I32), 0)
+        for window, rows in ((scale_win1, tab_scales), (scale_win2, tab2_scales)):
+            twice = rows[0].bitcast(I32).unsqueeze(1).to_broadcast([16, 2, T // 4])
+            nc.sync.dma_start(window[0:32, :].bitcast(I32), twice)
+            nc.vector.memset(window[32:64, :].bitcast(I32), 0)
+            nc.vector.memset(window[64:P, :].bitcast(I32), 0)
+        nc.vector.memset(picked_plane[:].bitcast(I32), 0)
 
         warm_in = keep.tile([P, 1], F32, name="warm_in")
         warm_out = keep.tile([P, 1], F32, name="warm_out")
@@ -56,7 +61,6 @@ def tile_list_flow_residual_refine_kernel(
                 row = 32 * quad + first_row
                 queue.dma_start(plane[row : row + 4, :].bitcast(I32), rows[0, 4 * quad : 4 * quad + 4, :].bitcast(I32))
 
-        load_scale_rows(nc.scalar, scale_win1, V_ROW, tab_scales)
         nc.scalar.activation(warm_out[:], warm_in[:], ACT.Sqrt)
 
         word_win1 = keep.tile([P, T], I32, name="word_win1")
@@ -69,7 +73,6 @@ def tile_list_flow_residual_refine_kernel(
         nc.sync.dma_start(w2_raw[:], w2_words[0].bitcast(I32))
         nc.sync.dma_start(word_win2[:], tab2_words[0].rearrange("p t i -> p (t i)").bitcast(I32))
 
-        load_scale_rows(nc.gpsimd, scale_win2, 0, tab2_scales)
         load_scale_rows(nc.gpsimd, w2_scale_raw, 0, w2_scales)
         gain_sq = keep.tile([P, HALVES * PACK], F32, name="gain_sq")
         gain_neg = keep.tile([P, HALVES * PACK], F32, name="gain_neg")
@@ -80,7 +83,7 @@ def tile_list_flow_residual_refine_kernel(
         nc.vector.memset(gain_rows[:], 0.0)
         gain_by_slot = gain.rearrange("(b q t s) -> b t q s", b=HALVES, t=PACK, s=8)
         for b in range(HALVES):
-            nc.scalar.dma_start(gain_rows[PACK * b : PACK * (b + 1), :], gain_by_slot[b])
+            nc.gpsimd.dma_start(gain_rows[PACK * b : PACK * (b + 1), :], gain_by_slot[b])
         gain_turned = psum.tile([P, CHUNK], F32, name="gain_turned", tag="d_acc", bufs=6)
         nc.tensor.transpose(gain_turned[:, 0:P], gain_rows[:], identity[:])
         gain_cols = keep.tile([P, HALVES * PACK], F32, name="gain_cols")
@@ -92,19 +95,20 @@ def tile_list_flow_residual_refine_kernel(
         def list_cols(c):
             return slice(c * CHUNK // 16, (c + 1) * CHUNK // 16)
 
-        def gather_scales(name, window, offsets, c):
-            picked = keep.tile([P, CHUNK], U8, name="%s%d" % (name, c), align_bytes=64)
-            nc.vector.tensor_copy(picked[:], window[:].indirect(offsets[:, list_cols(c)]))
-            return picked
-
         def gather_words(name, window, offsets, c):
             picked = keep.tile([P, CHUNK], U32, name="%s%d" % (name, c), tag="%s%d" % (name, c), align_bytes=64)
             nc.vector.tensor_copy(picked[:], window[:].bitcast(U32).indirect(offsets[:, list_cols(c)]))
             return picked
 
-        v_scales = [gather_scales("v_scales", scale_win1, list1, c) for c in range(CHUNKS)]
-        v2_scales = [gather_scales("v2_scales", scale_win2, list2, c) for c in range(CHUNKS)]
-        v_words = [gather_words("v_words", word_win1, list1, 0)]
+        picked_rows = keep.tile([P, 2 * S], U8, name="picked_rows", align_bytes=64)
+        nc.vector.tensor_copy(picked_rows[:, 0:S], scale_win1[:].indirect(list1[:]))
+        nc.vector.tensor_copy(picked_rows[:, S : 2 * S], scale_win2[:].indirect(list2[:]))
+        for quad in range(4):
+            nc.scalar.dma_start(
+                picked_plane[32 * quad : 32 * quad + 4, :].bitcast(I32),
+                picked_rows[8 * quad : 8 * quad + 8 : 2, :].bitcast(I32),
+            )
+        v_words = [gather_words("v_words", word_win1, list1, c) for c in range(2)]
 
         w1_raw1 = keep.tile([P, PACK, 512], F32, name="w1_raw1", tag="win1_then_w1")
         nc.sync.dma_start(w1_raw1[:], w1_rows[:, :, 512:1024])
@@ -171,11 +175,11 @@ def tile_list_flow_residual_refine_kernel(
             cols = slice((PACK * b + t) * P, (PACK * b + t + 1) * P)
             nc.tensor.matmul_mx(
                 acc[:], w1_codes[:, cols].bitcast(FP8X4), w1_plane[:, cols],
-                v_words[c][:].bitcast(FP8X4), v_scales[c][V_ROW:P, :], start=True, stop=False,
+                v_words[c][:].bitcast(FP8X4), picked_plane[:, c * CHUNK : (c + 1) * CHUNK], start=True, stop=False,
             )
             nc.tensor.matmul_mx(
                 acc[:], w2_codes[:, 2 * cols.start : 2 * cols.stop].bitcast(FP4X4), w2_plane[:, cols],
-                v2_words[c][:].bitcast(FP8X4), v2_scales[c][:], start=False, stop=True,
+                v2_words[c][:].bitcast(FP8X4), picked_plane[:, S + c * CHUNK : S + (c + 1) * CHUNK], start=False, stop=True,
             )
             return acc
 
@@ -185,6 +189,13 @@ def tile_list_flow_residual_refine_kernel(
             else:
                 sq = keep.tile([P, CHUNK], F32, name="sq_" + tag, tag=tag, align_bytes=64)
             nc.scalar.activation(sq[:], acc[:], ACT.Square)
+            return sq
+
+        def square_on_vector(acc):
+            d = ring.tile([P, CHUNK], F32, name="d_copy")
+            nc.vector.tensor_copy(d[:], acc[:])
+            sq = ring.tile([P, CHUNK], F32, name="sq_vector")
+            nc.vector.tensor_tensor(sq[:], acc[:], d[:], ALU.mult)
             return sq
 
         def root(sq, planes, b, t, cols=slice(0, CHUNK)):
@@ -229,7 +240,7 @@ def tile_list_flow_residual_refine_kernel(
         pending = None
         last = len(units) - 1
         last_squares = []
-        late_tags = ["v_words1", "v2_words1", "v_words2", "v2_words2"]
+        late_tags = ["v2_words1", "v_words2", "v2_words2", None]
 
         def finish_unit(u):
             quantized[u] = quantize_h(interleave(planes[u]))
@@ -246,21 +257,27 @@ def tile_list_flow_residual_refine_kernel(
             c, b = units[u]
             if t == 0:
                 planes[u] = ring.tile([P, PACK, CHUNK], BF16, name="h_planes", tag="h_planes", bufs=3)
-            sq = square(first_products(c, b, t), late_tags[t] if u == 0 else None)
+            on_vector = t == 0 and u in VECTOR_SQUARE_UNITS
+            if on_vector:
+                sq = square_on_vector(first_products(c, b, t))
+            else:
+                sq = square(first_products(c, b, t), late_tags[t] if u == 0 else None)
             if pending is not None:
                 root(*pending)
             pending = (sq, planes[u], b, t)
             if u == last:
                 pending = None
                 last_squares.append(sq)
+            elif on_vector:
+                deferred, pending = pending, None
+            elif t == PACK - 1 and u in VECTOR_SQUARE_UNITS:
+                root(*deferred)
             if t == 0 and u >= 1:
                 finish_unit(u - 1)
             if (u, t) == (0, 0):
                 grouped1 = prepare_w1_second_half()
                 nc.vector.quantize_mx(w1_codes[:, 512:1024].bitcast(FP8X4), w1_plane[:, 512:1024], grouped1[:])
             if (u, t) == (0, 1):
-                v_words.append(gather_words("v_words", word_win1, list1, 1))
-            if (u, t) == (0, 2):
                 v2_words.append(gather_words("v2_words", word_win2, list2, 1))
             if (u, t) == (1, 0):
                 grouped3 = prepare_w3()

@@ -22,7 +22,8 @@ PACK = 4
 CHUNK = 512
 CHUNKS = S // CHUNK
 HALVES = H // 512
-VECTOR_SQUARE_UNITS = (3, 4)
+RUN = 4
+VECTOR_SQUARE_UNITS = (3, 4, 5)
 LAST_PIECES = [slice(0, 256), slice(256, 384), slice(384, 512)]
 
 
@@ -42,19 +43,21 @@ def tile_list_flow_residual_refine_kernel(
 
         scale_win1 = keep.tile([P, T], U8, name="scale_win1")
         scale_win2 = keep.tile([P, T], U8, name="scale_win2", tag="win1_then_w1")
-        w2_scale_raw = keep.tile([P, H], U8, name="w2_scale_raw", tag="w2_scales_then_grouped", align_bytes=64)
+        w2_scale_raw = keep.tile([P, H], U8, name="w2_scale_raw")
         picked_plane = keep.tile([P, 2 * S], U8, name="picked_plane", align_bytes=64)
+        gain_rows = keep.tile([P, P], F32, name="gain_rows")
         nc.gpsimd.memset(w2_scale_raw[:].bitcast(I32), 0)
-        for window, rows in ((scale_win1, tab_scales), (scale_win2, tab2_scales)):
+        nc.gpsimd.memset(gain_rows[:], 0.0)
+        for window, rows, engine in ((scale_win1, tab_scales, nc.vector), (scale_win2, tab2_scales, nc.gpsimd)):
             twice = rows[0].bitcast(I32).unsqueeze(1).to_broadcast([16, 2, T // 4])
             nc.sync.dma_start(window[0:32, :].bitcast(I32), twice)
-            nc.vector.memset(window[32:64, :].bitcast(I32), 0)
-            nc.vector.memset(window[64:P, :].bitcast(I32), 0)
-        nc.vector.memset(picked_plane[:].bitcast(I32), 0)
+            engine.memset(window[32:64, :].bitcast(I32), 0)
+            engine.memset(window[64:P, :].bitcast(I32), 0)
 
+        nc.vector.memset(picked_plane[:].bitcast(I32), 0)
         warm_in = keep.tile([P, 1], F32, name="warm_in")
         warm_out = keep.tile([P, 1], F32, name="warm_out")
-        nc.gpsimd.memset(warm_in[:], 1.0)
+        nc.vector.memset(warm_in[:], 1.0)
 
         def load_scale_rows(queue, plane, first_row, rows):
             for quad in range(4):
@@ -69,21 +72,19 @@ def tile_list_flow_residual_refine_kernel(
         w1_raw0 = keep.tile([P, PACK, 512], F32, name="w1_raw0", tag="w1_then_w3")
         w2_raw = keep.tile([P, H // 2], I32, name="w2_raw")
         nc.sync.dma_start(word_win1[:], tab_words[0].rearrange("p t i -> p (t i)").bitcast(I32))
+        load_scale_rows(nc.sync, w2_scale_raw, 0, w2_scales)
         nc.sync.dma_start(w1_raw0[:], w1_rows[:, :, 0:512])
         nc.sync.dma_start(w2_raw[:], w2_words[0].bitcast(I32))
         nc.sync.dma_start(word_win2[:], tab2_words[0].rearrange("p t i -> p (t i)").bitcast(I32))
 
-        load_scale_rows(nc.gpsimd, w2_scale_raw, 0, w2_scales)
         gain_sq = keep.tile([P, HALVES * PACK], F32, name="gain_sq")
         gain_neg = keep.tile([P, HALVES * PACK], F32, name="gain_neg")
         gain_sign = keep.tile([P, HALVES * PACK], F32, name="gain_sign")
         identity = keep.tile([P, P], F32, name="identity")
         make_identity(nc, identity[:])
-        gain_rows = keep.tile([P, P], F32, name="gain_rows")
-        nc.vector.memset(gain_rows[:], 0.0)
-        gain_by_slot = gain.rearrange("(b q t s) -> b t q s", b=HALVES, t=PACK, s=8)
+        gain_by_slot = gain.rearrange("(b u t e) -> b t u e", b=HALVES, t=PACK, e=RUN)
         for b in range(HALVES):
-            nc.gpsimd.dma_start(gain_rows[PACK * b : PACK * (b + 1), :], gain_by_slot[b])
+            nc.scalar.dma_start(gain_rows[PACK * b : PACK * (b + 1), :], gain_by_slot[b])
         gain_turned = psum.tile([P, CHUNK], F32, name="gain_turned", tag="d_acc", bufs=6)
         nc.tensor.transpose(gain_turned[:, 0:P], gain_rows[:], identity[:])
         gain_cols = keep.tile([P, HALVES * PACK], F32, name="gain_cols")
@@ -104,7 +105,7 @@ def tile_list_flow_residual_refine_kernel(
         nc.vector.tensor_copy(picked_rows[:, 0:S], scale_win1[:].indirect(list1[:]))
         nc.vector.tensor_copy(picked_rows[:, S : 2 * S], scale_win2[:].indirect(list2[:]))
         for quad in range(4):
-            nc.scalar.dma_start(
+            nc.sync.dma_start(
                 picked_plane[32 * quad : 32 * quad + 4, :].bitcast(I32),
                 picked_rows[8 * quad : 8 * quad + 8 : 2, :].bitcast(I32),
             )
@@ -116,42 +117,43 @@ def tile_list_flow_residual_refine_kernel(
         w2_codes = keep.tile([P, 2 * H], U8, name="w2_codes", align_bytes=64)
         w2_plane = keep.tile([P, H], U8, name="w2_plane", align_bytes=64)
         nc.vector.tensor_copy(
-            w2_codes[:].bitcast(I32).rearrange("p (b t q w) -> p b t q w", b=HALVES, t=PACK, w=4),
-            w2_raw[:].rearrange("p (b q t w) -> p b t q w", b=HALVES, t=PACK, w=4),
+            w2_codes[:].bitcast(I32).rearrange("p (b t u w) -> p b t u w", b=HALVES, t=PACK, w=2),
+            w2_raw[:].rearrange("p (b u t w) -> p b t u w", b=HALVES, t=PACK, w=2),
         )
         nc.vector.tensor_copy(
-            w2_plane[:].bitcast(I32).rearrange("p (b t q w) -> p b t q w", b=HALVES, t=PACK, w=2),
-            w2_scale_raw[:].bitcast(I32).rearrange("p (b q t w) -> p b t q w", b=HALVES, t=PACK, w=2),
+            w2_plane[:].bitcast(I32).rearrange("p (b t u) -> p b t u", b=HALVES, t=PACK),
+            w2_scale_raw[:].bitcast(I32).rearrange("p (b u t) -> p b t u", b=HALVES, t=PACK),
         )
 
         w1_codes = keep.tile([P, H], U32, name="w1_codes", align_bytes=64)
         w1_plane = keep.tile([P, H], U8, name="w1_plane", align_bytes=64)
 
         def w1_views(raw, grouped, t):
-            src = raw[:].rearrange("p j (q t s) -> p t q j s", t=PACK, s=8)[:, t]
-            dst = grouped[:, t * 512 : (t + 1) * 512].rearrange("p (q s j) -> p q j s", s=8, j=PACK)
+            src = raw[:].rearrange("p j (u t e) -> p t u j e", t=PACK, e=RUN)[:, t]
+            dst = grouped.rearrange("p (u e j) -> p u j e", e=RUN, j=PACK)
             return dst, src
 
-        grouped0 = keep.tile([P, PACK * 512], BF16, name="w1_grouped0", align_bytes=64)
+        first_tags = ["w1_grouped00", "v2_words0", "v2_words1", "v2_words2"]
+        grouped0 = [keep.tile([P, 512], BF16, name="w1_grouped0%d" % t, tag=first_tags[t], align_bytes=64) for t in range(PACK)]
         for t in range(PACK):
-            dst, src = w1_views(w1_raw0, grouped0, t)
+            dst, src = w1_views(w1_raw0, grouped0[t][:], t)
             nc.scalar.activation(dst, src, ACT.Copy, scale=-1.0)
         for t in range(PACK):
             cols = slice(t * P, (t + 1) * P)
-            nc.vector.quantize_mx(w1_codes[:, cols].bitcast(FP8X4), w1_plane[:, cols], grouped0[:, t * 512 : (t + 1) * 512])
+            nc.vector.quantize_mx(w1_codes[:, cols].bitcast(FP8X4), w1_plane[:, cols], grouped0[t][:])
 
-        v2_words = [gather_words("v2_words", word_win2, list2, 0)]
+        v2_words = [gather_words("v2_words", word_win2, list2, c) for c in range(CHUNKS)]
 
         w3_raw = keep.tile([P, HALVES, PACK, N], F32, name="w3_raw", tag="w1_then_w3")
-        w3_rows = w3.rearrange("(b q t s) n -> b t q s n", b=HALVES, t=PACK, s=8)
+        w3_rows = w3.rearrange("(b u t e) n -> b t u e n", b=HALVES, t=PACK, e=RUN)
         for b in range(HALVES):
             for t in range(PACK):
                 nc.sync.dma_start(w3_raw[:, b, t, :], w3_rows[b, t])
 
         def prepare_w1_second_half():
-            grouped1 = keep.tile([P, PACK * 512], BF16, name="w1_grouped1", tag="w2_scales_then_grouped", align_bytes=64)
+            grouped1 = keep.tile([P, PACK * 512], BF16, name="w1_grouped1", tag="grouped", align_bytes=64)
             for t in range(PACK):
-                dst, src = w1_views(w1_raw1, grouped1, t)
+                dst, src = w1_views(w1_raw1, grouped1[:, t * 512 : (t + 1) * 512], t)
                 nc.vector.tensor_scalar(dst, src, -1.0, None, ALU.mult)
             return grouped1
 
@@ -159,7 +161,7 @@ def tile_list_flow_residual_refine_kernel(
         w3_plane = keep.tile([P, HALVES * N], U8, name="w3_plane", align_bytes=64)
 
         def prepare_w3():
-            grouped3 = keep.tile([P, HALVES * N * PACK], BF16, name="w3_grouped", tag="w2_scales_then_grouped", align_bytes=64)
+            grouped3 = keep.tile([P, HALVES * N * PACK], BF16, name="w3_grouped", tag="grouped", align_bytes=64)
             for b in range(HALVES):
                 sign = gain_sign[:, PACK * b : PACK * (b + 1)].unsqueeze(1).unsqueeze(3).to_broadcast([P, N // 4, PACK, 4])
                 nc.vector.tensor_tensor(
@@ -174,12 +176,12 @@ def tile_list_flow_residual_refine_kernel(
             acc = psum.tile([P, CHUNK], F32, name="d_acc", tag="d_acc", bufs=6)
             cols = slice((PACK * b + t) * P, (PACK * b + t + 1) * P)
             nc.tensor.matmul_mx(
-                acc[:], w1_codes[:, cols].bitcast(FP8X4), w1_plane[:, cols],
-                v_words[c][:].bitcast(FP8X4), picked_plane[:, c * CHUNK : (c + 1) * CHUNK], start=True, stop=False,
+                acc[:], w2_codes[:, 2 * cols.start : 2 * cols.stop].bitcast(FP4X4), w2_plane[:, cols],
+                v2_words[c][:].bitcast(FP8X4), picked_plane[:, S + c * CHUNK : S + (c + 1) * CHUNK], start=True, stop=False,
             )
             nc.tensor.matmul_mx(
-                acc[:], w2_codes[:, 2 * cols.start : 2 * cols.stop].bitcast(FP4X4), w2_plane[:, cols],
-                v2_words[c][:].bitcast(FP8X4), picked_plane[:, S + c * CHUNK : S + (c + 1) * CHUNK], start=False, stop=True,
+                acc[:], w1_codes[:, cols].bitcast(FP8X4), w1_plane[:, cols],
+                v_words[c][:].bitcast(FP8X4), picked_plane[:, c * CHUNK : (c + 1) * CHUNK], start=False, stop=True,
             )
             return acc
 
@@ -232,7 +234,7 @@ def tile_list_flow_residual_refine_kernel(
                 nc.vector.tensor_copy(res[:], accs[half][:])
                 nc.sync.dma_start(out[half * P : (half + 1) * P, c * CHUNK : (c + 1) * CHUNK], res[:])
 
-        units = [(c, b) for c in range(CHUNKS) for b in range(HALVES)]
+        units = [(0, 0), (1, 0), (0, 1), (1, 1), (2, 0), (2, 1)]
         steps = [(u, t) for u in range(len(units)) for t in range(PACK)]
         planes = {}
         quantized = {}
@@ -240,18 +242,18 @@ def tile_list_flow_residual_refine_kernel(
         pending = None
         last = len(units) - 1
         last_squares = []
-        late_tags = ["v2_words1", "v_words2", "v2_words2", None]
+        late_tags = ["grouped", "v_words2", None, None]
 
         def finish_unit(u):
             quantized[u] = quantize_h(interleave(planes[u]))
 
         def multiply_unit(u):
             c, b = units[u]
-            if b == 0:
-                out_accs[c] = [psum.tile([P, CHUNK], F32, name="o_acc%d" % h, tag="o_acc%d" % h) for h in range(N // P)]
-            last_product(out_accs[c], b, *quantized[u])
             if b == HALVES - 1:
-                store(out_accs[c], c)
+                accs = [psum.tile([P, CHUNK], F32, name="o_acc%d" % h, tag="o_acc%d" % h) for h in range(N // P)]
+                for half_of_r in range(HALVES):
+                    last_product(accs, half_of_r, *quantized[units.index((c, half_of_r))])
+                store(accs, c)
 
         for u, t in steps:
             c, b = units[u]
@@ -274,17 +276,15 @@ def tile_list_flow_residual_refine_kernel(
                 root(*deferred)
             if t == 0 and u >= 1:
                 finish_unit(u - 1)
-            if (u, t) == (0, 0):
+            if (u, t) == (0, 1):
                 grouped1 = prepare_w1_second_half()
                 nc.vector.quantize_mx(w1_codes[:, 512:1024].bitcast(FP8X4), w1_plane[:, 512:1024], grouped1[:])
-            if (u, t) == (0, 1):
-                v2_words.append(gather_words("v2_words", word_win2, list2, 1))
+            if (u, t) == (0, 2):
+                v_words.append(gather_words("v_words", word_win1, list1, 2))
             if (u, t) == (1, 0):
                 grouped3 = prepare_w3()
-                v_words.append(gather_words("v_words", word_win1, list1, 2))
+            if (u, t) == (2, 0):
                 nc.vector.quantize_mx(w3_codes[:].bitcast(FP8X4), w3_plane[:], grouped3[:])
-            if (u, t) == (1, 1):
-                v2_words.append(gather_words("v2_words", word_win2, list2, 2))
             if t == 3 and 1 <= u < last:
                 multiply_unit(u - 1)
 

@@ -23,7 +23,7 @@ CHUNK = 512
 CHUNKS = S // CHUNK
 HALVES = H // 512
 RUN = 4
-VECTOR_SQUARE_UNITS = (3, 4, 5)
+VECTOR_SQUARE_UNITS = (3, 4)
 LAST_PIECES = [slice(0, 256), slice(256, 384), slice(384, 512)]
 
 
@@ -72,7 +72,6 @@ def tile_list_flow_residual_refine_kernel(
         w1_raw0 = keep.tile([P, PACK, 512], F32, name="w1_raw0", tag="w1_then_w3")
         w2_raw = keep.tile([P, H // 2], I32, name="w2_raw")
         nc.sync.dma_start(word_win1[:], tab_words[0].rearrange("p t i -> p (t i)").bitcast(I32))
-        load_scale_rows(nc.sync, w2_scale_raw, 0, w2_scales)
         nc.sync.dma_start(w1_raw0[:], w1_rows[:, :, 0:512])
         nc.sync.dma_start(w2_raw[:], w2_words[0].bitcast(I32))
         nc.sync.dma_start(word_win2[:], tab2_words[0].rearrange("p t i -> p (t i)").bitcast(I32))
@@ -82,6 +81,7 @@ def tile_list_flow_residual_refine_kernel(
         gain_sign = keep.tile([P, HALVES * PACK], F32, name="gain_sign")
         identity = keep.tile([P, P], F32, name="identity")
         make_identity(nc, identity[:])
+        load_scale_rows(nc.gpsimd, w2_scale_raw, 0, w2_scales)
         gain_by_slot = gain.rearrange("(b u t e) -> b t u e", b=HALVES, t=PACK, e=RUN)
         for b in range(HALVES):
             nc.scalar.dma_start(gain_rows[PACK * b : PACK * (b + 1), :], gain_by_slot[b])

@@ -16,6 +16,7 @@ FP8X4 = mybir.dt.float8_e4m3fn_x4
 FP4X4 = mybir.dt.float4_e2m1fn_x4
 ALU = mybir.AluOpType
 ACT = mybir.ActivationFunctionType
+AXIS = mybir.AxisListType
 
 P = 128
 PACK = 4
@@ -23,7 +24,9 @@ CHUNK = 512
 CHUNKS = S // CHUNK
 HALVES = H // 512
 RUN = 4
-VECTOR_SQUARE_UNITS = (3, 4)
+SCALE_ROWS = 16
+FIRST_ROW = P - SCALE_ROWS
+VECTOR_SQUARE_UNITS = (3, 4, 5)
 LAST_PIECES = [slice(0, 256), slice(256, 384), slice(384, 512)]
 
 
@@ -38,57 +41,58 @@ def tile_list_flow_residual_refine_kernel(
 
         list1 = keep.tile([P, S // 16], U16, name="list1")
         list2 = keep.tile([P, S // 16], U16, name="list2")
-        nc.sync.dma_start(list1[:], offs)
-        nc.sync.dma_start(list2[:], offs2)
-
         scale_win1 = keep.tile([P, T], U8, name="scale_win1")
-        scale_win2 = keep.tile([P, T], U8, name="scale_win2", tag="win1_then_w1")
-        w2_scale_raw = keep.tile([P, H], U8, name="w2_scale_raw")
+        scale_win2 = keep.tile([P, T], U8, name="scale_win2", tag="scales_then_w1")
+        nc.sync.dma_start(list1[:], offs)
+        nc.sync.dma_start(scale_win1[FIRST_ROW:P, :].bitcast(I32), tab_scales[0].bitcast(I32))
+        nc.sync.dma_start(list2[:], offs2)
+        nc.sync.dma_start(scale_win2[FIRST_ROW:P, :].bitcast(I32), tab2_scales[0].bitcast(I32))
+        nc.vector.memset(scale_win1[0:FIRST_ROW, :].bitcast(I32), 0)
+        nc.vector.memset(scale_win2[0:FIRST_ROW, :].bitcast(I32), 0)
         picked_plane = keep.tile([P, 2 * S], U8, name="picked_plane", align_bytes=64)
-        gain_rows = keep.tile([P, P], F32, name="gain_rows")
-        nc.gpsimd.memset(w2_scale_raw[:].bitcast(I32), 0)
-        nc.gpsimd.memset(gain_rows[:], 0.0)
-        for window, rows, engine in ((scale_win1, tab_scales, nc.vector), (scale_win2, tab2_scales, nc.gpsimd)):
-            twice = rows[0].bitcast(I32).unsqueeze(1).to_broadcast([16, 2, T // 4])
-            nc.sync.dma_start(window[0:32, :].bitcast(I32), twice)
-            engine.memset(window[32:64, :].bitcast(I32), 0)
-            engine.memset(window[64:P, :].bitcast(I32), 0)
 
-        nc.vector.memset(picked_plane[:].bitcast(I32), 0)
         warm_in = keep.tile([P, 1], F32, name="warm_in")
         warm_out = keep.tile([P, 1], F32, name="warm_out")
         nc.vector.memset(warm_in[:], 1.0)
-
-        def load_scale_rows(queue, plane, first_row, rows):
-            for quad in range(4):
-                row = 32 * quad + first_row
-                queue.dma_start(plane[row : row + 4, :].bitcast(I32), rows[0, 4 * quad : 4 * quad + 4, :].bitcast(I32))
-
         nc.scalar.activation(warm_out[:], warm_in[:], ACT.Sqrt)
 
-        word_win1 = keep.tile([P, T], I32, name="word_win1")
-        word_win2 = keep.tile([P, T], I32, name="word_win2")
+        word_win1 = keep.tile([P, T], I32, name="word_win1", tag="words_then_w3")
         w1_rows = w1.rearrange("(p j) r -> p j r", j=PACK)
-        w1_raw0 = keep.tile([P, PACK, 512], F32, name="w1_raw0", tag="w1_then_w3")
+        w1_raw0 = keep.tile([P, PACK, 512], F32, name="w1_raw0")
         w2_raw = keep.tile([P, H // 2], I32, name="w2_raw")
-        nc.sync.dma_start(word_win1[:], tab_words[0].rearrange("p t i -> p (t i)").bitcast(I32))
-        nc.sync.dma_start(w1_raw0[:], w1_rows[:, :, 0:512])
+        gain_rows = keep.tile([P, HALVES * P], F32, name="gain_rows", tag="gain_then_words")
+        nc.sync.dma_start(
+            gain_rows[P - PACK : P, :].rearrange("t (u e) -> t u e", e=RUN),
+            gain.rearrange("(u t e) -> t u e", t=PACK, e=RUN),
+        )
+        nc.gpsimd.memset(gain_rows[0 : P - PACK, :], 0.0)
         nc.sync.dma_start(w2_raw[:], w2_words[0].bitcast(I32))
-        nc.sync.dma_start(word_win2[:], tab2_words[0].rearrange("p t i -> p (t i)").bitcast(I32))
+        nc.sync.dma_start(w1_raw0[:], w1_rows[:, :, 0:512])
+        nc.sync.dma_start(word_win1[:], tab_words[0].rearrange("p t i -> p (t i)").bitcast(I32))
 
+        w2_scale_raw = keep.tile([P, H], U8, name="w2_scale_raw")
+        nc.gpsimd.memset(w2_scale_raw[:].bitcast(I32), 0)
+        for quad in range(4):
+            nc.sync.dma_start(
+                w2_scale_raw[32 * quad : 32 * quad + 4, :].bitcast(I32),
+                w2_scales[0, 4 * quad : 4 * quad + 4, :].bitcast(I32),
+            )
+        identity = keep.tile([P, P], F32, name="identity")
+        make_identity(nc, identity[:])
+        nc.gpsimd.memset(picked_plane[:].bitcast(I32), 0)
+        gain_turned = psum.tile([P, CHUNK], F32, name="gain_turned", tag="d_acc", bufs=6)
+        for b in range(HALVES):
+            nc.tensor.transpose(gain_turned[:, b * P : (b + 1) * P], gain_rows[:, b * P : (b + 1) * P], identity[:])
+        word_win2 = keep.tile([P, T], I32, name="word_win2", tag="gain_then_words")
+        nc.sync.dma_start(word_win2[:], tab2_words[0].rearrange("p t i -> p (t i)").bitcast(I32))
+        gain_cols = keep.tile([P, HALVES * PACK], F32, name="gain_cols")
         gain_sq = keep.tile([P, HALVES * PACK], F32, name="gain_sq")
         gain_neg = keep.tile([P, HALVES * PACK], F32, name="gain_neg")
         gain_sign = keep.tile([P, HALVES * PACK], F32, name="gain_sign")
-        identity = keep.tile([P, P], F32, name="identity")
-        make_identity(nc, identity[:])
-        load_scale_rows(nc.gpsimd, w2_scale_raw, 0, w2_scales)
-        gain_by_slot = gain.rearrange("(b u t e) -> b t u e", b=HALVES, t=PACK, e=RUN)
-        for b in range(HALVES):
-            nc.scalar.dma_start(gain_rows[PACK * b : PACK * (b + 1), :], gain_by_slot[b])
-        gain_turned = psum.tile([P, CHUNK], F32, name="gain_turned", tag="d_acc", bufs=6)
-        nc.tensor.transpose(gain_turned[:, 0:P], gain_rows[:], identity[:])
-        gain_cols = keep.tile([P, HALVES * PACK], F32, name="gain_cols")
-        nc.scalar.copy(gain_cols[:], gain_turned[:, 0 : HALVES * PACK])
+        nc.scalar.copy(
+            gain_cols[:].rearrange("p (b t) -> p b t", t=PACK),
+            gain_turned[:, 0 : HALVES * P].rearrange("p (b x) -> p b x", x=P)[:, :, P - PACK : P],
+        )
         nc.gpsimd.tensor_tensor(gain_sq[:], gain_cols[:], gain_cols[:], ALU.mult)
         nc.gpsimd.tensor_scalar(gain_neg[:], gain_cols[:], 0.0, -2.0, ALU.is_lt, ALU.mult)
         nc.gpsimd.tensor_scalar(gain_sign[:], gain_neg[:], 1.0, 1.0, ALU.mult, ALU.add)
@@ -105,14 +109,27 @@ def tile_list_flow_residual_refine_kernel(
         nc.vector.tensor_copy(picked_rows[:, 0:S], scale_win1[:].indirect(list1[:]))
         nc.vector.tensor_copy(picked_rows[:, S : 2 * S], scale_win2[:].indirect(list2[:]))
         for quad in range(4):
-            nc.sync.dma_start(
-                picked_plane[32 * quad : 32 * quad + 4, :].bitcast(I32),
-                picked_rows[8 * quad : 8 * quad + 8 : 2, :].bitcast(I32),
+            row = FIRST_ROW + 4 * quad
+            nc.scalar.dma_start(
+                picked_plane[32 * quad : 32 * quad + 4, :].bitcast(I32), picked_rows[row : row + 4, :].bitcast(I32)
             )
-        v_words = [gather_words("v_words", word_win1, list1, c) for c in range(2)]
 
-        w1_raw1 = keep.tile([P, PACK, 512], F32, name="w1_raw1", tag="win1_then_w1")
+        w1_raw1 = keep.tile([P, PACK, 512], F32, name="w1_raw1", tag="scales_then_w1")
         nc.sync.dma_start(w1_raw1[:], w1_rows[:, :, 512:1024])
+
+        w1_codes = keep.tile([P, H], U32, name="w1_codes", align_bytes=64)
+        w1_plane = keep.tile([P, H], U8, name="w1_plane", align_bytes=64)
+
+        def w1_views(raw, grouped, t):
+            src = raw[:].rearrange("p j (u t e) -> p t u j e", t=PACK, e=RUN)[:, t]
+            dst = grouped[:, t * 512 : (t + 1) * 512].rearrange("p (u e j) -> p u j e", e=RUN, j=PACK)
+            return dst, src
+
+        grouped0 = keep.tile([P, PACK * 512], BF16, name="w1_grouped0", tag="grouped", align_bytes=64)
+        for t in range(PACK):
+            dst, src = w1_views(w1_raw0, grouped0, t)
+            nc.scalar.activation(dst, src, ACT.Copy, scale=-1.0)
+        nc.vector.quantize_mx(w1_codes[:, 0:512].bitcast(FP8X4), w1_plane[:, 0:512], grouped0[:])
 
         w2_codes = keep.tile([P, 2 * H], U8, name="w2_codes", align_bytes=64)
         w2_plane = keep.tile([P, H], U8, name="w2_plane", align_bytes=64)
@@ -125,42 +142,28 @@ def tile_list_flow_residual_refine_kernel(
             w2_scale_raw[:].bitcast(I32).rearrange("p (b u t) -> p b t u", b=HALVES, t=PACK),
         )
 
-        w1_codes = keep.tile([P, H], U32, name="w1_codes", align_bytes=64)
-        w1_plane = keep.tile([P, H], U8, name="w1_plane", align_bytes=64)
-
-        def w1_views(raw, grouped, t):
-            src = raw[:].rearrange("p j (u t e) -> p t u j e", t=PACK, e=RUN)[:, t]
-            dst = grouped.rearrange("p (u e j) -> p u j e", e=RUN, j=PACK)
-            return dst, src
-
-        first_tags = ["w1_grouped00", "v2_words0", "v2_words1", "v2_words2"]
-        grouped0 = [keep.tile([P, 512], BF16, name="w1_grouped0%d" % t, tag=first_tags[t], align_bytes=64) for t in range(PACK)]
-        for t in range(PACK):
-            dst, src = w1_views(w1_raw0, grouped0[t][:], t)
-            nc.scalar.activation(dst, src, ACT.Copy, scale=-1.0)
-        for t in range(PACK):
-            cols = slice(t * P, (t + 1) * P)
-            nc.vector.quantize_mx(w1_codes[:, cols].bitcast(FP8X4), w1_plane[:, cols], grouped0[t][:])
-
+        v_words = [gather_words("v_words", word_win1, list1, c) for c in range(CHUNKS - 1)]
         v2_words = [gather_words("v2_words", word_win2, list2, c) for c in range(CHUNKS)]
-
-        w3_raw = keep.tile([P, HALVES, PACK, N], F32, name="w3_raw", tag="w1_then_w3")
-        w3_rows = w3.rearrange("(b u t e) n -> b t u e n", b=HALVES, t=PACK, e=RUN)
-        for b in range(HALVES):
-            for t in range(PACK):
-                nc.sync.dma_start(w3_raw[:, b, t, :], w3_rows[b, t])
 
         def prepare_w1_second_half():
             grouped1 = keep.tile([P, PACK * 512], BF16, name="w1_grouped1", tag="grouped", align_bytes=64)
             for t in range(PACK):
-                dst, src = w1_views(w1_raw1, grouped1[:, t * 512 : (t + 1) * 512], t)
+                dst, src = w1_views(w1_raw1, grouped1, t)
                 nc.vector.tensor_scalar(dst, src, -1.0, None, ALU.mult)
             return grouped1
 
         w3_codes = keep.tile([P, HALVES * N], U32, name="w3_codes", align_bytes=64)
         w3_plane = keep.tile([P, HALVES * N], U8, name="w3_plane", align_bytes=64)
 
-        def prepare_w3():
+        def load_w3():
+            raw = keep.tile([P, HALVES, PACK, N], F32, name="w3_raw", tag="words_then_w3")
+            rows = w3.rearrange("(b u t e) n -> b t u e n", b=HALVES, t=PACK, e=RUN)
+            for b in range(HALVES):
+                for t in range(PACK):
+                    nc.sync.dma_start(raw[:, b, t, :], rows[b, t])
+            return raw
+
+        def prepare_w3(w3_raw):
             grouped3 = keep.tile([P, HALVES * N * PACK], BF16, name="w3_grouped", tag="grouped", align_bytes=64)
             for b in range(HALVES):
                 sign = gain_sign[:, PACK * b : PACK * (b + 1)].unsqueeze(1).unsqueeze(3).to_broadcast([P, N // 4, PACK, 4])
@@ -176,12 +179,12 @@ def tile_list_flow_residual_refine_kernel(
             acc = psum.tile([P, CHUNK], F32, name="d_acc", tag="d_acc", bufs=6)
             cols = slice((PACK * b + t) * P, (PACK * b + t + 1) * P)
             nc.tensor.matmul_mx(
-                acc[:], w2_codes[:, 2 * cols.start : 2 * cols.stop].bitcast(FP4X4), w2_plane[:, cols],
-                v2_words[c][:].bitcast(FP8X4), picked_plane[:, S + c * CHUNK : S + (c + 1) * CHUNK], start=True, stop=False,
+                acc[:], w1_codes[:, cols].bitcast(FP8X4), w1_plane[:, cols],
+                v_words[c][:].bitcast(FP8X4), picked_plane[:, c * CHUNK : (c + 1) * CHUNK], start=True, stop=False,
             )
             nc.tensor.matmul_mx(
-                acc[:], w1_codes[:, cols].bitcast(FP8X4), w1_plane[:, cols],
-                v_words[c][:].bitcast(FP8X4), picked_plane[:, c * CHUNK : (c + 1) * CHUNK], start=False, stop=True,
+                acc[:], w2_codes[:, 2 * cols.start : 2 * cols.stop].bitcast(FP4X4), w2_plane[:, cols],
+                v2_words[c][:].bitcast(FP8X4), picked_plane[:, S + c * CHUNK : S + (c + 1) * CHUNK], start=False, stop=True,
             )
             return acc
 
@@ -194,123 +197,100 @@ def tile_list_flow_residual_refine_kernel(
             return sq
 
         def square_on_vector(acc):
-            d = ring.tile([P, CHUNK], F32, name="d_copy")
-            nc.vector.tensor_copy(d[:], acc[:])
             sq = ring.tile([P, CHUNK], F32, name="sq_vector")
-            nc.vector.tensor_tensor(sq[:], acc[:], d[:], ALU.mult)
+            nc.vector.tensor_reduce(sq[:], acc[:].unsqueeze(2).to_broadcast([P, CHUNK, 2]), AXIS.X, ALU.mult)
             return sq
 
         def root(sq, planes, b, t, cols=slice(0, CHUNK)):
             g2 = gain_sq[:, PACK * b + t : PACK * b + t + 1]
             nc.scalar.activation(planes[:, t, cols], sq[:, cols], ACT.Sqrt, bias=g2, scale=g2)
 
-        def interleave(planes, cols=slice(0, CHUNK)):
+        def interleave(planes, cols):
             width = cols.stop - cols.start
-            grouped = ring.tile([P, width * PACK], BF16, name="h_grouped", align_bytes=64)
+            grouped = ring.tile([P, width * PACK], BF16, name="h_grouped", align_bytes=64, bufs=3)
             nc.vector.tensor_copy(
                 grouped[:].rearrange("p (c i t) -> p c t i", i=4, t=PACK),
                 planes[:, :, cols].rearrange("p t (c i) -> p c t i", i=4),
             )
             return grouped
 
-        def quantize_h(grouped):
-            width = grouped.shape[1] // PACK
-            codes = ring.tile([P, width], U32, name="h_codes", align_bytes=64, bufs=4)
-            plane = ring.tile([P, width], U8, name="h_plane", align_bytes=64, bufs=4)
-            nc.vector.quantize_mx(codes[:].bitcast(FP8X4), plane[:], grouped[:])
-            return codes, plane
+        h_codes = [keep.tile([P, CHUNK], U32, name="h_codes%d" % u, align_bytes=64) for u in range(CHUNKS * HALVES)]
+        h_plane = [keep.tile([P, CHUNK], U8, name="h_plane%d" % u, align_bytes=64) for u in range(CHUNKS * HALVES)]
 
-        def last_product(accs, b, codes, plane):
-            for half in range(N // P):
-                cols = slice(b * N + half * P, b * N + (half + 1) * P)
+        def quantize_h(u, grouped, cols):
+            nc.vector.quantize_mx(h_codes[u][:, cols].bitcast(FP8X4), h_plane[u][:, cols], grouped[:])
+
+        def last_products(acc, c, half, cols):
+            for b in range(HALVES):
+                w_cols = slice(b * N + half * P, b * N + (half + 1) * P)
+                u = b * CHUNKS + c
                 nc.tensor.matmul_mx(
-                    accs[half][:], w3_codes[:, cols].bitcast(FP8X4), w3_plane[:, cols],
-                    codes[:].bitcast(FP8X4), plane[:], start=(b == 0), stop=(b == HALVES - 1),
+                    acc, w3_codes[:, w_cols].bitcast(FP8X4), w3_plane[:, w_cols],
+                    h_codes[u][:, cols].bitcast(FP8X4), h_plane[u][:, cols], start=(b == 0), stop=(b == HALVES - 1),
                 )
 
-        def store(accs, c):
+        def multiply_chunk(c):
             for half in range(N // P):
+                acc = psum.tile([P, CHUNK], F32, name="o_acc%d" % half, tag="o_acc%d" % half)
+                last_products(acc[:], c, half, slice(0, CHUNK))
                 res = ring.tile([P, CHUNK], F32, name="res", bufs=4)
-                nc.vector.tensor_copy(res[:], accs[half][:])
+                nc.vector.tensor_copy(res[:], acc[:])
                 nc.sync.dma_start(out[half * P : (half + 1) * P, c * CHUNK : (c + 1) * CHUNK], res[:])
 
-        units = [(0, 0), (1, 0), (0, 1), (1, 1), (2, 0), (2, 1)]
-        steps = [(u, t) for u in range(len(units)) for t in range(PACK)]
         planes = {}
-        quantized = {}
-        out_accs = {}
-        pending = None
-        last = len(units) - 1
-        last_squares = []
-        late_tags = ["grouped", "v_words2", None, None]
 
         def finish_unit(u):
-            quantized[u] = quantize_h(interleave(planes[u]))
+            parts = [slice(0, CHUNK // 2), slice(CHUNK // 2, CHUNK)]
+            grouped = [interleave(planes[u], cols) for cols in parts]
+            for part, cols in zip(grouped, parts):
+                quantize_h(u, part, cols)
 
-        def multiply_unit(u):
-            c, b = units[u]
-            if b == HALVES - 1:
-                accs = [psum.tile([P, CHUNK], F32, name="o_acc%d" % h, tag="o_acc%d" % h) for h in range(N // P)]
-                for half_of_r in range(HALVES):
-                    last_product(accs, half_of_r, *quantized[units.index((c, half_of_r))])
-                store(accs, c)
-
-        for u, t in steps:
-            c, b = units[u]
-            if t == 0:
-                planes[u] = ring.tile([P, PACK, CHUNK], BF16, name="h_planes", tag="h_planes", bufs=3)
-            on_vector = t == 0 and u in VECTOR_SQUARE_UNITS
-            if on_vector:
-                sq = square_on_vector(first_products(c, b, t))
-            else:
-                sq = square(first_products(c, b, t), late_tags[t] if u == 0 else None)
-            if pending is not None:
-                root(*pending)
-            pending = (sq, planes[u], b, t)
-            if u == last:
-                pending = None
-                last_squares.append(sq)
-            elif on_vector:
-                deferred, pending = pending, None
-            elif t == PACK - 1 and u in VECTOR_SQUARE_UNITS:
-                root(*deferred)
-            if t == 0 and u >= 1:
-                finish_unit(u - 1)
-            if (u, t) == (0, 1):
-                grouped1 = prepare_w1_second_half()
-                nc.vector.quantize_mx(w1_codes[:, 512:1024].bitcast(FP8X4), w1_plane[:, 512:1024], grouped1[:])
-            if (u, t) == (0, 2):
-                v_words.append(gather_words("v_words", word_win1, list1, 2))
-            if (u, t) == (1, 0):
-                grouped3 = prepare_w3()
-            if (u, t) == (2, 0):
-                nc.vector.quantize_mx(w3_codes[:].bitcast(FP8X4), w3_plane[:], grouped3[:])
-            if t == 3 and 1 <= u < last:
-                multiply_unit(u - 1)
+        units = [(c, b) for b in range(HALVES) for c in range(CHUNKS)]
+        last = len(units) - 1
+        pending = []
+        for u, (c, b) in enumerate(units):
+            planes[u] = ring.tile([P, PACK, CHUNK], BF16, name="h_planes", tag="h_planes", bufs=3)
+            deferred = []
+            for t in range(PACK):
+                acc = first_products(c, b, t)
+                if t == 0 and u in VECTOR_SQUARE_UNITS:
+                    deferred = [(square_on_vector(acc), planes[u], b, t)]
+                    fresh = []
+                else:
+                    fresh = [(square(acc, "v_words2" if (u, t) == (0, 0) else None), planes[u], b, t)]
+                if u < last or t == 0:
+                    for args in pending:
+                        root(*args)
+                    pending = []
+                pending = pending + fresh
+                if t == 0 and u >= 1:
+                    finish_unit(u - 1)
+                if (u, t) == (0, 1):
+                    v_words.append(gather_words("v_words", word_win1, list1, CHUNKS - 1))
+                    w3_raw = load_w3()
+                    grouped1 = prepare_w1_second_half()
+                    nc.vector.quantize_mx(w1_codes[:, 512:1024].bitcast(FP8X4), w1_plane[:, 512:1024], grouped1[:])
+                if (u, t) == (1, 3):
+                    grouped3 = prepare_w3(w3_raw)
+                if (u, t) == (2, 3):
+                    nc.vector.quantize_mx(w3_codes[:].bitcast(FP8X4), w3_plane[:], grouped3[:])
+                if t == 1 and u > CHUNKS:
+                    multiply_chunk(u - 1 - CHUNKS)
+            pending = pending + deferred
 
         out_halves = out.rearrange("(h p) j -> p h j", p=P)
         first_col = (CHUNKS - 1) * CHUNK
         for piece in LAST_PIECES:
+            for args in pending:
+                root(*args, piece)
+        for index, piece in enumerate(LAST_PIECES):
             width = piece.stop - piece.start
-            for t in range(PACK):
-                root(last_squares[t], planes[last], HALVES - 1, t, piece)
-            operands = [
-                (quantized[last - 1][0][:, piece], quantized[last - 1][1][:, piece]),
-                tuple(x[:] for x in quantize_h(interleave(planes[last], piece))),
-            ]
-            acc = psum.tile([P, CHUNK], F32, name="piece_acc", tag="o_acc%d" % (LAST_PIECES.index(piece) % 2))
+            quantize_h(last, interleave(planes[last], piece), piece)
+            acc = psum.tile([P, CHUNK], F32, name="piece_acc", tag=["o_acc0", "o_acc1", "d_acc"][index], bufs=[1, 1, 6][index])
             for half in range(N // P):
-                for b in range(HALVES):
-                    cols = slice(b * N + half * P, b * N + (half + 1) * P)
-                    nc.tensor.matmul_mx(
-                        acc[:, half * width : (half + 1) * width], w3_codes[:, cols].bitcast(FP8X4), w3_plane[:, cols],
-                        operands[b][0].bitcast(FP8X4), operands[b][1], start=(b == 0), stop=(b == HALVES - 1),
-                    )
+                last_products(acc[:, half * width : (half + 1) * width], CHUNKS - 1, half, piece)
             res = ring.tile([P, (N // P) * width], F32, name="res", bufs=4)
-            if piece.stop == CHUNK:
-                nc.scalar.copy(res[:], acc[:, 0 : (N // P) * width])
-            else:
-                nc.vector.tensor_copy(res[:], acc[:, 0 : (N // P) * width])
+            nc.scalar.copy(res[:], acc[:, 0 : (N // P) * width])
             nc.sync.dma_start(
                 out_halves[:, :, first_col + piece.start : first_col + piece.stop],
                 res[:].rearrange("p (h j) -> p h j", j=width),

@@ -26,7 +26,7 @@ HALVES = H // 512
 RUN = 4
 SCALE_ROWS = 16
 FIRST_ROW = P - SCALE_ROWS
-VECTOR_SQUARE_UNITS = (3, 4, 5)
+VECTOR_SQUARE_UNITS = (2, 3, 4, 5)
 LAST_PIECES = [slice(0, 256), slice(256, 384), slice(384, 512)]
 
 
@@ -39,10 +39,12 @@ def tile_list_flow_residual_refine_kernel(
         ring = ctx.enter_context(tc.tile_pool(name="ring", bufs=2))
         psum = ctx.enter_context(tc.psum_pool(name="psum", bufs=1))
 
+        w2_scale_raw = keep.tile([P, H], U8, name="w2_scale_raw")
+        nc.gpsimd.memset(w2_scale_raw[:].bitcast(I32), 0)
         list1 = keep.tile([P, S // 16], U16, name="list1")
         list2 = keep.tile([P, S // 16], U16, name="list2")
         scale_win1 = keep.tile([P, T], U8, name="scale_win1")
-        scale_win2 = keep.tile([P, T], U8, name="scale_win2", tag="scales_then_w1")
+        scale_win2 = keep.tile([P, T], U8, name="scale_win2")
         nc.sync.dma_start(list1[:], offs)
         nc.sync.dma_start(scale_win1[FIRST_ROW:P, :].bitcast(I32), tab_scales[0].bitcast(I32))
         nc.sync.dma_start(list2[:], offs2)
@@ -58,40 +60,40 @@ def tile_list_flow_residual_refine_kernel(
 
         word_win1 = keep.tile([P, T], I32, name="word_win1", tag="words_then_w3")
         w1_rows = w1.rearrange("(p j) r -> p j r", j=PACK)
-        w1_raw0 = keep.tile([P, PACK, 512], F32, name="w1_raw0")
+        w1_raw0 = keep.tile([P, PACK, 512], F32, name="w1_raw0", tag="w1_raw")
         w2_raw = keep.tile([P, H // 2], I32, name="w2_raw")
-        gain_rows = keep.tile([P, HALVES * P], F32, name="gain_rows", tag="gain_then_words")
-        nc.sync.dma_start(
-            gain_rows[P - PACK : P, :].rearrange("t (u e) -> t u e", e=RUN),
-            gain.rearrange("(u t e) -> t u e", t=PACK, e=RUN),
-        )
-        nc.gpsimd.memset(gain_rows[0 : P - PACK, :], 0.0)
+        gain_rows = keep.tile([P, 512], F32, name="gain_rows")
+        nc.sync.dma_start(gain_rows[P - HALVES : P, :], gain.rearrange("(b r) -> b r", b=HALVES))
+        nc.gpsimd.memset(gain_rows[0 : P - HALVES, :], 0.0)
         nc.sync.dma_start(w2_raw[:], w2_words[0].bitcast(I32))
         nc.sync.dma_start(w1_raw0[:], w1_rows[:, :, 0:512])
         nc.sync.dma_start(word_win1[:], tab_words[0].rearrange("p t i -> p (t i)").bitcast(I32))
 
-        w2_scale_raw = keep.tile([P, H], U8, name="w2_scale_raw")
-        nc.gpsimd.memset(w2_scale_raw[:].bitcast(I32), 0)
         for quad in range(4):
             nc.sync.dma_start(
                 w2_scale_raw[32 * quad : 32 * quad + 4, :].bitcast(I32),
                 w2_scales[0, 4 * quad : 4 * quad + 4, :].bitcast(I32),
             )
+        word_win2 = keep.tile([P, T], I32, name="word_win2")
+        nc.sync.dma_start(word_win2[:], tab2_words[0].rearrange("p t i -> p (t i)").bitcast(I32))
         identity = keep.tile([P, P], F32, name="identity")
         make_identity(nc, identity[:])
         nc.gpsimd.memset(picked_plane[:].bitcast(I32), 0)
         gain_turned = psum.tile([P, CHUNK], F32, name="gain_turned", tag="d_acc", bufs=6)
-        for b in range(HALVES):
-            nc.tensor.transpose(gain_turned[:, b * P : (b + 1) * P], gain_rows[:, b * P : (b + 1) * P], identity[:])
-        word_win2 = keep.tile([P, T], I32, name="word_win2", tag="gain_then_words")
-        nc.sync.dma_start(word_win2[:], tab2_words[0].rearrange("p t i -> p (t i)").bitcast(I32))
+        gain_dealt = keep.tile([P, 512], F32, name="gain_dealt")
+        nc.scalar.copy(
+            gain_dealt[:].rearrange("p (t u e) -> p t u e", t=PACK, e=RUN),
+            gain_rows[:].rearrange("p (u t e) -> p t u e", t=PACK, e=RUN),
+        )
+        for t in range(PACK):
+            nc.tensor.transpose(gain_turned[:, t * P : (t + 1) * P], gain_dealt[:, t * P : (t + 1) * P], identity[:])
         gain_cols = keep.tile([P, HALVES * PACK], F32, name="gain_cols")
         gain_sq = keep.tile([P, HALVES * PACK], F32, name="gain_sq")
         gain_neg = keep.tile([P, HALVES * PACK], F32, name="gain_neg")
         gain_sign = keep.tile([P, HALVES * PACK], F32, name="gain_sign")
         nc.scalar.copy(
             gain_cols[:].rearrange("p (b t) -> p b t", t=PACK),
-            gain_turned[:, 0 : HALVES * P].rearrange("p (b x) -> p b x", x=P)[:, :, P - PACK : P],
+            gain_turned[:].rearrange("p (t x) -> p x t", x=P)[:, P - HALVES : P, :],
         )
         nc.gpsimd.tensor_tensor(gain_sq[:], gain_cols[:], gain_cols[:], ALU.mult)
         nc.gpsimd.tensor_scalar(gain_neg[:], gain_cols[:], 0.0, -2.0, ALU.is_lt, ALU.mult)
@@ -110,12 +112,9 @@ def tile_list_flow_residual_refine_kernel(
         nc.vector.tensor_copy(picked_rows[:, S : 2 * S], scale_win2[:].indirect(list2[:]))
         for quad in range(4):
             row = FIRST_ROW + 4 * quad
-            nc.scalar.dma_start(
+            nc.sync.dma_start(
                 picked_plane[32 * quad : 32 * quad + 4, :].bitcast(I32), picked_rows[row : row + 4, :].bitcast(I32)
             )
-
-        w1_raw1 = keep.tile([P, PACK, 512], F32, name="w1_raw1", tag="scales_then_w1")
-        nc.sync.dma_start(w1_raw1[:], w1_rows[:, :, 512:1024])
 
         w1_codes = keep.tile([P, H], U32, name="w1_codes", align_bytes=64)
         w1_plane = keep.tile([P, H], U8, name="w1_plane", align_bytes=64)
@@ -129,6 +128,8 @@ def tile_list_flow_residual_refine_kernel(
         for t in range(PACK):
             dst, src = w1_views(w1_raw0, grouped0, t)
             nc.scalar.activation(dst, src, ACT.Copy, scale=-1.0)
+        w1_raw1 = keep.tile([P, PACK, 512], F32, name="w1_raw1", tag="w1_raw")
+        nc.sync.dma_start(w1_raw1[:], w1_rows[:, :, 512:1024])
         nc.vector.quantize_mx(w1_codes[:, 0:512].bitcast(FP8X4), w1_plane[:, 0:512], grouped0[:])
 
         w2_codes = keep.tile([P, 2 * H], U8, name="w2_codes", align_bytes=64)
@@ -178,14 +179,17 @@ def tile_list_flow_residual_refine_kernel(
         def first_products(c, b, t):
             acc = psum.tile([P, CHUNK], F32, name="d_acc", tag="d_acc", bufs=6)
             cols = slice((PACK * b + t) * P, (PACK * b + t + 1) * P)
-            nc.tensor.matmul_mx(
-                acc[:], w1_codes[:, cols].bitcast(FP8X4), w1_plane[:, cols],
-                v_words[c][:].bitcast(FP8X4), picked_plane[:, c * CHUNK : (c + 1) * CHUNK], start=True, stop=False,
-            )
-            nc.tensor.matmul_mx(
-                acc[:], w2_codes[:, 2 * cols.start : 2 * cols.stop].bitcast(FP4X4), w2_plane[:, cols],
-                v2_words[c][:].bitcast(FP8X4), picked_plane[:, S + c * CHUNK : S + (c + 1) * CHUNK], start=False, stop=True,
-            )
+            passes = [
+                (w2_codes[:, 2 * cols.start : 2 * cols.stop].bitcast(FP4X4), w2_plane, v2_words, S),
+                (w1_codes[:, cols].bitcast(FP8X4), w1_plane, v_words, 0),
+            ]
+            if (c, b) == (0, 0) and t < 2:
+                passes = passes[::-1]
+            for index, (codes, plane, words, first) in enumerate(passes):
+                nc.tensor.matmul_mx(
+                    acc[:], codes, plane[:, cols], words[c][:].bitcast(FP8X4),
+                    picked_plane[:, first + c * CHUNK : first + (c + 1) * CHUNK], start=(index == 0), stop=(index == 1),
+                )
             return acc
 
         def square(acc, tag):
@@ -220,19 +224,19 @@ def tile_list_flow_residual_refine_kernel(
         def quantize_h(u, grouped, cols):
             nc.vector.quantize_mx(h_codes[u][:, cols].bitcast(FP8X4), h_plane[u][:, cols], grouped[:])
 
-        def last_products(acc, c, half, cols):
-            for b in range(HALVES):
-                w_cols = slice(b * N + half * P, b * N + (half + 1) * P)
-                u = b * CHUNKS + c
-                nc.tensor.matmul_mx(
-                    acc, w3_codes[:, w_cols].bitcast(FP8X4), w3_plane[:, w_cols],
-                    h_codes[u][:, cols].bitcast(FP8X4), h_plane[u][:, cols], start=(b == 0), stop=(b == HALVES - 1),
-                )
+        def last_product(acc, c, half, b, cols, start, stop):
+            w_cols = slice(b * N + half * P, b * N + (half + 1) * P)
+            u = b * CHUNKS + c
+            nc.tensor.matmul_mx(
+                acc, w3_codes[:, w_cols].bitcast(FP8X4), w3_plane[:, w_cols],
+                h_codes[u][:, cols].bitcast(FP8X4), h_plane[u][:, cols], start=start, stop=stop,
+            )
 
         def multiply_chunk(c):
             for half in range(N // P):
                 acc = psum.tile([P, CHUNK], F32, name="o_acc%d" % half, tag="o_acc%d" % half)
-                last_products(acc[:], c, half, slice(0, CHUNK))
+                for b in range(HALVES):
+                    last_product(acc[:], c, half, b, slice(0, CHUNK), b == 0, b == HALVES - 1)
                 res = ring.tile([P, CHUNK], F32, name="res", bufs=4)
                 nc.vector.tensor_copy(res[:], acc[:])
                 nc.sync.dma_start(out[half * P : (half + 1) * P, c * CHUNK : (c + 1) * CHUNK], res[:])
@@ -287,11 +291,14 @@ def tile_list_flow_residual_refine_kernel(
             width = piece.stop - piece.start
             quantize_h(last, interleave(planes[last], piece), piece)
             acc = psum.tile([P, CHUNK], F32, name="piece_acc", tag=["o_acc0", "o_acc1", "d_acc"][index], bufs=[1, 1, 6][index])
-            for half in range(N // P):
-                last_products(acc[:, half * width : (half + 1) * width], CHUNKS - 1, half, piece)
+            for b in range(HALVES):
+                for half in range(N // P):
+                    first, final = (b, half) == (0, 0), (b, half) == (HALVES - 1, N // P - 1)
+                    last_product(acc[:, half * width : (half + 1) * width], CHUNKS - 1, half, b, piece, first, final)
             res = ring.tile([P, (N // P) * width], F32, name="res", bufs=4)
             nc.scalar.copy(res[:], acc[:, 0 : (N // P) * width])
-            nc.sync.dma_start(
+            queue = nc.scalar if piece.stop == CHUNK else nc.sync
+            queue.dma_start(
                 out_halves[:, :, first_col + piece.start : first_col + piece.stop],
                 res[:].rearrange("p (h j) -> p h j", j=width),
             )

@@ -27,6 +27,7 @@ RUN = 4
 SCALE_ROWS = 16
 FIRST_ROW = P - SCALE_ROWS
 VECTOR_SQUARE_UNITS = (2, 3, 4, 5)
+TILES = CHUNKS * HALVES * PACK
 LAST_PIECES = [slice(0, 256), slice(256, 384), slice(384, 512)]
 
 
@@ -194,14 +195,14 @@ def tile_list_flow_residual_refine_kernel(
 
         def square(acc, tag):
             if tag is None:
-                sq = ring.tile([P, CHUNK], F32, name="sq", tag="sq", bufs=5)
+                sq = ring.tile([P, CHUNK], F32, name="sq", tag="sq", bufs=TILES)
             else:
                 sq = keep.tile([P, CHUNK], F32, name="sq_" + tag, tag=tag, align_bytes=64)
             nc.scalar.activation(sq[:], acc[:], ACT.Square)
             return sq
 
         def square_on_vector(acc):
-            sq = ring.tile([P, CHUNK], F32, name="sq_vector")
+            sq = ring.tile([P, CHUNK], F32, name="sq", tag="sq", bufs=TILES)
             nc.vector.tensor_reduce(sq[:], acc[:].unsqueeze(2).to_broadcast([P, CHUNK, 2]), AXIS.X, ALU.mult)
             return sq
 
@@ -211,7 +212,7 @@ def tile_list_flow_residual_refine_kernel(
 
         def interleave(planes, cols):
             width = cols.stop - cols.start
-            grouped = ring.tile([P, width * PACK], BF16, name="h_grouped", align_bytes=64, bufs=3)
+            grouped = ring.tile([P, width * PACK], BF16, name="h_grouped", align_bytes=64, bufs=CHUNKS * HALVES + 2)
             nc.vector.tensor_copy(
                 grouped[:].rearrange("p (c i t) -> p c t i", i=4, t=PACK),
                 planes[:, :, cols].rearrange("p t (c i) -> p c t i", i=4),
@@ -233,69 +234,73 @@ def tile_list_flow_residual_refine_kernel(
             )
 
         def multiply_chunk(c):
+            accs = [psum.tile([P, CHUNK], F32, name="o_acc%d" % half, tag="o_acc%d" % half) for half in range(N // P)]
             for half in range(N // P):
-                acc = psum.tile([P, CHUNK], F32, name="o_acc%d" % half, tag="o_acc%d" % half)
                 for b in range(HALVES):
-                    last_product(acc[:], c, half, b, slice(0, CHUNK), b == 0, b == HALVES - 1)
-                res = ring.tile([P, CHUNK], F32, name="res", bufs=4)
-                nc.vector.tensor_copy(res[:], acc[:])
+                    last_product(accs[half][:], c, half, b, slice(0, CHUNK), b == 0, b == HALVES - 1)
+            return accs
+
+        def store_chunk(accs, c, copy):
+            for half in reversed(range(N // P)):
+                res = ring.tile([P, CHUNK], F32, name="res", bufs=7)
+                copy(res[:], accs[half][:])
                 nc.sync.dma_start(out[half * P : (half + 1) * P, c * CHUNK : (c + 1) * CHUNK], res[:])
-
-        planes = {}
-
-        def finish_unit(u):
-            parts = [slice(0, CHUNK // 2), slice(CHUNK // 2, CHUNK)]
-            grouped = [interleave(planes[u], cols) for cols in parts]
-            for part, cols in zip(grouped, parts):
-                quantize_h(u, part, cols)
 
         units = [(c, b) for b in range(HALVES) for c in range(CHUNKS)]
         last = len(units) - 1
-        pending = []
+        planes = [keep.tile([P, PACK, CHUNK], BF16, name="h_planes%d" % u) for u in range(len(units))]
+        whole = slice(0, CHUNK)
+        squares = {}
         for u, (c, b) in enumerate(units):
-            planes[u] = ring.tile([P, PACK, CHUNK], BF16, name="h_planes", tag="h_planes", bufs=3)
-            deferred = []
-            for t in range(PACK):
-                acc = first_products(c, b, t)
-                if t == 0 and u in VECTOR_SQUARE_UNITS:
-                    deferred = [(square_on_vector(acc), planes[u], b, t)]
-                    fresh = []
-                else:
-                    fresh = [(square(acc, "v_words2" if (u, t) == (0, 0) else None), planes[u], b, t)]
-                if u < last or t == 0:
-                    for args in pending:
-                        root(*args)
-                    pending = []
-                pending = pending + fresh
-                if t == 0 and u >= 1:
-                    finish_unit(u - 1)
-                if (u, t) == (0, 1):
-                    v_words.append(gather_words("v_words", word_win1, list1, CHUNKS - 1))
-                    w3_raw = load_w3()
-                    grouped1 = prepare_w1_second_half()
-                    nc.vector.quantize_mx(w1_codes[:, 512:1024].bitcast(FP8X4), w1_plane[:, 512:1024], grouped1[:])
-                if (u, t) == (1, 3):
-                    grouped3 = prepare_w3(w3_raw)
-                if (u, t) == (2, 3):
-                    nc.vector.quantize_mx(w3_codes[:].bitcast(FP8X4), w3_plane[:], grouped3[:])
-                if t == 1 and u > CHUNKS:
-                    multiply_chunk(u - 1 - CHUNKS)
-            pending = pending + deferred
+            if u == 0:
+                for t in range(PACK):
+                    squares[u, t] = square(first_products(c, b, t), "v_words2" if t == 0 else None)
+                    if t > 0:
+                        root(squares[u, t - 1], planes[u], b, t - 1)
+                root_order = [PACK - 1]
+                v_words.append(gather_words("v_words", word_win1, list1, CHUNKS - 1))
+                w3_raw = load_w3()
+                grouped1 = prepare_w1_second_half()
+                nc.vector.quantize_mx(w1_codes[:, 512:1024].bitcast(FP8X4), w1_plane[:, 512:1024], grouped1[:])
+            else:
+                own = [t for t in range(PACK) if (u, t) not in squares]
+                accs = {t: first_products(c, b, t) for t in own}
+                for t in reversed(own):
+                    squares[u, t] = square(accs[t], None)
+                root_order = [0, 1, 2, 3] if 0 not in own else [1, 2, 3, 0]
+            if u >= 1:
+                grouped = interleave(planes[u - 1], whole)
+            if u + 1 in VECTOR_SQUARE_UNITS:
+                squares[u + 1, 0] = square_on_vector(first_products(*units[u + 1], 0))
+            if u == last:
+                store_chunk(out_accs, 0, nc.vector.tensor_copy)
+            if u >= 1:
+                quantize_h(u - 1, grouped, whole)
+            if u == 1:
+                grouped3 = prepare_w3(w3_raw)
+            if u == 2:
+                nc.vector.quantize_mx(w3_codes[:].bitcast(FP8X4), w3_plane[:], grouped3[:])
+            if u > CHUNKS:
+                out_accs = multiply_chunk(u - 1 - CHUNKS)
+            if u < last:
+                for t in root_order:
+                    root(squares[u, t], planes[u], b, t)
 
         out_halves = out.rearrange("(h p) j -> p h j", p=P)
         first_col = (CHUNKS - 1) * CHUNK
         for piece in LAST_PIECES:
-            for args in pending:
-                root(*args, piece)
+            for t in root_order:
+                root(squares[last, t], planes[last], HALVES - 1, t, piece)
+        store_chunk(out_accs, 1, nc.scalar.copy)
         for index, piece in enumerate(LAST_PIECES):
             width = piece.stop - piece.start
             quantize_h(last, interleave(planes[last], piece), piece)
-            acc = psum.tile([P, CHUNK], F32, name="piece_acc", tag=["o_acc0", "o_acc1", "d_acc"][index], bufs=[1, 1, 6][index])
+            acc = psum.tile([P, CHUNK], F32, name="piece_acc", tag="d_acc", bufs=6)
             for b in range(HALVES):
                 for half in range(N // P):
                     first, final = (b, half) == (0, 0), (b, half) == (HALVES - 1, N // P - 1)
                     last_product(acc[:, half * width : (half + 1) * width], CHUNKS - 1, half, b, piece, first, final)
-            res = ring.tile([P, (N // P) * width], F32, name="res", bufs=4)
+            res = ring.tile([P, (N // P) * width], F32, name="res", bufs=7)
             nc.scalar.copy(res[:], acc[:, 0 : (N // P) * width])
             queue = nc.scalar if piece.stop == CHUNK else nc.sync
             queue.dma_start(

@@ -26,7 +26,8 @@ HALVES = H // 512
 RUN = 4
 SCALE_ROWS = 16
 FIRST_ROW = P - SCALE_ROWS
-VECTOR_SQUARE_UNITS = (2, 3, 4, 5)
+VECTOR_TILES = ((1, 0), (2, 0), (2, 1), (3, 0), (3, 1), (4, 0), (5, 0))
+GPSIMD_UNITS = (0, 1, 2)
 TILES = CHUNKS * HALVES * PACK
 LAST_PIECES = [slice(0, 256), slice(256, 384), slice(384, 512)]
 
@@ -52,7 +53,8 @@ def tile_list_flow_residual_refine_kernel(
         nc.sync.dma_start(scale_win2[FIRST_ROW:P, :].bitcast(I32), tab2_scales[0].bitcast(I32))
         nc.vector.memset(scale_win1[0:FIRST_ROW, :].bitcast(I32), 0)
         nc.vector.memset(scale_win2[0:FIRST_ROW, :].bitcast(I32), 0)
-        picked_plane = keep.tile([P, 2 * S], U8, name="picked_plane", align_bytes=64)
+        first_plane = keep.tile([P, 2 * CHUNK], U8, name="first_plane", align_bytes=64)
+        later_plane = keep.tile([P, 2 * (S - CHUNK)], U8, name="later_plane", align_bytes=64)
 
         warm_in = keep.tile([P, 1], F32, name="warm_in")
         warm_out = keep.tile([P, 1], F32, name="warm_out")
@@ -79,7 +81,8 @@ def tile_list_flow_residual_refine_kernel(
         nc.sync.dma_start(word_win2[:], tab2_words[0].rearrange("p t i -> p (t i)").bitcast(I32))
         identity = keep.tile([P, P], F32, name="identity")
         make_identity(nc, identity[:])
-        nc.gpsimd.memset(picked_plane[:].bitcast(I32), 0)
+        nc.gpsimd.memset(first_plane[:].bitcast(I32), 0)
+        nc.gpsimd.memset(later_plane[:].bitcast(I32), 0)
         gain_turned = psum.tile([P, CHUNK], F32, name="gain_turned", tag="d_acc", bufs=6)
         gain_dealt = keep.tile([P, 512], F32, name="gain_dealt")
         nc.scalar.copy(
@@ -111,11 +114,20 @@ def tile_list_flow_residual_refine_kernel(
         picked_rows = keep.tile([P, 2 * S], U8, name="picked_rows", align_bytes=64)
         nc.vector.tensor_copy(picked_rows[:, 0:S], scale_win1[:].indirect(list1[:]))
         nc.vector.tensor_copy(picked_rows[:, S : 2 * S], scale_win2[:].indirect(list2[:]))
-        for quad in range(4):
-            row = FIRST_ROW + 4 * quad
-            nc.sync.dma_start(
-                picked_plane[32 * quad : 32 * quad + 4, :].bitcast(I32), picked_rows[row : row + 4, :].bitcast(I32)
-            )
+        rows_by_table = picked_rows[:].bitcast(I32).rearrange("p (a w) -> p a w", a=2)
+        for plane, words in ((first_plane, slice(0, CHUNK // 4)), (later_plane, slice(CHUNK // 4, S // 4))):
+            for quad in range(4):
+                row = FIRST_ROW + 4 * quad
+                nc.sync.dma_start(
+                    plane[32 * quad : 32 * quad + 4, :].bitcast(I32).rearrange("p (a w) -> p a w", a=2),
+                    rows_by_table[row : row + 4, :, words],
+                )
+
+        def table_plane(table, c):
+            if c == 0:
+                return first_plane[:, table * CHUNK : (table + 1) * CHUNK]
+            first = table * (S - CHUNK) + (c - 1) * CHUNK
+            return later_plane[:, first : first + CHUNK]
 
         w1_codes = keep.tile([P, H], U32, name="w1_codes", align_bytes=64)
         w1_plane = keep.tile([P, H], U8, name="w1_plane", align_bytes=64)
@@ -150,11 +162,12 @@ def tile_list_flow_residual_refine_kernel(
         def prepare_w1_second_half():
             grouped1 = keep.tile([P, PACK * 512], BF16, name="w1_grouped1", tag="grouped", align_bytes=64)
             for t in range(PACK):
-                dst, src = w1_views(w1_raw1, grouped1, t)
-                nc.vector.tensor_scalar(dst, src, -1.0, None, ALU.mult)
+                src = w1_raw1[:].rearrange("p j (u t e) -> p t u e j", t=PACK, e=RUN)[:, t]
+                dst = grouped1[:, t * 512 : (t + 1) * 512].rearrange("p (u e j) -> p u e j", e=RUN, j=PACK)
+                nc.gpsimd.tensor_scalar(dst, src, -1.0, 0.0, ALU.mult, ALU.add)
             return grouped1
 
-        w3_codes = keep.tile([P, HALVES * N], U32, name="w3_codes", align_bytes=64)
+        w3_codes = {}
         w3_plane = keep.tile([P, HALVES * N], U8, name="w3_plane", align_bytes=64)
 
         def load_w3():
@@ -165,31 +178,34 @@ def tile_list_flow_residual_refine_kernel(
                     nc.sync.dma_start(raw[:, b, t, :], rows[b, t])
             return raw
 
-        def prepare_w3(w3_raw):
-            grouped3 = keep.tile([P, HALVES * N * PACK], BF16, name="w3_grouped", tag="grouped", align_bytes=64)
-            for b in range(HALVES):
-                sign = gain_sign[:, PACK * b : PACK * (b + 1)].unsqueeze(1).unsqueeze(3).to_broadcast([P, N // 4, PACK, 4])
-                nc.vector.tensor_tensor(
-                    grouped3[:, b * N * PACK : (b + 1) * N * PACK].rearrange("p (c i t) -> p c t i", i=4, t=PACK),
-                    w3_raw[:, b].rearrange("p t (c i) -> p c t i", i=4),
-                    sign,
-                    ALU.mult,
-                )
+        def cast_w3(w3_raw, b):
+            grouped3 = keep.tile([P, N * PACK], BF16, name="w3_grouped%d" % b, tag="h_grouped%d" % b, align_bytes=64)
+            sign = gain_sign[:, PACK * b : PACK * (b + 1)].unsqueeze(1).unsqueeze(3).to_broadcast([P, N // 4, PACK, 4])
+            nc.vector.tensor_tensor(
+                grouped3[:].rearrange("p (c i t) -> p c t i", i=4, t=PACK),
+                w3_raw[:, b].rearrange("p t (c i) -> p c t i", i=4),
+                sign,
+                ALU.mult,
+            )
             return grouped3
+
+        def quantize_w3(grouped3, b):
+            w3_codes[b] = keep.tile([P, N], U32, name="w3_codes%d" % b, tag="h_planes%d" % (b + 1), align_bytes=64)
+            nc.vector.quantize_mx(w3_codes[b][:].bitcast(FP8X4), w3_plane[:, b * N : (b + 1) * N], grouped3[:])
 
         def first_products(c, b, t):
             acc = psum.tile([P, CHUNK], F32, name="d_acc", tag="d_acc", bufs=6)
             cols = slice((PACK * b + t) * P, (PACK * b + t + 1) * P)
             passes = [
-                (w2_codes[:, 2 * cols.start : 2 * cols.stop].bitcast(FP4X4), w2_plane, v2_words, S),
+                (w2_codes[:, 2 * cols.start : 2 * cols.stop].bitcast(FP4X4), w2_plane, v2_words, 1),
                 (w1_codes[:, cols].bitcast(FP8X4), w1_plane, v_words, 0),
             ]
             if (c, b) == (0, 0) and t < 2:
                 passes = passes[::-1]
-            for index, (codes, plane, words, first) in enumerate(passes):
+            for index, (codes, plane, words, table) in enumerate(passes):
                 nc.tensor.matmul_mx(
                     acc[:], codes, plane[:, cols], words[c][:].bitcast(FP8X4),
-                    picked_plane[:, first + c * CHUNK : first + (c + 1) * CHUNK], start=(index == 0), stop=(index == 1),
+                    table_plane(table, c), start=(index == 0), stop=(index == 1),
                 )
             return acc
 
@@ -210,13 +226,20 @@ def tile_list_flow_residual_refine_kernel(
             g2 = gain_sq[:, PACK * b + t : PACK * b + t + 1]
             nc.scalar.activation(planes[:, t, cols], sq[:, cols], ACT.Sqrt, bias=g2, scale=g2)
 
-        def interleave(planes, cols):
+        def interleave(u, cols, tag):
             width = cols.stop - cols.start
-            grouped = ring.tile([P, width * PACK], BF16, name="h_grouped", align_bytes=64, bufs=CHUNKS * HALVES + 2)
-            nc.vector.tensor_copy(
-                grouped[:].rearrange("p (c i t) -> p c t i", i=4, t=PACK),
-                planes[:, :, cols].rearrange("p t (c i) -> p c t i", i=4),
-            )
+            grouped = keep.tile([P, width * PACK], BF16, name=tag, tag=tag, align_bytes=64)
+            if u in GPSIMD_UNITS:
+                nc.gpsimd.tensor_scalar(
+                    grouped[:].rearrange("p (j t) -> p j t", t=PACK),
+                    planes[u][:, :, cols].rearrange("p t j -> p j t"),
+                    1.0, 0.0, ALU.mult, ALU.add,
+                )
+            else:
+                nc.vector.tensor_copy(
+                    grouped[:].rearrange("p (c i t) -> p c t i", i=4, t=PACK),
+                    planes[u][:, :, cols].rearrange("p t (c i) -> p c t i", i=4),
+                )
             return grouped
 
         h_codes = [keep.tile([P, CHUNK], U32, name="h_codes%d" % u, align_bytes=64) for u in range(CHUNKS * HALVES)]
@@ -229,7 +252,7 @@ def tile_list_flow_residual_refine_kernel(
             w_cols = slice(b * N + half * P, b * N + (half + 1) * P)
             u = b * CHUNKS + c
             nc.tensor.matmul_mx(
-                acc, w3_codes[:, w_cols].bitcast(FP8X4), w3_plane[:, w_cols],
+                acc, w3_codes[b][:, half * P : (half + 1) * P].bitcast(FP8X4), w3_plane[:, w_cols],
                 h_codes[u][:, cols].bitcast(FP8X4), h_plane[u][:, cols], start=start, stop=stop,
             )
 
@@ -240,15 +263,14 @@ def tile_list_flow_residual_refine_kernel(
                     last_product(accs[half][:], c, half, b, slice(0, CHUNK), b == 0, b == HALVES - 1)
             return accs
 
-        def store_chunk(accs, c, copy):
-            for half in reversed(range(N // P)):
-                res = ring.tile([P, CHUNK], F32, name="res", bufs=7)
-                copy(res[:], accs[half][:])
-                nc.sync.dma_start(out[half * P : (half + 1) * P, c * CHUNK : (c + 1) * CHUNK], res[:])
+        def store_half(accs, c, half, copy):
+            res = ring.tile([P, CHUNK], F32, name="res", bufs=7)
+            copy(res[:], accs[half][:])
+            nc.sync.dma_start(out[half * P : (half + 1) * P, c * CHUNK : (c + 1) * CHUNK], res[:])
 
         units = [(c, b) for b in range(HALVES) for c in range(CHUNKS)]
         last = len(units) - 1
-        planes = [keep.tile([P, PACK, CHUNK], BF16, name="h_planes%d" % u) for u in range(len(units))]
+        planes = [keep.tile([P, PACK, CHUNK], BF16, name="h_planes%d" % u, tag="h_planes%d" % u, align_bytes=64) for u in range(len(units))]
         whole = slice(0, CHUNK)
         squares = {}
         for u, (c, b) in enumerate(units):
@@ -267,21 +289,23 @@ def tile_list_flow_residual_refine_kernel(
                 accs = {t: first_products(c, b, t) for t in own}
                 for t in reversed(own):
                     squares[u, t] = square(accs[t], None)
-                root_order = [0, 1, 2, 3] if 0 not in own else [1, 2, 3, 0]
+                root_order = own[1:] + own[:1] + [t for t in range(PACK) if t not in own]
             if u >= 1:
-                grouped = interleave(planes[u - 1], whole)
-            if u + 1 in VECTOR_SQUARE_UNITS:
-                squares[u + 1, 0] = square_on_vector(first_products(*units[u + 1], 0))
-            if u == last:
-                store_chunk(out_accs, 0, nc.vector.tensor_copy)
+                grouped = interleave(u - 1, whole, "h_grouped%d" % (u - 1))
+            for t in range(PACK):
+                if (u + 1, t) in VECTOR_TILES:
+                    squares[u + 1, t] = square_on_vector(first_products(*units[u + 1], t))
             if u >= 1:
                 quantize_h(u - 1, grouped, whole)
-            if u == 1:
-                grouped3 = prepare_w3(w3_raw)
-            if u == 2:
-                nc.vector.quantize_mx(w3_codes[:].bitcast(FP8X4), w3_plane[:], grouped3[:])
+            if 2 <= u < 2 + HALVES:
+                quantize_w3(grouped3, u - 2)
+            if 1 <= u < 1 + HALVES:
+                grouped3 = cast_w3(w3_raw, u - 1)
             if u > CHUNKS:
                 out_accs = multiply_chunk(u - 1 - CHUNKS)
+                if u < last:
+                    for half in reversed(range(N // P)):
+                        store_half(out_accs, u - 1 - CHUNKS, half, nc.vector.tensor_copy)
             if u < last:
                 for t in root_order:
                     root(squares[u, t], planes[u], b, t)
@@ -291,10 +315,17 @@ def tile_list_flow_residual_refine_kernel(
         for piece in LAST_PIECES:
             for t in root_order:
                 root(squares[last, t], planes[last], HALVES - 1, t, piece)
-        store_chunk(out_accs, 1, nc.scalar.copy)
+        waiting = None
         for index, piece in enumerate(LAST_PIECES):
+            grouped = interleave(last, piece, "piece_grouped%d" % index)
+            if waiting is not None:
+                quantize_h(last, *waiting)
+            waiting = (grouped, piece)
+        quantize_h(last, *waiting)
+        store_half(out_accs, CHUNKS - 2, 0, nc.scalar.copy)
+        store_half(out_accs, CHUNKS - 2, 1, nc.vector.tensor_copy)
+        for piece in LAST_PIECES:
             width = piece.stop - piece.start
-            quantize_h(last, interleave(planes[last], piece), piece)
             acc = psum.tile([P, CHUNK], F32, name="piece_acc", tag="d_acc", bufs=6)
             for b in range(HALVES):
                 for half in range(N // P):

@@ -26,8 +26,8 @@ HALVES = H // 512
 RUN = 4
 SCALE_ROWS = 16
 FIRST_ROW = P - SCALE_ROWS
-VECTOR_TILES = ((1, 0), (2, 0), (2, 1), (3, 0), (3, 1), (4, 0), (5, 0))
-GPSIMD_UNITS = (0, 1, 2)
+VECTOR_TILES = ((2, 0), (2, 1), (2, 2), (4, 0), (5, 0))
+GPSIMD_UNITS = (0,)
 TILES = CHUNKS * HALVES * PACK
 LAST_PIECES = [slice(0, 256), slice(256, 384), slice(384, 512)]
 
@@ -162,12 +162,11 @@ def tile_list_flow_residual_refine_kernel(
         def prepare_w1_second_half():
             grouped1 = keep.tile([P, PACK * 512], BF16, name="w1_grouped1", tag="grouped", align_bytes=64)
             for t in range(PACK):
-                src = w1_raw1[:].rearrange("p j (u t e) -> p t u e j", t=PACK, e=RUN)[:, t]
-                dst = grouped1[:, t * 512 : (t + 1) * 512].rearrange("p (u e j) -> p u e j", e=RUN, j=PACK)
-                nc.gpsimd.tensor_scalar(dst, src, -1.0, 0.0, ALU.mult, ALU.add)
+                dst, src = w1_views(w1_raw1, grouped1, t)
+                nc.vector.tensor_scalar(dst, src, -1.0, None, ALU.mult)
             return grouped1
 
-        w3_codes = {}
+        w3_codes = keep.tile([P, HALVES * N], U32, name="w3_codes", align_bytes=64)
         w3_plane = keep.tile([P, HALVES * N], U8, name="w3_plane", align_bytes=64)
 
         def load_w3():
@@ -178,20 +177,21 @@ def tile_list_flow_residual_refine_kernel(
                     nc.sync.dma_start(raw[:, b, t, :], rows[b, t])
             return raw
 
-        def cast_w3(w3_raw, b):
-            grouped3 = keep.tile([P, N * PACK], BF16, name="w3_grouped%d" % b, tag="h_grouped%d" % b, align_bytes=64)
-            sign = gain_sign[:, PACK * b : PACK * (b + 1)].unsqueeze(1).unsqueeze(3).to_broadcast([P, N // 4, PACK, 4])
-            nc.vector.tensor_tensor(
-                grouped3[:].rearrange("p (c i t) -> p c t i", i=4, t=PACK),
-                w3_raw[:, b].rearrange("p t (c i) -> p c t i", i=4),
-                sign,
-                ALU.mult,
-            )
-            return grouped3
-
-        def quantize_w3(grouped3, b):
-            w3_codes[b] = keep.tile([P, N], U32, name="w3_codes%d" % b, tag="h_planes%d" % (b + 1), align_bytes=64)
-            nc.vector.quantize_mx(w3_codes[b][:].bitcast(FP8X4), w3_plane[:, b * N : (b + 1) * N], grouped3[:])
+        def prepare_w3(w3_raw):
+            grouped3 = keep.tile([P, HALVES * N * PACK], BF16, name="w3_grouped", tag="grouped", align_bytes=64)
+            for b in range(HALVES):
+                sign = gain_sign[:, PACK * b : PACK * (b + 1)].unsqueeze(1).unsqueeze(3).to_broadcast([P, N // 4, PACK, 4])
+                nc.vector.tensor_tensor(
+                    grouped3[:, b * N * PACK : (b + 1) * N * PACK].rearrange("p (c i t) -> p c t i", i=4, t=PACK),
+                    w3_raw[:, b].rearrange("p t (c i) -> p c t i", i=4),
+                    sign,
+                    ALU.mult,
+                )
+            for b in range(HALVES):
+                cols = slice(b * N, (b + 1) * N)
+                nc.vector.quantize_mx(
+                    w3_codes[:, cols].bitcast(FP8X4), w3_plane[:, cols], grouped3[:, b * N * PACK : (b + 1) * N * PACK]
+                )
 
         def first_products(c, b, t):
             acc = psum.tile([P, CHUNK], F32, name="d_acc", tag="d_acc", bufs=6)
@@ -228,7 +228,7 @@ def tile_list_flow_residual_refine_kernel(
 
         def interleave(u, cols, tag):
             width = cols.stop - cols.start
-            grouped = keep.tile([P, width * PACK], BF16, name=tag, tag=tag, align_bytes=64)
+            grouped = keep.tile([P, width * PACK], BF16, name="h_grouped", tag=tag, align_bytes=64)
             if u in GPSIMD_UNITS:
                 nc.gpsimd.tensor_scalar(
                     grouped[:].rearrange("p (j t) -> p j t", t=PACK),
@@ -252,7 +252,7 @@ def tile_list_flow_residual_refine_kernel(
             w_cols = slice(b * N + half * P, b * N + (half + 1) * P)
             u = b * CHUNKS + c
             nc.tensor.matmul_mx(
-                acc, w3_codes[b][:, half * P : (half + 1) * P].bitcast(FP8X4), w3_plane[:, w_cols],
+                acc, w3_codes[:, w_cols].bitcast(FP8X4), w3_plane[:, w_cols],
                 h_codes[u][:, cols].bitcast(FP8X4), h_plane[u][:, cols], start=start, stop=stop,
             )
 
@@ -291,16 +291,14 @@ def tile_list_flow_residual_refine_kernel(
                     squares[u, t] = square(accs[t], None)
                 root_order = own[1:] + own[:1] + [t for t in range(PACK) if t not in own]
             if u >= 1:
-                grouped = interleave(u - 1, whole, "h_grouped%d" % (u - 1))
+                grouped = interleave(u - 1, whole, "grouped" if u - 1 in GPSIMD_UNITS else "h_grouped%d" % (u - 1))
             for t in range(PACK):
                 if (u + 1, t) in VECTOR_TILES:
                     squares[u + 1, t] = square_on_vector(first_products(*units[u + 1], t))
             if u >= 1:
                 quantize_h(u - 1, grouped, whole)
-            if 2 <= u < 2 + HALVES:
-                quantize_w3(grouped3, u - 2)
-            if 1 <= u < 1 + HALVES:
-                grouped3 = cast_w3(w3_raw, u - 1)
+            if u == 1:
+                prepare_w3(w3_raw)
             if u > CHUNKS:
                 out_accs = multiply_chunk(u - 1 - CHUNKS)
                 if u < last:

@@ -26,7 +26,8 @@ HALVES = H // 512
 RUN = 4
 SCALE_ROWS = 16
 FIRST_ROW = P - SCALE_ROWS
-VECTOR_TILES = ((2, 0), (2, 1), (2, 2), (4, 0), (5, 0))
+VECTOR_TILES = ((1, 0), (1, 1), (2, 0), (2, 1), (2, 2), (3, 0))
+HELD_TILES = [(2, 1), (2, 2)]
 GPSIMD_UNITS = (0,)
 TILES = CHUNKS * HALVES * PACK
 LAST_PIECES = [slice(0, 256), slice(256, 384), slice(384, 512)]
@@ -156,14 +157,15 @@ def tile_list_flow_residual_refine_kernel(
             w2_scale_raw[:].bitcast(I32).rearrange("p (b u t) -> p b t u", b=HALVES, t=PACK),
         )
 
-        v_words = [gather_words("v_words", word_win1, list1, c) for c in range(CHUNKS - 1)]
+        v_words = [gather_words("v_words", word_win1, list1, c) for c in range(CHUNKS)]
         v2_words = [gather_words("v2_words", word_win2, list2, c) for c in range(CHUNKS)]
 
         def prepare_w1_second_half():
             grouped1 = keep.tile([P, PACK * 512], BF16, name="w1_grouped1", tag="grouped", align_bytes=64)
             for t in range(PACK):
-                dst, src = w1_views(w1_raw1, grouped1, t)
-                nc.vector.tensor_scalar(dst, src, -1.0, None, ALU.mult)
+                src = w1_raw1[:].rearrange("p j (u t e) -> p t u e j", t=PACK, e=RUN)[:, t]
+                dst = grouped1[:, t * 512 : (t + 1) * 512].rearrange("p (u e j) -> p u e j", e=RUN, j=PACK)
+                nc.gpsimd.tensor_scalar(dst, src, -1.0, 0.0, ALU.mult, ALU.add)
             return grouped1
 
         w3_codes = keep.tile([P, HALVES * N], U32, name="w3_codes", align_bytes=64)
@@ -209,16 +211,12 @@ def tile_list_flow_residual_refine_kernel(
                 )
             return acc
 
-        def square(acc, tag):
-            if tag is None:
-                sq = ring.tile([P, CHUNK], F32, name="sq", tag="sq", bufs=TILES)
-            else:
-                sq = keep.tile([P, CHUNK], F32, name="sq_" + tag, tag=tag, align_bytes=64)
+        def square(acc):
+            sq = ring.tile([P, CHUNK], F32, name="sq", tag="sq", bufs=TILES)
             nc.scalar.activation(sq[:], acc[:], ACT.Square)
             return sq
 
-        def square_on_vector(acc):
-            sq = ring.tile([P, CHUNK], F32, name="sq", tag="sq", bufs=TILES)
+        def square_on_vector(acc, sq):
             nc.vector.tensor_reduce(sq[:], acc[:].unsqueeze(2).to_broadcast([P, CHUNK, 2]), AXIS.X, ALU.mult)
             return sq
 
@@ -276,11 +274,10 @@ def tile_list_flow_residual_refine_kernel(
         for u, (c, b) in enumerate(units):
             if u == 0:
                 for t in range(PACK):
-                    squares[u, t] = square(first_products(c, b, t), "v_words2" if t == 0 else None)
+                    squares[u, t] = square(first_products(c, b, t))
                     if t > 0:
                         root(squares[u, t - 1], planes[u], b, t - 1)
                 root_order = [PACK - 1]
-                v_words.append(gather_words("v_words", word_win1, list1, CHUNKS - 1))
                 w3_raw = load_w3()
                 grouped1 = prepare_w1_second_half()
                 nc.vector.quantize_mx(w1_codes[:, 512:1024].bitcast(FP8X4), w1_plane[:, 512:1024], grouped1[:])
@@ -288,13 +285,19 @@ def tile_list_flow_residual_refine_kernel(
                 own = [t for t in range(PACK) if (u, t) not in squares]
                 accs = {t: first_products(c, b, t) for t in own}
                 for t in reversed(own):
-                    squares[u, t] = square(accs[t], None)
+                    squares[u, t] = square(accs[t])
                 root_order = own[1:] + own[:1] + [t for t in range(PACK) if t not in own]
             if u >= 1:
                 grouped = interleave(u - 1, whole, "grouped" if u - 1 in GPSIMD_UNITS else "h_grouped%d" % (u - 1))
+            if u == 1:
+                held = keep.tile([P, len(HELD_TILES), CHUNK], F32, name="held_squares", tag="w1_raw")
             for t in range(PACK):
                 if (u + 1, t) in VECTOR_TILES:
-                    squares[u + 1, t] = square_on_vector(first_products(*units[u + 1], t))
+                    if (u + 1, t) in HELD_TILES:
+                        sq = held[:, HELD_TILES.index((u + 1, t)), :]
+                    else:
+                        sq = ring.tile([P, CHUNK], F32, name="sq", tag="sq", bufs=TILES)
+                    squares[u + 1, t] = square_on_vector(first_products(*units[u + 1], t), sq)
             if u >= 1:
                 quantize_h(u - 1, grouped, whole)
             if u == 1:

@@ -26,8 +26,8 @@ HALVES = H // 512
 RUN = 4
 SCALE_ROWS = 16
 FIRST_ROW = P - SCALE_ROWS
-VECTOR_TILES = ((1, 0), (1, 1), (2, 0), (2, 1), (2, 2), (3, 0))
-HELD_TILES = [(2, 1), (2, 2)]
+VECTOR_TILES = ((0, 3), (1, 0), (1, 1), (2, 0), (2, 1), (2, 2))
+HELD_TILES = [(2, 0), (2, 1), (2, 2)]
 GPSIMD_UNITS = (0,)
 TILES = CHUNKS * HALVES * PACK
 LAST_PIECES = [slice(0, 256), slice(256, 384), slice(384, 512)]
@@ -40,6 +40,7 @@ def tile_list_flow_residual_refine_kernel(
     with ExitStack() as ctx:
         keep = ctx.enter_context(tc.tile_pool(name="keep", bufs=1))
         ring = ctx.enter_context(tc.tile_pool(name="ring", bufs=2))
+        chain = ctx.enter_context(tc.tile_pool(name="chain", bufs=1))
         psum = ctx.enter_context(tc.psum_pool(name="psum", bufs=1))
 
         w2_scale_raw = keep.tile([P, H], U8, name="w2_scale_raw")
@@ -47,15 +48,14 @@ def tile_list_flow_residual_refine_kernel(
         list1 = keep.tile([P, S // 16], U16, name="list1")
         list2 = keep.tile([P, S // 16], U16, name="list2")
         scale_win1 = keep.tile([P, T], U8, name="scale_win1")
-        scale_win2 = keep.tile([P, T], U8, name="scale_win2")
+        scale_win2 = keep.tile([P, T], U8, name="scale_win2", tag="w1_raw")
         nc.sync.dma_start(list1[:], offs)
         nc.sync.dma_start(scale_win1[FIRST_ROW:P, :].bitcast(I32), tab_scales[0].bitcast(I32))
         nc.sync.dma_start(list2[:], offs2)
         nc.sync.dma_start(scale_win2[FIRST_ROW:P, :].bitcast(I32), tab2_scales[0].bitcast(I32))
         nc.vector.memset(scale_win1[0:FIRST_ROW, :].bitcast(I32), 0)
         nc.vector.memset(scale_win2[0:FIRST_ROW, :].bitcast(I32), 0)
-        first_plane = keep.tile([P, 2 * CHUNK], U8, name="first_plane", align_bytes=64)
-        later_plane = keep.tile([P, 2 * (S - CHUNK)], U8, name="later_plane", align_bytes=64)
+        picked_plane = keep.tile([P, 2 * S], U8, name="picked_plane", align_bytes=64)
 
         warm_in = keep.tile([P, 1], F32, name="warm_in")
         warm_out = keep.tile([P, 1], F32, name="warm_out")
@@ -64,7 +64,7 @@ def tile_list_flow_residual_refine_kernel(
 
         word_win1 = keep.tile([P, T], I32, name="word_win1", tag="words_then_w3")
         w1_rows = w1.rearrange("(p j) r -> p j r", j=PACK)
-        w1_raw0 = keep.tile([P, PACK, 512], F32, name="w1_raw0", tag="w1_raw")
+        w1_raw0 = keep.tile([P, PACK, 512], F32, name="w1_raw0")
         w2_raw = keep.tile([P, H // 2], I32, name="w2_raw")
         gain_rows = keep.tile([P, 512], F32, name="gain_rows")
         nc.sync.dma_start(gain_rows[P - HALVES : P, :], gain.rearrange("(b r) -> b r", b=HALVES))
@@ -82,8 +82,7 @@ def tile_list_flow_residual_refine_kernel(
         nc.sync.dma_start(word_win2[:], tab2_words[0].rearrange("p t i -> p (t i)").bitcast(I32))
         identity = keep.tile([P, P], F32, name="identity")
         make_identity(nc, identity[:])
-        nc.gpsimd.memset(first_plane[:].bitcast(I32), 0)
-        nc.gpsimd.memset(later_plane[:].bitcast(I32), 0)
+        nc.gpsimd.memset(picked_plane[:].bitcast(I32), 0)
         gain_turned = psum.tile([P, CHUNK], F32, name="gain_turned", tag="d_acc", bufs=6)
         gain_dealt = keep.tile([P, 512], F32, name="gain_dealt")
         nc.scalar.copy(
@@ -115,20 +114,16 @@ def tile_list_flow_residual_refine_kernel(
         picked_rows = keep.tile([P, 2 * S], U8, name="picked_rows", align_bytes=64)
         nc.vector.tensor_copy(picked_rows[:, 0:S], scale_win1[:].indirect(list1[:]))
         nc.vector.tensor_copy(picked_rows[:, S : 2 * S], scale_win2[:].indirect(list2[:]))
-        rows_by_table = picked_rows[:].bitcast(I32).rearrange("p (a w) -> p a w", a=2)
-        for plane, words in ((first_plane, slice(0, CHUNK // 4)), (later_plane, slice(CHUNK // 4, S // 4))):
-            for quad in range(4):
-                row = FIRST_ROW + 4 * quad
-                nc.sync.dma_start(
-                    plane[32 * quad : 32 * quad + 4, :].bitcast(I32).rearrange("p (a w) -> p a w", a=2),
-                    rows_by_table[row : row + 4, :, words],
-                )
+        for quad in range(4):
+            row = FIRST_ROW + 4 * quad
+            nc.sync.dma_start(
+                picked_plane[32 * quad : 32 * quad + 4, :].bitcast(I32), picked_rows[row : row + 4, :].bitcast(I32)
+            )
+        w1_raw1 = keep.tile([P, PACK, 512], F32, name="w1_raw1", tag="w1_raw")
+        nc.sync.dma_start(w1_raw1[:], w1_rows[:, :, 512:1024])
 
         def table_plane(table, c):
-            if c == 0:
-                return first_plane[:, table * CHUNK : (table + 1) * CHUNK]
-            first = table * (S - CHUNK) + (c - 1) * CHUNK
-            return later_plane[:, first : first + CHUNK]
+            return picked_plane[:, table * S + c * CHUNK : table * S + (c + 1) * CHUNK]
 
         w1_codes = keep.tile([P, H], U32, name="w1_codes", align_bytes=64)
         w1_plane = keep.tile([P, H], U8, name="w1_plane", align_bytes=64)
@@ -138,12 +133,10 @@ def tile_list_flow_residual_refine_kernel(
             dst = grouped[:, t * 512 : (t + 1) * 512].rearrange("p (u e j) -> p u j e", e=RUN, j=PACK)
             return dst, src
 
-        grouped0 = keep.tile([P, PACK * 512], BF16, name="w1_grouped0", tag="grouped", align_bytes=64)
+        grouped0 = chain.tile([P, PACK * 512], BF16, name="w1_grouped0", tag="w1_grouped", align_bytes=64, offset=2048)
         for t in range(PACK):
             dst, src = w1_views(w1_raw0, grouped0, t)
             nc.scalar.activation(dst, src, ACT.Copy, scale=-1.0)
-        w1_raw1 = keep.tile([P, PACK, 512], F32, name="w1_raw1", tag="w1_raw")
-        nc.sync.dma_start(w1_raw1[:], w1_rows[:, :, 512:1024])
         nc.vector.quantize_mx(w1_codes[:, 0:512].bitcast(FP8X4), w1_plane[:, 0:512], grouped0[:])
 
         w2_codes = keep.tile([P, 2 * H], U8, name="w2_codes", align_bytes=64)
@@ -161,7 +154,7 @@ def tile_list_flow_residual_refine_kernel(
         v2_words = [gather_words("v2_words", word_win2, list2, c) for c in range(CHUNKS)]
 
         def prepare_w1_second_half():
-            grouped1 = keep.tile([P, PACK * 512], BF16, name="w1_grouped1", tag="grouped", align_bytes=64)
+            grouped1 = chain.tile([P, PACK * 512], BF16, name="w1_grouped1", tag="w1_grouped", align_bytes=64, offset=2048)
             for t in range(PACK):
                 src = w1_raw1[:].rearrange("p j (u t e) -> p t u e j", t=PACK, e=RUN)[:, t]
                 dst = grouped1[:, t * 512 : (t + 1) * 512].rearrange("p (u e j) -> p u e j", e=RUN, j=PACK)
@@ -180,7 +173,7 @@ def tile_list_flow_residual_refine_kernel(
             return raw
 
         def prepare_w3(w3_raw):
-            grouped3 = keep.tile([P, HALVES * N * PACK], BF16, name="w3_grouped", tag="grouped", align_bytes=64)
+            grouped3 = chain.tile([P, HALVES * N * PACK], BF16, name="w3_grouped", tag="grouped", align_bytes=64, offset=0)
             for b in range(HALVES):
                 sign = gain_sign[:, PACK * b : PACK * (b + 1)].unsqueeze(1).unsqueeze(3).to_broadcast([P, N // 4, PACK, 4])
                 nc.vector.tensor_tensor(
@@ -226,14 +219,15 @@ def tile_list_flow_residual_refine_kernel(
 
         def interleave(u, cols, tag):
             width = cols.stop - cols.start
-            grouped = keep.tile([P, width * PACK], BF16, name="h_grouped", tag=tag, align_bytes=64)
             if u in GPSIMD_UNITS:
+                grouped = chain.tile([P, width * PACK], BF16, name="h_grouped", tag=tag, align_bytes=64, offset=0)
                 nc.gpsimd.tensor_scalar(
                     grouped[:].rearrange("p (j t) -> p j t", t=PACK),
                     planes[u][:, :, cols].rearrange("p t j -> p j t"),
                     1.0, 0.0, ALU.mult, ALU.add,
                 )
             else:
+                grouped = keep.tile([P, width * PACK], BF16, name="h_grouped", tag=tag, align_bytes=64)
                 nc.vector.tensor_copy(
                     grouped[:].rearrange("p (c i t) -> p c t i", i=4, t=PACK),
                     planes[u][:, :, cols].rearrange("p t (c i) -> p c t i", i=4),
@@ -274,7 +268,11 @@ def tile_list_flow_residual_refine_kernel(
         for u, (c, b) in enumerate(units):
             if u == 0:
                 for t in range(PACK):
-                    squares[u, t] = square(first_products(c, b, t))
+                    if (u, t) in VECTOR_TILES:
+                        sq = ring.tile([P, CHUNK], F32, name="sq", tag="sq", bufs=TILES)
+                        squares[u, t] = square_on_vector(first_products(c, b, t), sq)
+                    else:
+                        squares[u, t] = square(first_products(c, b, t))
                     if t > 0:
                         root(squares[u, t - 1], planes[u], b, t - 1)
                 root_order = [PACK - 1]
@@ -288,9 +286,11 @@ def tile_list_flow_residual_refine_kernel(
                     squares[u, t] = square(accs[t])
                 root_order = own[1:] + own[:1] + [t for t in range(PACK) if t not in own]
             if u >= 1:
-                grouped = interleave(u - 1, whole, "grouped" if u - 1 in GPSIMD_UNITS else "h_grouped%d" % (u - 1))
+                parts = [whole] if u - 1 in GPSIMD_UNITS else [slice(0, CHUNK // 2), slice(CHUNK // 2, CHUNK)]
+                tags = ["grouped"] if u - 1 in GPSIMD_UNITS else ["h_grouped%d_%d" % (u - 1, i) for i in range(2)]
+                grouped = [interleave(u - 1, cols, tag) for cols, tag in zip(parts, tags)]
             if u == 1:
-                held = keep.tile([P, len(HELD_TILES), CHUNK], F32, name="held_squares", tag="w1_raw")
+                held = chain.tile([P, len(HELD_TILES), CHUNK], F32, name="held_squares", align_bytes=64, offset=4096)
             for t in range(PACK):
                 if (u + 1, t) in VECTOR_TILES:
                     if (u + 1, t) in HELD_TILES:
@@ -299,7 +299,8 @@ def tile_list_flow_residual_refine_kernel(
                         sq = ring.tile([P, CHUNK], F32, name="sq", tag="sq", bufs=TILES)
                     squares[u + 1, t] = square_on_vector(first_products(*units[u + 1], t), sq)
             if u >= 1:
-                quantize_h(u - 1, grouped, whole)
+                for part, cols in zip(grouped, parts):
+                    quantize_h(u - 1, part, cols)
             if u == 1:
                 prepare_w3(w3_raw)
             if u > CHUNKS:
@@ -324,7 +325,7 @@ def tile_list_flow_residual_refine_kernel(
             waiting = (grouped, piece)
         quantize_h(last, *waiting)
         store_half(out_accs, CHUNKS - 2, 0, nc.scalar.copy)
-        store_half(out_accs, CHUNKS - 2, 1, nc.vector.tensor_copy)
+        store_half(out_accs, CHUNKS - 2, 1, nc.scalar.copy)
         for piece in LAST_PIECES:
             width = piece.stop - piece.start
             acc = psum.tile([P, CHUNK], F32, name="piece_acc", tag="d_acc", bufs=6)

@@ -55,7 +55,8 @@ def tile_list_flow_residual_refine_kernel(
         nc.sync.dma_start(scale_win2[FIRST_ROW:P, :].bitcast(I32), tab2_scales[0].bitcast(I32))
         nc.vector.memset(scale_win1[0:FIRST_ROW, :].bitcast(I32), 0)
         nc.vector.memset(scale_win2[0:FIRST_ROW, :].bitcast(I32), 0)
-        picked_plane = keep.tile([P, 2 * S], U8, name="picked_plane", align_bytes=64)
+        first_plane = keep.tile([P, 2 * (S - CHUNK)], U8, name="first_plane", align_bytes=64)
+        later_plane = keep.tile([P, 2 * CHUNK], U8, name="later_plane", align_bytes=64)
 
         warm_in = keep.tile([P, 1], F32, name="warm_in")
         warm_out = keep.tile([P, 1], F32, name="warm_out")
@@ -82,7 +83,8 @@ def tile_list_flow_residual_refine_kernel(
         nc.sync.dma_start(word_win2[:], tab2_words[0].rearrange("p t i -> p (t i)").bitcast(I32))
         identity = keep.tile([P, P], F32, name="identity")
         make_identity(nc, identity[:])
-        nc.gpsimd.memset(picked_plane[:].bitcast(I32), 0)
+        nc.gpsimd.memset(first_plane[:].bitcast(I32), 0)
+        nc.gpsimd.memset(later_plane[:].bitcast(I32), 0)
         gain_turned = psum.tile([P, CHUNK], F32, name="gain_turned", tag="d_acc", bufs=6)
         gain_dealt = keep.tile([P, 512], F32, name="gain_dealt")
         nc.scalar.copy(
@@ -114,16 +116,26 @@ def tile_list_flow_residual_refine_kernel(
         picked_rows = keep.tile([P, 2 * S], U8, name="picked_rows", align_bytes=64)
         nc.vector.tensor_copy(picked_rows[:, 0:S], scale_win1[:].indirect(list1[:]))
         nc.vector.tensor_copy(picked_rows[:, S : 2 * S], scale_win2[:].indirect(list2[:]))
-        for quad in range(4):
-            row = FIRST_ROW + 4 * quad
-            nc.sync.dma_start(
-                picked_plane[32 * quad : 32 * quad + 4, :].bitcast(I32), picked_rows[row : row + 4, :].bitcast(I32)
-            )
+        rows_by_table = picked_rows[:].bitcast(I32).rearrange("p (a w) -> p a w", a=2)
+
+        def move_scale_rows(plane, words):
+            for quad in range(4):
+                row = FIRST_ROW + 4 * quad
+                nc.sync.dma_start(
+                    plane[32 * quad : 32 * quad + 4, :].bitcast(I32).rearrange("p (a w) -> p a w", a=2),
+                    rows_by_table[row : row + 4, :, words],
+                )
+
+        move_scale_rows(first_plane, slice(0, (S - CHUNK) // 4))
         w1_raw1 = keep.tile([P, PACK, 512], F32, name="w1_raw1", tag="w1_raw")
         nc.sync.dma_start(w1_raw1[:], w1_rows[:, :, 512:1024])
+        move_scale_rows(later_plane, slice((S - CHUNK) // 4, S // 4))
 
         def table_plane(table, c):
-            return picked_plane[:, table * S + c * CHUNK : table * S + (c + 1) * CHUNK]
+            if c == CHUNKS - 1:
+                return later_plane[:, table * CHUNK : (table + 1) * CHUNK]
+            first = table * (S - CHUNK) + c * CHUNK
+            return first_plane[:, first : first + CHUNK]
 
         w1_codes = keep.tile([P, H], U32, name="w1_codes", align_bytes=64)
         w1_plane = keep.tile([P, H], U8, name="w1_plane", align_bytes=64)
@@ -152,6 +164,14 @@ def tile_list_flow_residual_refine_kernel(
 
         v_words = [gather_words("v_words", word_win1, list1, c) for c in range(CHUNKS)]
         v2_words = [gather_words("v2_words", word_win2, list2, c) for c in range(CHUNKS)]
+
+        warm_acc = psum.tile([P, CHUNK], F32, name="warm_acc", tag="o_acc0")
+        for t in range(4):
+            cols = slice((t % PACK) * P, (t % PACK + 1) * P)
+            nc.tensor.matmul_mx(
+                warm_acc[:], w1_codes[:, cols].bitcast(FP8X4), w1_plane[:, cols],
+                v_words[1][:].bitcast(FP8X4), w1_plane[:, 0:CHUNK], start=True, stop=True,
+            )
 
         def prepare_w1_second_half():
             grouped1 = chain.tile([P, PACK * 512], BF16, name="w1_grouped1", tag="w1_grouped", align_bytes=64, offset=2048)
@@ -266,25 +286,22 @@ def tile_list_flow_residual_refine_kernel(
         whole = slice(0, CHUNK)
         squares = {}
         for u, (c, b) in enumerate(units):
+            behind = None
+            for t in range(PACK):
+                if u == 0 and (u, t) in VECTOR_TILES:
+                    sq = ring.tile([P, CHUNK], F32, name="sq", tag="sq", bufs=TILES)
+                    squares[u, t] = square_on_vector(first_products(c, b, t), sq)
+                elif (u, t) not in squares:
+                    squares[u, t] = square(first_products(c, b, t))
+                    if behind is not None and u < last:
+                        root(squares[u, behind], planes[u], b, behind)
+                    behind = t
+            shared = [t for t in range(PACK) if (u, t) in VECTOR_TILES]
+            root_order = shared[:1] + [behind] + shared[1:] if u < last else list(range(PACK))
             if u == 0:
-                for t in range(PACK):
-                    if (u, t) in VECTOR_TILES:
-                        sq = ring.tile([P, CHUNK], F32, name="sq", tag="sq", bufs=TILES)
-                        squares[u, t] = square_on_vector(first_products(c, b, t), sq)
-                    else:
-                        squares[u, t] = square(first_products(c, b, t))
-                    if t > 0:
-                        root(squares[u, t - 1], planes[u], b, t - 1)
-                root_order = [PACK - 1]
                 w3_raw = load_w3()
                 grouped1 = prepare_w1_second_half()
                 nc.vector.quantize_mx(w1_codes[:, 512:1024].bitcast(FP8X4), w1_plane[:, 512:1024], grouped1[:])
-            else:
-                own = [t for t in range(PACK) if (u, t) not in squares]
-                accs = {t: first_products(c, b, t) for t in own}
-                for t in reversed(own):
-                    squares[u, t] = square(accs[t])
-                root_order = own[1:] + own[:1] + [t for t in range(PACK) if t not in own]
             if u >= 1:
                 parts = [whole] if u - 1 in GPSIMD_UNITS else [slice(0, CHUNK // 2), slice(CHUNK // 2, CHUNK)]
                 tags = ["grouped"] if u - 1 in GPSIMD_UNITS else ["h_grouped%d_%d" % (u - 1, i) for i in range(2)]
@@ -325,7 +342,7 @@ def tile_list_flow_residual_refine_kernel(
             waiting = (grouped, piece)
         quantize_h(last, *waiting)
         store_half(out_accs, CHUNKS - 2, 0, nc.scalar.copy)
-        store_half(out_accs, CHUNKS - 2, 1, nc.scalar.copy)
+        store_half(out_accs, CHUNKS - 2, 1, nc.vector.tensor_copy)
         for piece in LAST_PIECES:
             width = piece.stop - piece.start
             acc = psum.tile([P, CHUNK], F32, name="piece_acc", tag="d_acc", bufs=6)

@@ -20,16 +20,22 @@ AXIS = mybir.AxisListType
 
 P = 128
 PACK = 4
+PASS = P * PACK
 CHUNK = 512
 CHUNKS = S // CHUNK
-HALVES = H // 512
+HALVES = H // PASS
 RUN = 4
-SCALE_ROWS = 16
-FIRST_ROW = P - SCALE_ROWS
-VECTOR_TILES = ((0, 3), (1, 0), (1, 1), (2, 0), (2, 1), (2, 2))
-HELD_TILES = [(2, 0), (2, 1), (2, 2)]
-GPSIMD_UNITS = (0,)
-TILES = CHUNKS * HALVES * PACK
+QUADS = 4
+FIRST_ROW = P - 4 * QUADS
+BANKS = 6
+
+UNITS = [(c, b) for b in range(HALVES) for c in range(CHUNKS)]
+LAST = len(UNITS) - 1
+SQUARES_BESIDE_CAST = [(0, 3), (1, 0), (1, 1)]
+SQUARES_BESIDE_INTERLEAVE = [(2, 0), (2, 1), (2, 2)]
+GPSIMD_COLUMNS = 384
+W1_FIRST_GROUPS = 2
+WARM_PASSES = 5
 LAST_PIECES = [slice(0, 256), slice(256, 384), slice(384, 512)]
 
 
@@ -40,7 +46,9 @@ def tile_list_flow_residual_refine_kernel(
     with ExitStack() as ctx:
         keep = ctx.enter_context(tc.tile_pool(name="keep", bufs=1))
         ring = ctx.enter_context(tc.tile_pool(name="ring", bufs=2))
-        chain = ctx.enter_context(tc.tile_pool(name="chain", bufs=1))
+        after_w1 = ctx.enter_context(tc.tile_pool(name="after_w1", bufs=1))
+        after_w2 = ctx.enter_context(tc.tile_pool(name="after_w2", bufs=1))
+        after_unit3 = ctx.enter_context(tc.tile_pool(name="after_unit3", bufs=1))
         psum = ctx.enter_context(tc.psum_pool(name="psum", bufs=1))
 
         w2_scale_raw = keep.tile([P, H], U8, name="w2_scale_raw")
@@ -48,7 +56,7 @@ def tile_list_flow_residual_refine_kernel(
         list1 = keep.tile([P, S // 16], U16, name="list1")
         list2 = keep.tile([P, S // 16], U16, name="list2")
         scale_win1 = keep.tile([P, T], U8, name="scale_win1")
-        scale_win2 = keep.tile([P, T], U8, name="scale_win2", tag="w1_raw")
+        scale_win2 = keep.tile([P, T], U8, name="scale_win2", tag="scales_then_w1")
         nc.sync.dma_start(list1[:], offs)
         nc.sync.dma_start(scale_win1[FIRST_ROW:P, :].bitcast(I32), tab_scales[0].bitcast(I32))
         nc.sync.dma_start(list2[:], offs2)
@@ -64,29 +72,29 @@ def tile_list_flow_residual_refine_kernel(
         nc.scalar.activation(warm_out[:], warm_in[:], ACT.Sqrt)
 
         word_win1 = keep.tile([P, T], I32, name="word_win1", tag="words_then_w3")
-        w1_rows = w1.rearrange("(p j) r -> p j r", j=PACK)
-        w1_raw0 = keep.tile([P, PACK, 512], F32, name="w1_raw0")
-        w2_raw = keep.tile([P, H // 2], I32, name="w2_raw")
-        gain_rows = keep.tile([P, 512], F32, name="gain_rows")
+        w1_rows = w1.rearrange("(p i) r -> p i r", i=PACK)
+        w1_raw0 = keep.tile([P, PACK, PASS], F32, name="w1_raw0")
+        gain_rows = keep.tile([P, PASS], F32, name="gain_rows")
         nc.sync.dma_start(gain_rows[P - HALVES : P, :], gain.rearrange("(b r) -> b r", b=HALVES))
         nc.gpsimd.memset(gain_rows[0 : P - HALVES, :], 0.0)
-        nc.sync.dma_start(w2_raw[:], w2_words[0].bitcast(I32))
-        nc.sync.dma_start(w1_raw0[:], w1_rows[:, :, 0:512])
+        nc.sync.dma_start(w1_raw0[:], w1_rows[:, :, 0:PASS])
         nc.sync.dma_start(word_win1[:], tab_words[0].rearrange("p t i -> p (t i)").bitcast(I32))
-
-        for quad in range(4):
+        for quad in range(QUADS):
             nc.sync.dma_start(
                 w2_scale_raw[32 * quad : 32 * quad + 4, :].bitcast(I32),
                 w2_scales[0, 4 * quad : 4 * quad + 4, :].bitcast(I32),
             )
         word_win2 = keep.tile([P, T], I32, name="word_win2")
         nc.sync.dma_start(word_win2[:], tab2_words[0].rearrange("p t i -> p (t i)").bitcast(I32))
+        w2_raw = after_w2.tile([P, H // 2], I32, name="w2_raw", align_bytes=64, offset=2 * CHUNK)
+        nc.sync.dma_start(w2_raw[:], w2_words[0].bitcast(I32))
+
         identity = keep.tile([P, P], F32, name="identity")
         make_identity(nc, identity[:])
         nc.gpsimd.memset(first_plane[:].bitcast(I32), 0)
         nc.gpsimd.memset(later_plane[:].bitcast(I32), 0)
-        gain_turned = psum.tile([P, CHUNK], F32, name="gain_turned", tag="d_acc", bufs=6)
-        gain_dealt = keep.tile([P, 512], F32, name="gain_dealt")
+        gain_turned = psum.tile([P, CHUNK], F32, name="gain_turned", tag="bank", bufs=BANKS)
+        gain_dealt = keep.tile([P, PASS], F32, name="gain_dealt")
         nc.scalar.copy(
             gain_dealt[:].rearrange("p (t u e) -> p t u e", t=PACK, e=RUN),
             gain_rows[:].rearrange("p (u t e) -> p t u e", t=PACK, e=RUN),
@@ -105,31 +113,23 @@ def tile_list_flow_residual_refine_kernel(
         nc.gpsimd.tensor_scalar(gain_neg[:], gain_cols[:], 0.0, -2.0, ALU.is_lt, ALU.mult)
         nc.gpsimd.tensor_scalar(gain_sign[:], gain_neg[:], 1.0, 1.0, ALU.mult, ALU.add)
 
-        def list_cols(c):
-            return slice(c * CHUNK // 16, (c + 1) * CHUNK // 16)
-
-        def gather_words(name, window, offsets, c):
-            picked = keep.tile([P, CHUNK], U32, name="%s%d" % (name, c), tag="%s%d" % (name, c), align_bytes=64)
-            nc.vector.tensor_copy(picked[:], window[:].bitcast(U32).indirect(offsets[:, list_cols(c)]))
-            return picked
-
         picked_rows = keep.tile([P, 2 * S], U8, name="picked_rows", align_bytes=64)
         nc.vector.tensor_copy(picked_rows[:, 0:S], scale_win1[:].indirect(list1[:]))
         nc.vector.tensor_copy(picked_rows[:, S : 2 * S], scale_win2[:].indirect(list2[:]))
         rows_by_table = picked_rows[:].bitcast(I32).rearrange("p (a w) -> p a w", a=2)
 
-        def move_scale_rows(plane, words):
-            for quad in range(4):
+        def move_scale_rows(plane, first_entry, end_entry):
+            for quad in range(QUADS):
                 row = FIRST_ROW + 4 * quad
                 nc.sync.dma_start(
                     plane[32 * quad : 32 * quad + 4, :].bitcast(I32).rearrange("p (a w) -> p a w", a=2),
-                    rows_by_table[row : row + 4, :, words],
+                    rows_by_table[row : row + 4, :, first_entry // 4 : end_entry // 4],
                 )
 
-        move_scale_rows(first_plane, slice(0, (S - CHUNK) // 4))
-        w1_raw1 = keep.tile([P, PACK, 512], F32, name="w1_raw1", tag="w1_raw")
-        nc.sync.dma_start(w1_raw1[:], w1_rows[:, :, 512:1024])
-        move_scale_rows(later_plane, slice((S - CHUNK) // 4, S // 4))
+        move_scale_rows(first_plane, 0, S - CHUNK)
+        w1_raw1 = keep.tile([P, PACK, PASS], F32, name="w1_raw1", tag="scales_then_w1")
+        nc.sync.dma_start(w1_raw1[:], w1_rows[:, :, PASS:H])
+        move_scale_rows(later_plane, S - CHUNK, S)
 
         def table_plane(table, c):
             if c == CHUNKS - 1:
@@ -140,49 +140,62 @@ def tile_list_flow_residual_refine_kernel(
         w1_codes = keep.tile([P, H], U32, name="w1_codes", align_bytes=64)
         w1_plane = keep.tile([P, H], U8, name="w1_plane", align_bytes=64)
 
-        def w1_views(raw, grouped, t):
-            src = raw[:].rearrange("p j (u t e) -> p t u j e", t=PACK, e=RUN)[:, t]
-            dst = grouped[:, t * 512 : (t + 1) * 512].rearrange("p (u e j) -> p u j e", e=RUN, j=PACK)
-            return dst, src
+        def w1_cast_tile(name):
+            return after_w1.tile([P, PACK, PASS], BF16, name=name, tag="w1_cast", align_bytes=64, offset=2048)
 
-        grouped0 = chain.tile([P, PACK * 512], BF16, name="w1_grouped0", tag="w1_grouped", align_bytes=64, offset=2048)
+        def quantize_w1(cast, b):
+            cols = slice(b * PASS, (b + 1) * PASS)
+            nc.vector.quantize_mx(w1_codes[:, cols].bitcast(FP8X4), w1_plane[:, cols], cast[:].rearrange("p t x -> p (t x)"))
+
+        w1_cast0 = w1_cast_tile("w1_cast0")
         for t in range(PACK):
-            dst, src = w1_views(w1_raw0, grouped0, t)
-            nc.scalar.activation(dst, src, ACT.Copy, scale=-1.0)
-        nc.vector.quantize_mx(w1_codes[:, 0:512].bitcast(FP8X4), w1_plane[:, 0:512], grouped0[:])
+            nc.scalar.activation(
+                w1_cast0[:, t, :].rearrange("p (u e i) -> p u i e", e=RUN, i=PACK),
+                w1_raw0[:].rearrange("p i (u t e) -> p t u i e", t=PACK, e=RUN)[:, t],
+                ACT.Copy,
+                scale=-1.0,
+            )
+        quantize_w1(w1_cast0, 0)
 
         w2_codes = keep.tile([P, 2 * H], U8, name="w2_codes", align_bytes=64)
         w2_plane = keep.tile([P, H], U8, name="w2_plane", align_bytes=64)
-        nc.vector.tensor_copy(
-            w2_codes[:].bitcast(I32).rearrange("p (b t u w) -> p b t u w", b=HALVES, t=PACK, w=2),
-            w2_raw[:].rearrange("p (b u t w) -> p b t u w", b=HALVES, t=PACK, w=2),
-        )
         nc.vector.tensor_copy(
             w2_plane[:].bitcast(I32).rearrange("p (b t u) -> p b t u", b=HALVES, t=PACK),
             w2_scale_raw[:].bitcast(I32).rearrange("p (b u t) -> p b t u", b=HALVES, t=PACK),
         )
 
-        v_words = [gather_words("v_words", word_win1, list1, c) for c in range(CHUNKS)]
-        v2_words = [gather_words("v2_words", word_win2, list2, c) for c in range(CHUNKS)]
+        def gather_words(picked, window, offsets, c):
+            entries = offsets[:, c * CHUNK // 16 : (c + 1) * CHUNK // 16]
+            nc.vector.tensor_copy(picked[:], window[:].bitcast(U32).indirect(entries))
+            return picked
 
-        warm_acc = psum.tile([P, CHUNK], F32, name="warm_acc", tag="o_acc0")
-        for t in range(4):
-            cols = slice((t % PACK) * P, (t % PACK + 1) * P)
+        v_words = [
+            gather_words(keep.tile([P, CHUNK], U32, name="v_words%d" % c, align_bytes=64), word_win1, list1, c)
+            for c in range(CHUNKS)
+        ]
+        v2_words = [gather_words(keep.tile([P, CHUNK], U32, name="v2_words0", align_bytes=64), word_win2, list2, 0)]
+        nc.vector.tensor_copy(
+            w2_codes[:].bitcast(I32).rearrange("p (b t u w) -> p b t u w", b=HALVES, t=PACK, w=2),
+            w2_raw[:].rearrange("p (b u t w) -> p b t u w", b=HALVES, t=PACK, w=2),
+        )
+        for c in range(1, CHUNKS):
+            picked = after_w2.tile([P, CHUNK], U32, name="v2_words%d" % c, align_bytes=64, offset=(c - 1) * 4 * CHUNK)
+            v2_words.append(gather_words(picked, word_win2, list2, c))
+
+        warm_acc = psum.tile([P, CHUNK], F32, name="warm_acc", tag="out_acc0")
+        for index in range(WARM_PASSES):
+            cols = slice((index % PACK) * P, (index % PACK + 1) * P)
             nc.tensor.matmul_mx(
                 warm_acc[:], w1_codes[:, cols].bitcast(FP8X4), w1_plane[:, cols],
-                v_words[1][:].bitcast(FP8X4), w1_plane[:, 0:CHUNK], start=True, stop=True,
+                v_words[0][:].bitcast(FP8X4), w1_plane[:, 0:CHUNK], start=True, stop=True,
             )
-
-        def prepare_w1_second_half():
-            grouped1 = chain.tile([P, PACK * 512], BF16, name="w1_grouped1", tag="w1_grouped", align_bytes=64, offset=2048)
-            for t in range(PACK):
-                src = w1_raw1[:].rearrange("p j (u t e) -> p t u e j", t=PACK, e=RUN)[:, t]
-                dst = grouped1[:, t * 512 : (t + 1) * 512].rearrange("p (u e j) -> p u e j", e=RUN, j=PACK)
-                nc.gpsimd.tensor_scalar(dst, src, -1.0, 0.0, ALU.mult, ALU.add)
-            return grouped1
 
         w3_codes = keep.tile([P, HALVES * N], U32, name="w3_codes", align_bytes=64)
         w3_plane = keep.tile([P, HALVES * N], U8, name="w3_plane", align_bytes=64)
+        h_codes = [keep.tile([P, CHUNK], U32, name="h_codes%d" % u, align_bytes=64) for u in range(len(UNITS))]
+        h_plane = [keep.tile([P, CHUNK], U8, name="h_plane%d" % u, align_bytes=64) for u in range(len(UNITS))]
+        roots = [keep.tile([P, PACK, CHUNK], BF16, name="roots%d" % u, align_bytes=64) for u in range(len(UNITS))]
+        squares = {}
 
         def load_w3():
             raw = keep.tile([P, HALVES, PACK, N], F32, name="w3_raw", tag="words_then_w3")
@@ -192,168 +205,192 @@ def tile_list_flow_residual_refine_kernel(
                     nc.sync.dma_start(raw[:, b, t, :], rows[b, t])
             return raw
 
-        def prepare_w3(w3_raw):
-            grouped3 = chain.tile([P, HALVES * N * PACK], BF16, name="w3_grouped", tag="grouped", align_bytes=64, offset=0)
+        def prepare_w1_second_half():
+            cast = w1_cast_tile("w1_cast1")
+            for t in range(PACK):
+                nc.gpsimd.tensor_scalar(
+                    cast[:, t, :].rearrange("p (u e i) -> p u e i", e=RUN, i=PACK),
+                    w1_raw1[:].rearrange("p i (u t e) -> p t u e i", t=PACK, e=RUN)[:, t],
+                    -1.0, 0.0, ALU.mult, ALU.add,
+                )
+            quantize_w1(cast, 1)
+
+        def prepare_w3(raw):
+            cast = after_w1.tile([P, HALVES, N * PACK], BF16, name="w3_cast", tag="unit0_then_w3", align_bytes=64, offset=0)
             for b in range(HALVES):
                 sign = gain_sign[:, PACK * b : PACK * (b + 1)].unsqueeze(1).unsqueeze(3).to_broadcast([P, N // 4, PACK, 4])
                 nc.vector.tensor_tensor(
-                    grouped3[:, b * N * PACK : (b + 1) * N * PACK].rearrange("p (c i t) -> p c t i", i=4, t=PACK),
-                    w3_raw[:, b].rearrange("p t (c i) -> p c t i", i=4),
+                    cast[:, b, :].rearrange("p (c i t) -> p c t i", i=4, t=PACK),
+                    raw[:, b].rearrange("p t (c i) -> p c t i", i=4),
                     sign,
                     ALU.mult,
                 )
             for b in range(HALVES):
                 cols = slice(b * N, (b + 1) * N)
-                nc.vector.quantize_mx(
-                    w3_codes[:, cols].bitcast(FP8X4), w3_plane[:, cols], grouped3[:, b * N * PACK : (b + 1) * N * PACK]
-                )
+                nc.vector.quantize_mx(w3_codes[:, cols].bitcast(FP8X4), w3_plane[:, cols], cast[:, b, :])
 
-        def first_products(c, b, t):
-            acc = psum.tile([P, CHUNK], F32, name="d_acc", tag="d_acc", bufs=6)
+        def first_products(u, t):
+            c, b = UNITS[u]
+            bank = psum.tile([P, CHUNK], F32, name="bank", tag="bank", bufs=BANKS)
             cols = slice((PACK * b + t) * P, (PACK * b + t + 1) * P)
             passes = [
                 (w2_codes[:, 2 * cols.start : 2 * cols.stop].bitcast(FP4X4), w2_plane, v2_words, 1),
                 (w1_codes[:, cols].bitcast(FP8X4), w1_plane, v_words, 0),
             ]
-            if (c, b) == (0, 0) and t < 2:
+            if u == 0 and t < W1_FIRST_GROUPS:
                 passes = passes[::-1]
             for index, (codes, plane, words, table) in enumerate(passes):
                 nc.tensor.matmul_mx(
-                    acc[:], codes, plane[:, cols], words[c][:].bitcast(FP8X4),
+                    bank[:], codes, plane[:, cols], words[c][:].bitcast(FP8X4),
                     table_plane(table, c), start=(index == 0), stop=(index == 1),
                 )
-            return acc
+            return bank
 
-        def square(acc):
-            sq = ring.tile([P, CHUNK], F32, name="sq", tag="sq", bufs=TILES)
-            nc.scalar.activation(sq[:], acc[:], ACT.Square)
-            return sq
+        def square_tile():
+            return ring.tile([P, CHUNK], F32, name="square", tag="square", bufs=len(UNITS) * PACK)[:]
 
-        def square_on_vector(acc, sq):
-            nc.vector.tensor_reduce(sq[:], acc[:].unsqueeze(2).to_broadcast([P, CHUNK, 2]), AXIS.X, ALU.mult)
-            return sq
+        def square_on_scalar(u, t):
+            bank = first_products(u, t)
+            squares[u, t] = square_tile()
+            nc.scalar.activation(squares[u, t], bank[:], ACT.Square)
 
-        def root(sq, planes, b, t, cols=slice(0, CHUNK)):
-            g2 = gain_sq[:, PACK * b + t : PACK * b + t + 1]
-            nc.scalar.activation(planes[:, t, cols], sq[:, cols], ACT.Sqrt, bias=g2, scale=g2)
+        def square_on_vector(u, t, square):
+            bank = first_products(u, t)
+            squares[u, t] = square
+            nc.vector.tensor_reduce(square, bank[:].unsqueeze(2).to_broadcast([P, CHUNK, 2]), AXIS.X, ALU.mult)
 
-        def interleave(u, cols, tag):
-            width = cols.stop - cols.start
-            if u in GPSIMD_UNITS:
-                grouped = chain.tile([P, width * PACK], BF16, name="h_grouped", tag=tag, align_bytes=64, offset=0)
-                nc.gpsimd.tensor_scalar(
-                    grouped[:].rearrange("p (j t) -> p j t", t=PACK),
-                    planes[u][:, :, cols].rearrange("p t j -> p j t"),
-                    1.0, 0.0, ALU.mult, ALU.add,
-                )
-            else:
-                grouped = keep.tile([P, width * PACK], BF16, name="h_grouped", tag=tag, align_bytes=64)
-                nc.vector.tensor_copy(
-                    grouped[:].rearrange("p (c i t) -> p c t i", i=4, t=PACK),
-                    planes[u][:, :, cols].rearrange("p t (c i) -> p c t i", i=4),
-                )
-            return grouped
+        def root(u, t, cols):
+            column = PACK * UNITS[u][1] + t
+            g2 = gain_sq[:, column : column + 1]
+            nc.scalar.activation(roots[u][:, t, cols], squares[u, t][:, cols], ACT.Sqrt, bias=g2, scale=g2)
 
-        h_codes = [keep.tile([P, CHUNK], U32, name="h_codes%d" % u, align_bytes=64) for u in range(CHUNKS * HALVES)]
-        h_plane = [keep.tile([P, CHUNK], U8, name="h_plane%d" % u, align_bytes=64) for u in range(CHUNKS * HALVES)]
+        def interleave_on_vector(words, u, cols):
+            nc.vector.tensor_copy(
+                words.rearrange("p (c i) t -> p c t i", i=4), roots[u][:, :, cols].rearrange("p t (c i) -> p c t i", i=4)
+            )
 
-        def quantize_h(u, grouped, cols):
-            nc.vector.quantize_mx(h_codes[u][:, cols].bitcast(FP8X4), h_plane[u][:, cols], grouped[:])
+        def interleave_on_gpsimd(words, u, cols):
+            nc.gpsimd.tensor_scalar(words, roots[u][:, :, cols].rearrange("p t j -> p j t"), 1.0, 0.0, ALU.mult, ALU.add)
+
+        def quantize_h(words, u, cols):
+            nc.vector.quantize_mx(h_codes[u][:, cols].bitcast(FP8X4), h_plane[u][:, cols], words.rearrange("p j t -> p (j t)"))
 
         def last_product(acc, c, half, b, cols, start, stop):
             w_cols = slice(b * N + half * P, b * N + (half + 1) * P)
-            u = b * CHUNKS + c
+            u = UNITS.index((c, b))
             nc.tensor.matmul_mx(
                 acc, w3_codes[:, w_cols].bitcast(FP8X4), w3_plane[:, w_cols],
                 h_codes[u][:, cols].bitcast(FP8X4), h_plane[u][:, cols], start=start, stop=stop,
             )
 
+        whole = slice(0, CHUNK)
+        halves_of_chunk = [slice(0, CHUNK // 2), slice(CHUNK // 2, CHUNK)]
+
         def multiply_chunk(c):
-            accs = [psum.tile([P, CHUNK], F32, name="o_acc%d" % half, tag="o_acc%d" % half) for half in range(N // P)]
+            accs = [psum.tile([P, CHUNK], F32, name="out_acc%d" % half, tag="out_acc%d" % half) for half in range(N // P)]
             for half in range(N // P):
                 for b in range(HALVES):
-                    last_product(accs[half][:], c, half, b, slice(0, CHUNK), b == 0, b == HALVES - 1)
+                    last_product(accs[half][:], c, half, b, whole, b == 0, b == HALVES - 1)
             return accs
 
-        def store_half(accs, c, half, copy):
-            res = ring.tile([P, CHUNK], F32, name="res", bufs=7)
-            copy(res[:], accs[half][:])
-            nc.sync.dma_start(out[half * P : (half + 1) * P, c * CHUNK : (c + 1) * CHUNK], res[:])
+        def result_tile(width):
+            return ring.tile([P, width], F32, name="result", tag="result", bufs=7)
 
-        units = [(c, b) for b in range(HALVES) for c in range(CHUNKS)]
-        last = len(units) - 1
-        planes = [keep.tile([P, PACK, CHUNK], BF16, name="h_planes%d" % u, tag="h_planes%d" % u, align_bytes=64) for u in range(len(units))]
-        whole = slice(0, CHUNK)
-        squares = {}
-        for u, (c, b) in enumerate(units):
+        def store_half(accs, c, half, copy):
+            result = result_tile(CHUNK)
+            copy(result[:], accs[half][:])
+            nc.sync.dma_start(out[half * P : (half + 1) * P, c * CHUNK : (c + 1) * CHUNK], result[:])
+
+        def open_unit(u):
+            by_vector = [t for t in range(PACK) if (u, t) in squares or (u, t) in SQUARES_BESIDE_CAST]
             behind = None
             for t in range(PACK):
-                if u == 0 and (u, t) in VECTOR_TILES:
-                    sq = ring.tile([P, CHUNK], F32, name="sq", tag="sq", bufs=TILES)
-                    squares[u, t] = square_on_vector(first_products(c, b, t), sq)
-                elif (u, t) not in squares:
-                    squares[u, t] = square(first_products(c, b, t))
-                    if behind is not None and u < last:
-                        root(squares[u, behind], planes[u], b, behind)
+                if t not in by_vector:
+                    square_on_scalar(u, t)
+                    if behind is not None and u < LAST:
+                        root(u, behind, whole)
                     behind = t
-            shared = [t for t in range(PACK) if (u, t) in VECTOR_TILES]
-            root_order = shared[:1] + [behind] + shared[1:] if u < last else list(range(PACK))
-            if u == 0:
-                w3_raw = load_w3()
-                grouped1 = prepare_w1_second_half()
-                nc.vector.quantize_mx(w1_codes[:, 512:1024].bitcast(FP8X4), w1_plane[:, 512:1024], grouped1[:])
-            if u >= 1:
-                parts = [whole] if u - 1 in GPSIMD_UNITS else [slice(0, CHUNK // 2), slice(CHUNK // 2, CHUNK)]
-                tags = ["grouped"] if u - 1 in GPSIMD_UNITS else ["h_grouped%d_%d" % (u - 1, i) for i in range(2)]
-                grouped = [interleave(u - 1, cols, tag) for cols, tag in zip(parts, tags)]
-            if u == 1:
-                held = chain.tile([P, len(HELD_TILES), CHUNK], F32, name="held_squares", align_bytes=64, offset=4096)
-            for t in range(PACK):
-                if (u + 1, t) in VECTOR_TILES:
-                    if (u + 1, t) in HELD_TILES:
-                        sq = held[:, HELD_TILES.index((u + 1, t)), :]
-                    else:
-                        sq = ring.tile([P, CHUNK], F32, name="sq", tag="sq", bufs=TILES)
-                    squares[u + 1, t] = square_on_vector(first_products(*units[u + 1], t), sq)
-            if u >= 1:
-                for part, cols in zip(grouped, parts):
-                    quantize_h(u - 1, part, cols)
-            if u == 1:
-                prepare_w3(w3_raw)
-            if u > CHUNKS:
-                out_accs = multiply_chunk(u - 1 - CHUNKS)
-                if u < last:
-                    for half in reversed(range(N // P)):
-                        store_half(out_accs, u - 1 - CHUNKS, half, nc.vector.tensor_copy)
-            if u < last:
-                for t in root_order:
-                    root(squares[u, t], planes[u], b, t)
+                elif (u, t) not in squares:
+                    square_on_vector(u, t, square_tile())
+            return by_vector[:1] + [behind] + by_vector[1:]
 
+        def close_unit(u, waiting):
+            for t in waiting:
+                root(u, t, whole)
+
+        def finish_on_vector(u, last_half=None):
+            words = [keep.tile([P, CHUNK // 2, PACK], BF16, name="words%d_0" % u, align_bytes=64)]
+            words.append(last_half or keep.tile([P, CHUNK // 2, PACK], BF16, name="words%d_1" % u, align_bytes=64))
+            for part, cols in zip(words, halves_of_chunk):
+                interleave_on_vector(part[:], u, cols)
+            for part, cols in zip(words, halves_of_chunk):
+                quantize_h(part[:], u, cols)
+
+        waiting = open_unit(0)
+        w3_raw = load_w3()
+        prepare_w1_second_half()
+        for u, t in SQUARES_BESIDE_CAST:
+            if u == 1:
+                square_on_vector(u, t, square_tile())
+        close_unit(0, waiting)
+
+        waiting = open_unit(1)
+        words0 = after_w1.tile([P, CHUNK, PACK], BF16, name="words0", tag="unit0_then_w3", align_bytes=64, offset=0)
+        interleave_on_gpsimd(words0[:], 0, whole)
+        held = after_w1.tile([P, len(SQUARES_BESIDE_INTERLEAVE), CHUNK], F32, name="held", align_bytes=64, offset=4096)
+        for index, (u, t) in enumerate(SQUARES_BESIDE_INTERLEAVE):
+            square_on_vector(u, t, held[:, index, :])
+        quantize_h(words0[:], 0, whole)
+        prepare_w3(w3_raw)
+        close_unit(1, waiting)
+
+        waiting = open_unit(2)
+        finish_on_vector(1)
+        close_unit(2, waiting)
+        close_unit(3, open_unit(3))
+
+        waiting = open_unit(4)
+        finish_on_vector(3, after_unit3.tile([P, CHUNK // 2, PACK], BF16, name="words3_1", align_bytes=64, offset=3072))
+        words2 = after_unit3.tile([P, CHUNK, PACK], BF16, name="words2", align_bytes=64, offset=0)
+        interleave_on_gpsimd(words2[:, 0:GPSIMD_COLUMNS, :], 2, slice(0, GPSIMD_COLUMNS))
+        late_square = after_unit3.tile([P, CHUNK], F32, name="late_square", align_bytes=64, offset=4096)
+        square_on_vector(LAST, 0, late_square[:])
+        accs = multiply_chunk(0)
+        for half in reversed(range(N // P)):
+            store_half(accs, 0, half, nc.vector.tensor_copy)
+        interleave_on_vector(words2[:, GPSIMD_COLUMNS:CHUNK, :], 2, slice(GPSIMD_COLUMNS, CHUNK))
+        quantize_h(words2[:], 2, whole)
+        close_unit(4, waiting)
+
+        open_unit(LAST)
+        finish_on_vector(4)
+        accs = multiply_chunk(1)
+        for piece in LAST_PIECES:
+            for t in range(PACK):
+                root(LAST, t, piece)
+        interleaved = None
+        for index, piece in enumerate(LAST_PIECES):
+            words = keep.tile([P, piece.stop - piece.start, PACK], BF16, name="piece_words%d" % index, align_bytes=64)
+            interleave_on_vector(words[:], LAST, piece)
+            if interleaved is not None:
+                quantize_h(*interleaved)
+            interleaved = (words[:], LAST, piece)
+        quantize_h(*interleaved)
+        for half in range(N // P):
+            store_half(accs, 1, half, nc.scalar.copy)
         out_halves = out.rearrange("(h p) j -> p h j", p=P)
         first_col = (CHUNKS - 1) * CHUNK
         for piece in LAST_PIECES:
-            for t in root_order:
-                root(squares[last, t], planes[last], HALVES - 1, t, piece)
-        waiting = None
-        for index, piece in enumerate(LAST_PIECES):
-            grouped = interleave(last, piece, "piece_grouped%d" % index)
-            if waiting is not None:
-                quantize_h(last, *waiting)
-            waiting = (grouped, piece)
-        quantize_h(last, *waiting)
-        store_half(out_accs, CHUNKS - 2, 0, nc.scalar.copy)
-        store_half(out_accs, CHUNKS - 2, 1, nc.vector.tensor_copy)
-        for piece in LAST_PIECES:
             width = piece.stop - piece.start
-            acc = psum.tile([P, CHUNK], F32, name="piece_acc", tag="d_acc", bufs=6)
+            bank = psum.tile([P, CHUNK], F32, name="piece_bank", tag="bank", bufs=BANKS)
             for b in range(HALVES):
                 for half in range(N // P):
                     first, final = (b, half) == (0, 0), (b, half) == (HALVES - 1, N // P - 1)
-                    last_product(acc[:, half * width : (half + 1) * width], CHUNKS - 1, half, b, piece, first, final)
-            res = ring.tile([P, (N // P) * width], F32, name="res", bufs=7)
-            nc.scalar.copy(res[:], acc[:, 0 : (N // P) * width])
+                    last_product(bank[:, half * width : (half + 1) * width], CHUNKS - 1, half, b, piece, first, final)
+            result = result_tile((N // P) * width)
+            nc.scalar.copy(result[:], bank[:, 0 : (N // P) * width])
             queue = nc.scalar if piece.stop == CHUNK else nc.sync
             queue.dma_start(
                 out_halves[:, :, first_col + piece.start : first_col + piece.stop],
-                res[:].rearrange("p (h j) -> p h j", j=width),
+                result[:].rearrange("p (h j) -> p h j", j=width),
             )

@@ -103,15 +103,18 @@ def tile_list_flow_residual_refine_kernel(
             nc.tensor.transpose(gain_turned[:, t * P : (t + 1) * P], gain_dealt[:, t * P : (t + 1) * P], identity[:])
         gain_cols = keep.tile([P, HALVES * PACK], F32, name="gain_cols")
         gain_sq = keep.tile([P, HALVES * PACK], F32, name="gain_sq")
-        gain_neg = keep.tile([P, HALVES * PACK], F32, name="gain_neg")
-        gain_sign = keep.tile([P, HALVES * PACK], F32, name="gain_sign")
         nc.scalar.copy(
             gain_cols[:].rearrange("p (b t) -> p b t", t=PACK),
             gain_turned[:].rearrange("p (t x) -> p x t", x=P)[:, P - HALVES : P, :],
         )
         nc.gpsimd.tensor_tensor(gain_sq[:], gain_cols[:], gain_cols[:], ALU.mult)
-        nc.gpsimd.tensor_scalar(gain_neg[:], gain_cols[:], 0.0, -2.0, ALU.is_lt, ALU.mult)
-        nc.gpsimd.tensor_scalar(gain_sign[:], gain_neg[:], 1.0, 1.0, ALU.mult, ALU.add)
+        sign_raw = keep.tile([P, PASS], F32, name="sign_raw")
+        sign_dealt = keep.tile([P, PASS], F32, name="sign_dealt")
+        nc.scalar.activation(sign_raw[:], gain_dealt[:], ACT.Sign)
+        nc.scalar.activation(sign_dealt[:], sign_raw[:], ACT.Sign, bias=0.5)
+        sign_turned = psum.tile([P, CHUNK], F32, name="sign_turned", tag="out_acc1")
+        for t in range(PACK):
+            nc.tensor.transpose(sign_turned[:, t * P : (t + 1) * P], sign_dealt[:, t * P : (t + 1) * P], identity[:])
 
         picked_rows = keep.tile([P, 2 * S], U8, name="picked_rows", align_bytes=64)
         nc.vector.tensor_copy(picked_rows[:, 0:S], scale_win1[:].indirect(list1[:]))
@@ -141,7 +144,7 @@ def tile_list_flow_residual_refine_kernel(
         w1_plane = keep.tile([P, H], U8, name="w1_plane", align_bytes=64)
 
         def w1_cast_tile(name):
-            return after_w1.tile([P, PACK, PASS], BF16, name=name, tag="w1_cast", align_bytes=64, offset=2048)
+            return after_w1.tile([P, PACK, PASS], BF16, name=name, tag="w1_cast", align_bytes=64, offset=7168)
 
         def quantize_w1(cast, b):
             cols = slice(b * PASS, (b + 1) * PASS)
@@ -215,16 +218,21 @@ def tile_list_flow_residual_refine_kernel(
                 )
             quantize_w1(cast, 1)
 
-        def prepare_w3(raw):
-            cast = after_w1.tile([P, HALVES, N * PACK], BF16, name="w3_cast", tag="unit0_then_w3", align_bytes=64, offset=0)
+        def cast_w3(raw):
+            cast = after_w1.tile([P, HALVES, N * PACK], BF16, name="w3_cast", align_bytes=64, offset=6208)
+            signs = sign_turned[:].rearrange("p (t x) -> p t x", x=P)
             for b in range(HALVES):
-                sign = gain_sign[:, PACK * b : PACK * (b + 1)].unsqueeze(1).unsqueeze(3).to_broadcast([P, N // 4, PACK, 4])
+                column = P - HALVES + b
+                sign = signs[:, :, column : column + 1].unsqueeze(1).to_broadcast([P, N // 4, PACK, 4])
                 nc.vector.tensor_tensor(
                     cast[:, b, :].rearrange("p (c i t) -> p c t i", i=4, t=PACK),
                     raw[:, b].rearrange("p t (c i) -> p c t i", i=4),
                     sign,
                     ALU.mult,
                 )
+            return cast
+
+        def quantize_w3(cast):
             for b in range(HALVES):
                 cols = slice(b * N, (b + 1) * N)
                 nc.vector.quantize_mx(w3_codes[:, cols].bitcast(FP8X4), w3_plane[:, cols], cast[:, b, :])
@@ -335,17 +343,22 @@ def tile_list_flow_residual_refine_kernel(
         close_unit(0, waiting)
 
         waiting = open_unit(1)
-        words0 = after_w1.tile([P, CHUNK, PACK], BF16, name="words0", tag="unit0_then_w3", align_bytes=64, offset=0)
+        words0 = after_w1.tile([P, CHUNK, PACK], BF16, name="words0", align_bytes=64, offset=4096)
         interleave_on_gpsimd(words0[:], 0, whole)
-        held = after_w1.tile([P, len(SQUARES_BESIDE_INTERLEAVE), CHUNK], F32, name="held", align_bytes=64, offset=4096)
+        held = after_w1.tile([P, len(SQUARES_BESIDE_INTERLEAVE), CHUNK], F32, name="held", align_bytes=64, offset=10304)
         for index, (u, t) in enumerate(SQUARES_BESIDE_INTERLEAVE):
             square_on_vector(u, t, held[:, index, :])
         quantize_h(words0[:], 0, whole)
-        prepare_w3(w3_raw)
         close_unit(1, waiting)
 
         waiting = open_unit(2)
-        finish_on_vector(1)
+        words1 = after_w1.tile([P, CHUNK, PACK], BF16, name="words1", align_bytes=64, offset=64)
+        interleave_on_gpsimd(words1[:], 1, whole)
+        square30 = after_w1.tile([P, CHUNK], F32, name="square30", align_bytes=64, offset=4160)
+        square_on_vector(3, 0, square30[:])
+        w3_cast = cast_w3(w3_raw)
+        quantize_h(words1[:], 1, whole)
+        quantize_w3(w3_cast)
         close_unit(2, waiting)
         close_unit(3, open_unit(3))
 

@@ -27,11 +27,13 @@ HALVES = H // PASS
 RUN = 4
 QUADS = 4
 FIRST_ROW = P - 4 * QUADS
+FIRST_ROW1 = 64 - 4 * QUADS
+PLANE1_ROW = 4
 BANKS = 6
 
 UNITS = [(c, b) for b in range(HALVES) for c in range(CHUNKS)]
 LAST = len(UNITS) - 1
-SQUARES_BESIDE_CAST = [(0, 3), (1, 0), (1, 1)]
+SQUARES_BESIDE_CAST = [(1, 0), (1, 1), (1, 2)]
 SQUARES_BESIDE_INTERLEAVE = [(2, 0), (2, 1), (2, 2)]
 GPSIMD_COLUMNS = 384
 W1_FIRST_GROUPS = 2
@@ -48,6 +50,7 @@ def tile_list_flow_residual_refine_kernel(
         ring = ctx.enter_context(tc.tile_pool(name="ring", bufs=2))
         after_w1 = ctx.enter_context(tc.tile_pool(name="after_w1", bufs=1))
         after_w2 = ctx.enter_context(tc.tile_pool(name="after_w2", bufs=1))
+        after_s1 = ctx.enter_context(tc.tile_pool(name="after_s1", bufs=1))
         after_unit3 = ctx.enter_context(tc.tile_pool(name="after_unit3", bufs=1))
         psum = ctx.enter_context(tc.psum_pool(name="psum", bufs=1))
 
@@ -55,16 +58,17 @@ def tile_list_flow_residual_refine_kernel(
         nc.gpsimd.memset(w2_scale_raw[:].bitcast(I32), 0)
         list1 = keep.tile([P, S // 16], U16, name="list1")
         list2 = keep.tile([P, S // 16], U16, name="list2")
-        scale_win1 = keep.tile([P, T], U8, name="scale_win1")
-        scale_win2 = keep.tile([P, T], U8, name="scale_win2", tag="scales_then_w1")
+        scale_win1 = after_s1.tile([P, T], U8, name="scale_win1", align_bytes=64, offset=16384)
+        scale_win2 = after_w2.tile([P, T], U8, name="scale_win2", align_bytes=64, offset=8192)
         nc.sync.dma_start(list1[:], offs)
-        nc.sync.dma_start(scale_win1[FIRST_ROW:P, :].bitcast(I32), tab_scales[0].bitcast(I32))
+        nc.sync.dma_start(scale_win1[FIRST_ROW1:64, :].bitcast(I32), tab_scales[0].bitcast(I32))
         nc.sync.dma_start(list2[:], offs2)
         nc.sync.dma_start(scale_win2[FIRST_ROW:P, :].bitcast(I32), tab2_scales[0].bitcast(I32))
-        nc.vector.memset(scale_win1[0:FIRST_ROW, :].bitcast(I32), 0)
+        nc.vector.memset(scale_win1[0:FIRST_ROW1, :].bitcast(I32), 0)
+        nc.vector.memset(scale_win1[64:P, :].bitcast(I32), 0)
         nc.vector.memset(scale_win2[0:FIRST_ROW, :].bitcast(I32), 0)
-        first_plane = keep.tile([P, 2 * (S - CHUNK)], U8, name="first_plane", align_bytes=64)
-        later_plane = keep.tile([P, 2 * CHUNK], U8, name="later_plane", align_bytes=64)
+        plane1 = keep.tile([P, S], U8, name="plane1", align_bytes=64)
+        plane2 = keep.tile([P, S], U8, name="plane2", align_bytes=64)
 
         warm_in = keep.tile([P, 1], F32, name="warm_in")
         warm_out = keep.tile([P, 1], F32, name="warm_out")
@@ -84,15 +88,11 @@ def tile_list_flow_residual_refine_kernel(
                 w2_scale_raw[32 * quad : 32 * quad + 4, :].bitcast(I32),
                 w2_scales[0, 4 * quad : 4 * quad + 4, :].bitcast(I32),
             )
-        word_win2 = keep.tile([P, T], I32, name="word_win2")
-        nc.sync.dma_start(word_win2[:], tab2_words[0].rearrange("p t i -> p (t i)").bitcast(I32))
-        w2_raw = after_w2.tile([P, H // 2], I32, name="w2_raw", align_bytes=64, offset=2 * CHUNK)
-        nc.sync.dma_start(w2_raw[:], w2_words[0].bitcast(I32))
 
         identity = keep.tile([P, P], F32, name="identity")
         make_identity(nc, identity[:])
-        nc.gpsimd.memset(first_plane[:].bitcast(I32), 0)
-        nc.gpsimd.memset(later_plane[:].bitcast(I32), 0)
+        nc.gpsimd.memset(plane1[:].bitcast(I32), 0)
+        nc.gpsimd.memset(plane2[:].bitcast(I32), 0)
         gain_turned = psum.tile([P, CHUNK], F32, name="gain_turned", tag="bank", bufs=BANKS)
         gain_dealt = keep.tile([P, PASS], F32, name="gain_dealt")
         nc.scalar.copy(
@@ -116,29 +116,34 @@ def tile_list_flow_residual_refine_kernel(
         for t in range(PACK):
             nc.tensor.transpose(sign_turned[:, t * P : (t + 1) * P], sign_dealt[:, t * P : (t + 1) * P], identity[:])
 
-        picked_rows = keep.tile([P, 2 * S], U8, name="picked_rows", align_bytes=64)
-        nc.vector.tensor_copy(picked_rows[:, 0:S], scale_win1[:].indirect(list1[:]))
-        nc.vector.tensor_copy(picked_rows[:, S : 2 * S], scale_win2[:].indirect(list2[:]))
-        rows_by_table = picked_rows[:].bitcast(I32).rearrange("p (a w) -> p a w", a=2)
+        picked1 = keep.tile([P, S], U8, name="picked1", align_bytes=64)
+        picked2 = keep.tile([P, S], U8, name="picked2", align_bytes=64)
+        nc.vector.tensor_copy(picked1[:], scale_win1[:].indirect(list1[:]))
+        nc.vector.tensor_copy(picked2[:], scale_win2[:].indirect(list2[:]))
 
-        def move_scale_rows(plane, first_entry, end_entry):
+        def move_scale_rows(plane, plane_row, picked, first_row):
             for quad in range(QUADS):
-                row = FIRST_ROW + 4 * quad
-                nc.sync.dma_start(
-                    plane[32 * quad : 32 * quad + 4, :].bitcast(I32).rearrange("p (a w) -> p a w", a=2),
-                    rows_by_table[row : row + 4, :, first_entry // 4 : end_entry // 4],
-                )
+                row = first_row + 4 * quad
+                to = 32 * quad + plane_row
+                nc.sync.dma_start(plane[to : to + 4, :].bitcast(I32), picked[row : row + 4, :].bitcast(I32))
 
-        move_scale_rows(first_plane, 0, S - CHUNK)
-        w1_raw1 = keep.tile([P, PACK, PASS], F32, name="w1_raw1", tag="scales_then_w1")
+        def load_w2(b, pool, offset):
+            raw = pool.tile([P, PASS // 2], I32, name="w2_raw%d" % b, align_bytes=64, offset=offset)
+            nc.sync.dma_start(raw[:], w2_words[0].bitcast(I32)[:, b * PASS // 2 : (b + 1) * PASS // 2])
+            return raw
+
+        move_scale_rows(plane1, PLANE1_ROW, picked1, FIRST_ROW1)
+        word_win2 = after_s1.tile([P, T], I32, name="word_win2", align_bytes=64, offset=64)
+        nc.sync.dma_start(word_win2[:], tab2_words[0].rearrange("p t i -> p (t i)").bitcast(I32))
+        w2_raw0 = load_w2(0, after_s1, 16448 + 512)
+        move_scale_rows(plane2, 0, picked2, FIRST_ROW)
+        w1_raw1 = after_w2.tile([P, PACK, PASS], F32, name="w1_raw1", align_bytes=64, offset=64)
         nc.sync.dma_start(w1_raw1[:], w1_rows[:, :, PASS:H])
-        move_scale_rows(later_plane, S - CHUNK, S)
+        w2_raw1 = load_w2(1, after_w2, 8192 + 64)
 
         def table_plane(table, c):
-            if c == CHUNKS - 1:
-                return later_plane[:, table * CHUNK : (table + 1) * CHUNK]
-            first = table * (S - CHUNK) + c * CHUNK
-            return first_plane[:, first : first + CHUNK]
+            cols = slice(c * CHUNK, (c + 1) * CHUNK)
+            return plane2[:, cols] if table == 1 else plane1[PLANE1_ROW:P, cols]
 
         w1_codes = keep.tile([P, H], U32, name="w1_codes", align_bytes=64)
         w1_plane = keep.tile([P, H], U8, name="w1_plane", align_bytes=64)
@@ -160,37 +165,43 @@ def tile_list_flow_residual_refine_kernel(
             )
         quantize_w1(w1_cast0, 0)
 
-        w2_codes = keep.tile([P, 2 * H], U8, name="w2_codes", align_bytes=64)
+        w2_codes = [keep.tile([P, 2 * PASS], U8, name="w2_codes0", align_bytes=64)]
+
+        def deal_w2(b, raw):
+            nc.vector.tensor_copy(
+                w2_codes[b][:].bitcast(I32).rearrange("p (t u w) -> p t u w", t=PACK, w=2),
+                raw[:].rearrange("p (u t w) -> p t u w", t=PACK, w=2),
+            )
+
         w2_plane = keep.tile([P, H], U8, name="w2_plane", align_bytes=64)
         nc.vector.tensor_copy(
             w2_plane[:].bitcast(I32).rearrange("p (b t u) -> p b t u", b=HALVES, t=PACK),
             w2_scale_raw[:].bitcast(I32).rearrange("p (b u t) -> p b t u", b=HALVES, t=PACK),
         )
 
-        def gather_words(picked, window, offsets, c):
-            entries = offsets[:, c * CHUNK // 16 : (c + 1) * CHUNK // 16]
-            nc.vector.tensor_copy(picked[:], window[:].bitcast(U32).indirect(entries))
+        def gather_words(picked, window, offsets, first, count):
+            entries = offsets[:, first // 16 : (first + count) // 16]
+            nc.vector.tensor_copy(picked, window[:].bitcast(U32).indirect(entries))
             return picked
 
         v_words = [
-            gather_words(keep.tile([P, CHUNK], U32, name="v_words%d" % c, align_bytes=64), word_win1, list1, c)
+            gather_words(keep.tile([P, CHUNK], U32, name="v_words%d" % c, align_bytes=64)[:], word_win1, list1, c * CHUNK, CHUNK)
             for c in range(CHUNKS)
         ]
-        v2_words = [gather_words(keep.tile([P, CHUNK], U32, name="v2_words0", align_bytes=64), word_win2, list2, 0)]
-        nc.vector.tensor_copy(
-            w2_codes[:].bitcast(I32).rearrange("p (b t u w) -> p b t u w", b=HALVES, t=PACK, w=2),
-            w2_raw[:].rearrange("p (b u t w) -> p b t u w", b=HALVES, t=PACK, w=2),
-        )
-        for c in range(1, CHUNKS):
-            picked = after_w2.tile([P, CHUNK], U32, name="v2_words%d" % c, align_bytes=64, offset=(c - 1) * 4 * CHUNK)
-            v2_words.append(gather_words(picked, word_win2, list2, c))
+        HALF = CHUNK // 2
+        v2_first = [gather_words(keep.tile([P, HALF], U32, name="v2_first0", align_bytes=64)[:], word_win2, list2, 0, HALF)]
+        deal_w2(0, w2_raw0)
+        picked = after_s1.tile([P, HALF], U32, name="v2_first1", align_bytes=64, offset=16448)
+        v2_first.append(gather_words(picked[:], word_win2, list2, HALF, HALF))
+        picked = after_s1.tile([P, CHUNKS - 1, CHUNK], U32, name="v2_later", align_bytes=64, offset=16448 + 1024)
+        v2_words = [None] + [gather_words(picked[:, c - 1, :], word_win2, list2, c * CHUNK, CHUNK) for c in range(1, CHUNKS)]
 
         warm_acc = psum.tile([P, CHUNK], F32, name="warm_acc", tag="out_acc0")
         for index in range(WARM_PASSES):
             cols = slice((index % PACK) * P, (index % PACK + 1) * P)
             nc.tensor.matmul_mx(
                 warm_acc[:], w1_codes[:, cols].bitcast(FP8X4), w1_plane[:, cols],
-                v_words[0][:].bitcast(FP8X4), w1_plane[:, 0:CHUNK], start=True, stop=True,
+                v_words[0].bitcast(FP8X4), w1_plane[:, 0:CHUNK], start=True, stop=True,
             )
 
         w3_codes = keep.tile([P, HALVES * N], U32, name="w3_codes", align_bytes=64)
@@ -210,12 +221,13 @@ def tile_list_flow_residual_refine_kernel(
 
         def prepare_w1_second_half():
             cast = w1_cast_tile("w1_cast1")
-            for t in range(PACK):
-                nc.gpsimd.tensor_scalar(
-                    cast[:, t, :].rearrange("p (u e i) -> p u e i", e=RUN, i=PACK),
-                    w1_raw1[:].rearrange("p i (u t e) -> p t u e i", t=PACK, e=RUN)[:, t],
-                    -1.0, 0.0, ALU.mult, ALU.add,
-                )
+            nc.gpsimd.tensor_scalar(
+                cast[:].rearrange("p t (u e i) -> p u t e i", e=RUN, i=PACK),
+                w1_raw1[:].rearrange("p i (u t e) -> p u t e i", t=PACK, e=RUN),
+                -1.0, 0.0, ALU.mult, ALU.add,
+            )
+            w2_codes.append(after_w2.tile([P, 2 * PASS], U8, name="w2_codes1", align_bytes=64, offset=64))
+            deal_w2(1, w2_raw1)
             quantize_w1(cast, 1)
 
         def cast_w3(raw):
@@ -237,22 +249,46 @@ def tile_list_flow_residual_refine_kernel(
                 cols = slice(b * N, (b + 1) * N)
                 nc.vector.quantize_mx(w3_codes[:, cols].bitcast(FP8X4), w3_plane[:, cols], cast[:, b, :])
 
+        def product_pair(acc, b, t, words1, plane1, words2, plane2, w1_first):
+            cols = slice((PACK * b + t) * P, (PACK * b + t + 1) * P)
+            passes = [
+                (w2_codes[b][:, 2 * t * P : 2 * (t + 1) * P].bitcast(FP4X4), w2_plane, words2, plane2),
+                (w1_codes[:, cols].bitcast(FP8X4), w1_plane, words1, plane1),
+            ]
+            if w1_first:
+                passes = passes[::-1]
+            for index, (codes, plane, words, moving_plane) in enumerate(passes):
+                nc.tensor.matmul_mx(
+                    acc, codes, plane[:, cols], words.bitcast(FP8X4), moving_plane, start=(index == 0), stop=(index == 1)
+                )
+
         def first_products(u, t):
             c, b = UNITS[u]
             bank = psum.tile([P, CHUNK], F32, name="bank", tag="bank", bufs=BANKS)
-            cols = slice((PACK * b + t) * P, (PACK * b + t + 1) * P)
-            passes = [
-                (w2_codes[:, 2 * cols.start : 2 * cols.stop].bitcast(FP4X4), w2_plane, v2_words, 1),
-                (w1_codes[:, cols].bitcast(FP8X4), w1_plane, v_words, 0),
-            ]
-            if u == 0 and t < W1_FIRST_GROUPS:
-                passes = passes[::-1]
-            for index, (codes, plane, words, table) in enumerate(passes):
-                nc.tensor.matmul_mx(
-                    bank[:], codes, plane[:, cols], words[c][:].bitcast(FP8X4),
-                    table_plane(table, c), start=(index == 0), stop=(index == 1),
-                )
+            if b == 0 and c == 0:
+                raise ValueError
+            words2 = v2_words[c] if c > 0 else None
+            if c > 0:
+                product_pair(bank[:], b, t, v_words[c], table_plane(0, c), words2, table_plane(1, c), False)
+            else:
+                for half in range(2):
+                    cols = slice(half * HALF, (half + 1) * HALF)
+                    product_pair(bank[:, cols], b, t, v_words[0][:, cols], table_plane(0, 0)[:, cols], v2_first[half], table_plane(1, 0)[:, cols], False)
             return bank
+
+        def open_first_unit():
+            tile = keep.tile([P, PACK, CHUNK], F32, name="squares0")
+            for t in range(PACK):
+                squares[0, t] = tile[:, t, :]
+            for half in range(2):
+                cols = slice(half * HALF, (half + 1) * HALF)
+                for pair in range(2):
+                    bank = psum.tile([P, 2, HALF], F32, name="bank", tag="bank", bufs=BANKS)
+                    for index in range(2):
+                        product_pair(bank[:, index, :], 0, 2 * pair + index, v_words[0][:, cols], table_plane(0, 0)[:, cols],
+                                     v2_first[half], table_plane(1, 0)[:, cols], half == 0 and pair == 0 and index == 0)
+                    nc.scalar.activation(tile[:, 2 * pair : 2 * pair + 2, cols], bank[:], ACT.Square)
+            return [0, 1, 2, 3]
 
         def square_tile():
             return ring.tile([P, CHUNK], F32, name="square", tag="square", bufs=len(UNITS) * PACK)[:]
@@ -334,7 +370,7 @@ def tile_list_flow_residual_refine_kernel(
             for part, cols in zip(words, halves_of_chunk):
                 quantize_h(part[:], u, cols)
 
-        waiting = open_unit(0)
+        waiting = open_first_unit()
         w3_raw = load_w3()
         prepare_w1_second_half()
         for u, t in SQUARES_BESIDE_CAST:
@@ -355,11 +391,14 @@ def tile_list_flow_residual_refine_kernel(
         words1 = after_w1.tile([P, CHUNK, PACK], BF16, name="words1", align_bytes=64, offset=64)
         interleave_on_gpsimd(words1[:], 1, whole)
         square30 = after_w1.tile([P, CHUNK], F32, name="square30", align_bytes=64, offset=4160)
-        square_on_vector(3, 0, square30[:])
+        bank30 = first_products(3, 0)
+        squares[3, 0] = square30[:]
+        nc.vector.tensor_reduce(square30[:, 0:HALF], bank30[:, 0:HALF].unsqueeze(2).to_broadcast([P, HALF, 2]), AXIS.X, ALU.mult)
         w3_cast = cast_w3(w3_raw)
         quantize_h(words1[:], 1, whole)
         quantize_w3(w3_cast)
         close_unit(2, waiting)
+        nc.scalar.activation(square30[:, HALF:CHUNK], bank30[:, HALF:CHUNK], ACT.Square)
         close_unit(3, open_unit(3))
 
         waiting = open_unit(4)

@@ -27,7 +27,7 @@ HALVES = H // PASS
 RUN = 4
 QUADS = 4
 FIRST_ROW = P - 4 * QUADS
-FIRST_ROW1 = 64 - 4 * QUADS
+FIRST_ROW2 = 64 - 4 * QUADS
 PLANE1_ROW = 4
 BANKS = 6
 
@@ -48,7 +48,6 @@ def tile_list_flow_residual_refine_kernel(
     with ExitStack() as ctx:
         keep = ctx.enter_context(tc.tile_pool(name="keep", bufs=1))
         ring = ctx.enter_context(tc.tile_pool(name="ring", bufs=2))
-        after_w1 = ctx.enter_context(tc.tile_pool(name="after_w1", bufs=1))
         after_w2 = ctx.enter_context(tc.tile_pool(name="after_w2", bufs=1))
         after_s1 = ctx.enter_context(tc.tile_pool(name="after_s1", bufs=1))
         after_unit3 = ctx.enter_context(tc.tile_pool(name="after_unit3", bufs=1))
@@ -61,14 +60,15 @@ def tile_list_flow_residual_refine_kernel(
         scale_win1 = after_s1.tile([P, T], U8, name="scale_win1", align_bytes=64, offset=16384)
         scale_win2 = after_w2.tile([P, T], U8, name="scale_win2", align_bytes=64, offset=8192)
         nc.sync.dma_start(list1[:], offs)
-        nc.sync.dma_start(scale_win1[FIRST_ROW1:64, :].bitcast(I32), tab_scales[0].bitcast(I32))
+        nc.sync.dma_start(scale_win1[FIRST_ROW:P, :].bitcast(I32), tab_scales[0].bitcast(I32))
         nc.sync.dma_start(list2[:], offs2)
-        nc.sync.dma_start(scale_win2[FIRST_ROW:P, :].bitcast(I32), tab2_scales[0].bitcast(I32))
-        nc.vector.memset(scale_win1[0:FIRST_ROW1, :].bitcast(I32), 0)
-        nc.vector.memset(scale_win1[64:P, :].bitcast(I32), 0)
-        nc.vector.memset(scale_win2[0:FIRST_ROW, :].bitcast(I32), 0)
+        nc.sync.dma_start(scale_win2[FIRST_ROW2:64, :].bitcast(I32), tab2_scales[0].bitcast(I32))
+        nc.vector.memset(scale_win1[0:FIRST_ROW, :].bitcast(I32), 0)
         plane1 = keep.tile([P, S], U8, name="plane1", align_bytes=64)
         plane2 = keep.tile([P, S], U8, name="plane2", align_bytes=64)
+        nc.gpsimd.memset(scale_win2[0:FIRST_ROW2, :].bitcast(I32), 0)
+        nc.gpsimd.memset(scale_win2[64:P, :].bitcast(I32), 0)
+        nc.gpsimd.memset(plane1[:].bitcast(I32), 0)
 
         warm_in = keep.tile([P, 1], F32, name="warm_in")
         warm_out = keep.tile([P, 1], F32, name="warm_out")
@@ -82,16 +82,15 @@ def tile_list_flow_residual_refine_kernel(
         nc.sync.dma_start(gain_rows[P - HALVES : P, :], gain.rearrange("(b r) -> b r", b=HALVES))
         nc.gpsimd.memset(gain_rows[0 : P - HALVES, :], 0.0)
         nc.sync.dma_start(w1_raw0[:], w1_rows[:, :, 0:PASS])
-        nc.sync.dma_start(word_win1[:], tab_words[0].rearrange("p t i -> p (t i)").bitcast(I32))
         for quad in range(QUADS):
             nc.sync.dma_start(
                 w2_scale_raw[32 * quad : 32 * quad + 4, :].bitcast(I32),
                 w2_scales[0, 4 * quad : 4 * quad + 4, :].bitcast(I32),
             )
+        nc.sync.dma_start(word_win1[:], tab_words[0].rearrange("p t i -> p (t i)").bitcast(I32))
 
         identity = keep.tile([P, P], F32, name="identity")
         make_identity(nc, identity[:])
-        nc.gpsimd.memset(plane1[:].bitcast(I32), 0)
         nc.gpsimd.memset(plane2[:].bitcast(I32), 0)
         gain_turned = psum.tile([P, CHUNK], F32, name="gain_turned", tag="bank", bufs=BANKS)
         gain_dealt = keep.tile([P, PASS], F32, name="gain_dealt")
@@ -132,11 +131,11 @@ def tile_list_flow_residual_refine_kernel(
             nc.sync.dma_start(raw[:], w2_words[0].bitcast(I32)[:, b * PASS // 2 : (b + 1) * PASS // 2])
             return raw
 
-        move_scale_rows(plane1, PLANE1_ROW, picked1, FIRST_ROW1)
+        move_scale_rows(plane1, PLANE1_ROW, picked1, FIRST_ROW)
         word_win2 = after_s1.tile([P, T], I32, name="word_win2", align_bytes=64, offset=64)
         nc.sync.dma_start(word_win2[:], tab2_words[0].rearrange("p t i -> p (t i)").bitcast(I32))
         w2_raw0 = load_w2(0, after_s1, 16448 + 512)
-        move_scale_rows(plane2, 0, picked2, FIRST_ROW)
+        move_scale_rows(plane2, 0, picked2, FIRST_ROW2)
         w1_raw1 = after_w2.tile([P, PACK, PASS], F32, name="w1_raw1", align_bytes=64, offset=64)
         nc.sync.dma_start(w1_raw1[:], w1_rows[:, :, PASS:H])
         w2_raw1 = load_w2(1, after_w2, 8192 + 64)
@@ -149,13 +148,13 @@ def tile_list_flow_residual_refine_kernel(
         w1_plane = keep.tile([P, H], U8, name="w1_plane", align_bytes=64)
 
         def w1_cast_tile(name):
-            return after_w1.tile([P, PACK, PASS], BF16, name=name, tag="w1_cast", align_bytes=64, offset=7168)
+            return after_s1.tile([P, PACK, PASS], BF16, name=name, tag="w1_cast", align_bytes=64, offset=7168)
 
         def quantize_w1(cast, b):
             cols = slice(b * PASS, (b + 1) * PASS)
             nc.vector.quantize_mx(w1_codes[:, cols].bitcast(FP8X4), w1_plane[:, cols], cast[:].rearrange("p t x -> p (t x)"))
 
-        w1_cast0 = w1_cast_tile("w1_cast0")
+        w1_cast0 = keep.tile([P, PACK, PASS], BF16, name="w1_cast0", align_bytes=64)
         for t in range(PACK):
             nc.scalar.activation(
                 w1_cast0[:, t, :].rearrange("p (u e i) -> p u i e", e=RUN, i=PACK),
@@ -196,14 +195,6 @@ def tile_list_flow_residual_refine_kernel(
         picked = after_s1.tile([P, CHUNKS - 1, CHUNK], U32, name="v2_later", align_bytes=64, offset=16448 + 1024)
         v2_words = [None] + [gather_words(picked[:, c - 1, :], word_win2, list2, c * CHUNK, CHUNK) for c in range(1, CHUNKS)]
 
-        warm_acc = psum.tile([P, CHUNK], F32, name="warm_acc", tag="out_acc0")
-        for index in range(WARM_PASSES):
-            cols = slice((index % PACK) * P, (index % PACK + 1) * P)
-            nc.tensor.matmul_mx(
-                warm_acc[:], w1_codes[:, cols].bitcast(FP8X4), w1_plane[:, cols],
-                v_words[0].bitcast(FP8X4), w1_plane[:, 0:CHUNK], start=True, stop=True,
-            )
-
         w3_codes = keep.tile([P, HALVES * N], U32, name="w3_codes", align_bytes=64)
         w3_plane = keep.tile([P, HALVES * N], U8, name="w3_plane", align_bytes=64)
         h_codes = [keep.tile([P, CHUNK], U32, name="h_codes%d" % u, align_bytes=64) for u in range(len(UNITS))]
@@ -231,7 +222,7 @@ def tile_list_flow_residual_refine_kernel(
             quantize_w1(cast, 1)
 
         def cast_w3(raw):
-            cast = after_w1.tile([P, HALVES, N * PACK], BF16, name="w3_cast", align_bytes=64, offset=6208)
+            cast = after_s1.tile([P, HALVES, N * PACK], BF16, name="w3_cast", align_bytes=64, offset=6208)
             signs = sign_turned[:].rearrange("p (t x) -> p t x", x=P)
             for b in range(HALVES):
                 column = P - HALVES + b
@@ -280,14 +271,23 @@ def tile_list_flow_residual_refine_kernel(
             tile = keep.tile([P, PACK, CHUNK], F32, name="squares0")
             for t in range(PACK):
                 squares[0, t] = tile[:, t, :]
-            for half in range(2):
-                cols = slice(half * HALF, (half + 1) * HALF)
-                for pair in range(2):
-                    bank = psum.tile([P, 2, HALF], F32, name="bank", tag="bank", bufs=BANKS)
-                    for index in range(2):
-                        product_pair(bank[:, index, :], 0, 2 * pair + index, v_words[0][:, cols], table_plane(0, 0)[:, cols],
-                                     v2_first[half], table_plane(1, 0)[:, cols], half == 0 and pair == 0 and index == 0)
-                    nc.scalar.activation(tile[:, 2 * pair : 2 * pair + 2, cols], bank[:], ACT.Square)
+            banks = [psum.tile([P, 2, HALF], F32, name="bank", tag="bank", bufs=BANKS) for index in range(PACK)]
+            for table in range(2):
+                for half in range(2):
+                    cols = slice(half * HALF, (half + 1) * HALF)
+                    for t in range(PACK):
+                        w_cols = slice(t * P, (t + 1) * P)
+                        acc = banks[2 * half + t // 2][:, t % 2, :]
+                        if table == 0:
+                            nc.tensor.matmul_mx(acc, w1_codes[:, w_cols].bitcast(FP8X4), w1_plane[:, w_cols],
+                                                v_words[0][:, cols].bitcast(FP8X4), table_plane(0, 0)[:, cols],
+                                                start=(t % 2 == 0), stop=False)
+                        else:
+                            nc.tensor.matmul_mx(acc, w2_codes[0][:, 2 * t * P : 2 * (t + 1) * P].bitcast(FP4X4), w2_plane[:, w_cols],
+                                                v2_first[half].bitcast(FP8X4), table_plane(1, 0)[:, cols],
+                                                start=False, stop=(t % 2 == 1))
+                            if t % 2 == 1:
+                                nc.scalar.activation(tile[:, t - 1 : t + 1, cols], banks[2 * half + t // 2][:], ACT.Square)
             return [0, 1, 2, 3]
 
         def square_tile():
@@ -379,18 +379,18 @@ def tile_list_flow_residual_refine_kernel(
         close_unit(0, waiting)
 
         waiting = open_unit(1)
-        words0 = after_w1.tile([P, CHUNK, PACK], BF16, name="words0", align_bytes=64, offset=4096)
+        words0 = after_s1.tile([P, CHUNK, PACK], BF16, name="words0", align_bytes=64, offset=4096)
         interleave_on_gpsimd(words0[:], 0, whole)
-        held = after_w1.tile([P, len(SQUARES_BESIDE_INTERLEAVE), CHUNK], F32, name="held", align_bytes=64, offset=10304)
+        held = after_s1.tile([P, len(SQUARES_BESIDE_INTERLEAVE), CHUNK], F32, name="held", align_bytes=64, offset=10304)
         for index, (u, t) in enumerate(SQUARES_BESIDE_INTERLEAVE):
             square_on_vector(u, t, held[:, index, :])
         quantize_h(words0[:], 0, whole)
         close_unit(1, waiting)
 
         waiting = open_unit(2)
-        words1 = after_w1.tile([P, CHUNK, PACK], BF16, name="words1", align_bytes=64, offset=64)
+        words1 = after_s1.tile([P, CHUNK, PACK], BF16, name="words1", align_bytes=64, offset=64)
         interleave_on_gpsimd(words1[:], 1, whole)
-        square30 = after_w1.tile([P, CHUNK], F32, name="square30", align_bytes=64, offset=4160)
+        square30 = after_s1.tile([P, CHUNK], F32, name="square30", align_bytes=64, offset=4160)
         bank30 = first_products(3, 0)
         squares[3, 0] = square30[:]
         nc.vector.tensor_reduce(square30[:, 0:HALF], bank30[:, 0:HALF].unsqueeze(2).to_broadcast([P, HALF, 2]), AXIS.X, ALU.mult)

@@ -58,7 +58,7 @@ def tile_list_flow_residual_refine_kernel(
         list1 = keep.tile([P, S // 16], U16, name="list1")
         list2 = keep.tile([P, S // 16], U16, name="list2")
         scale_win1 = after_s1.tile([P, T], U8, name="scale_win1", align_bytes=64, offset=16384)
-        scale_win2 = after_w2.tile([P, T], U8, name="scale_win2", align_bytes=64, offset=8192)
+        scale_win2 = after_w2.tile([P, T], U8, name="scale_win2", align_bytes=64, offset=16320)
         nc.sync.dma_start(list1[:], offs)
         nc.sync.dma_start(scale_win1[FIRST_ROW:P, :].bitcast(I32), tab_scales[0].bitcast(I32))
         nc.sync.dma_start(list2[:], offs2)
@@ -136,15 +136,15 @@ def tile_list_flow_residual_refine_kernel(
         nc.sync.dma_start(word_win2[:], tab2_words[0].rearrange("p t i -> p (t i)").bitcast(I32))
         w2_raw0 = load_w2(0, after_s1, 16448 + 512)
         move_scale_rows(plane2, 0, picked2, FIRST_ROW2)
-        w1_raw1 = after_w2.tile([P, PACK, PASS], F32, name="w1_raw1", align_bytes=64, offset=64)
+        w1_raw1 = after_w2.tile([P, PACK, PASS], F32, name="w1_raw1", align_bytes=64, offset=8192)
         nc.sync.dma_start(w1_raw1[:], w1_rows[:, :, PASS:H])
-        w2_raw1 = load_w2(1, after_w2, 8192 + 64)
+        w2_raw1 = load_w2(1, after_w2, 16384)
 
         def table_plane(table, c):
             cols = slice(c * CHUNK, (c + 1) * CHUNK)
             return plane2[:, cols] if table == 1 else plane1[PLANE1_ROW:P, cols]
 
-        w1_codes = keep.tile([P, H], U32, name="w1_codes", align_bytes=64)
+        w1_codes = [keep.tile([P, PASS], U32, name="w1_codes0", align_bytes=64)]
         w1_plane = keep.tile([P, H], U8, name="w1_plane", align_bytes=64)
 
         def w1_cast_tile(name):
@@ -152,7 +152,7 @@ def tile_list_flow_residual_refine_kernel(
 
         def quantize_w1(cast, b):
             cols = slice(b * PASS, (b + 1) * PASS)
-            nc.vector.quantize_mx(w1_codes[:, cols].bitcast(FP8X4), w1_plane[:, cols], cast[:].rearrange("p t x -> p (t x)"))
+            nc.vector.quantize_mx(w1_codes[b][:].bitcast(FP8X4), w1_plane[:, cols], cast[:].rearrange("p t x -> p (t x)"))
 
         w1_cast0 = keep.tile([P, PACK, PASS], BF16, name="w1_cast0", align_bytes=64)
         for t in range(PACK):
@@ -201,6 +201,7 @@ def tile_list_flow_residual_refine_kernel(
         h_plane = [keep.tile([P, CHUNK], U8, name="h_plane%d" % u, align_bytes=64) for u in range(len(UNITS))]
         roots = [keep.tile([P, PACK, CHUNK], BF16, name="roots%d" % u, align_bytes=64) for u in range(len(UNITS))]
         squares = {}
+        squares0 = after_w2.tile([P, PACK, CHUNK], F32, name="squares0", align_bytes=64, offset=0)
 
         def load_w3():
             raw = keep.tile([P, HALVES, PACK, N], F32, name="w3_raw", tag="words_then_w3")
@@ -217,9 +218,9 @@ def tile_list_flow_residual_refine_kernel(
                 w1_raw1[:].rearrange("p i (u t e) -> p u t e i", t=PACK, e=RUN),
                 -1.0, 0.0, ALU.mult, ALU.add,
             )
-            w2_codes.append(after_w2.tile([P, 2 * PASS], U8, name="w2_codes1", align_bytes=64, offset=64))
-            deal_w2(1, w2_raw1)
-            quantize_w1(cast, 1)
+            w2_codes.append(after_w2.tile([P, 2 * PASS], U8, name="w2_codes1", align_bytes=64, offset=7680))
+            w1_codes.append(after_w2.tile([P, PASS], U32, name="w1_codes1", align_bytes=64, offset=0))
+            return cast
 
         def cast_w3(raw):
             cast = after_s1.tile([P, HALVES, N * PACK], BF16, name="w3_cast", align_bytes=64, offset=6208)
@@ -244,7 +245,7 @@ def tile_list_flow_residual_refine_kernel(
             cols = slice((PACK * b + t) * P, (PACK * b + t + 1) * P)
             passes = [
                 (w2_codes[b][:, 2 * t * P : 2 * (t + 1) * P].bitcast(FP4X4), w2_plane, words2, plane2),
-                (w1_codes[:, cols].bitcast(FP8X4), w1_plane, words1, plane1),
+                (w1_codes[b][:, t * P : (t + 1) * P].bitcast(FP8X4), w1_plane, words1, plane1),
             ]
             if w1_first:
                 passes = passes[::-1]
@@ -268,7 +269,7 @@ def tile_list_flow_residual_refine_kernel(
             return bank
 
         def open_first_unit():
-            tile = keep.tile([P, PACK, CHUNK], F32, name="squares0")
+            tile = squares0
             for t in range(PACK):
                 squares[0, t] = tile[:, t, :]
             banks = [psum.tile([P, 2, HALF], F32, name="bank", tag="bank", bufs=BANKS) for index in range(PACK)]
@@ -279,7 +280,7 @@ def tile_list_flow_residual_refine_kernel(
                         w_cols = slice(t * P, (t + 1) * P)
                         acc = banks[2 * half + t // 2][:, t % 2, :]
                         if table == 0:
-                            nc.tensor.matmul_mx(acc, w1_codes[:, w_cols].bitcast(FP8X4), w1_plane[:, w_cols],
+                            nc.tensor.matmul_mx(acc, w1_codes[0][:, w_cols].bitcast(FP8X4), w1_plane[:, w_cols],
                                                 v_words[0][:, cols].bitcast(FP8X4), table_plane(0, 0)[:, cols],
                                                 start=(t % 2 == 0), stop=False)
                         else:
@@ -372,11 +373,13 @@ def tile_list_flow_residual_refine_kernel(
 
         waiting = open_first_unit()
         w3_raw = load_w3()
-        prepare_w1_second_half()
+        w1_cast1 = prepare_w1_second_half()
         for u, t in SQUARES_BESIDE_CAST:
             if u == 1:
                 square_on_vector(u, t, square_tile())
         close_unit(0, waiting)
+        deal_w2(1, w2_raw1)
+        quantize_w1(w1_cast1, 1)
 
         waiting = open_unit(1)
         words0 = after_s1.tile([P, CHUNK, PACK], BF16, name="words0", align_bytes=64, offset=4096)

@@ -22,23 +22,19 @@ P = 128
 PACK = 4
 PASS = P * PACK
 CHUNK = 512
+HALF = CHUNK // 2
 CHUNKS = S // CHUNK
 HALVES = H // PASS
 RUN = 4
 QUADS = 4
-FIRST_ROW = P - 4 * QUADS
-FIRST_ROW2 = 64 - 4 * QUADS
+ROWS1 = P - 4 * QUADS
+ROWS2 = P // 2 - 4 * QUADS
 PLANE1_ROW = 4
 BANKS = 6
-
-UNITS = [(c, b) for b in range(HALVES) for c in range(CHUNKS)]
+UNITS = [(0, 0), (1, 0), (0, 1), (1, 1), (2, 0), (2, 1)]
 LAST = len(UNITS) - 1
-SQUARES_BESIDE_CAST = [(1, 0), (1, 1), (1, 2)]
-SQUARES_BESIDE_INTERLEAVE = [(2, 0), (2, 1), (2, 2)]
-GPSIMD_COLUMNS = 384
-W1_FIRST_GROUPS = 2
-WARM_PASSES = 5
 LAST_PIECES = [slice(0, 256), slice(256, 384), slice(384, 512)]
+WHOLE = slice(0, CHUNK)
 
 
 def tile_list_flow_residual_refine_kernel(
@@ -48,26 +44,37 @@ def tile_list_flow_residual_refine_kernel(
     with ExitStack() as ctx:
         keep = ctx.enter_context(tc.tile_pool(name="keep", bufs=1))
         ring = ctx.enter_context(tc.tile_pool(name="ring", bufs=2))
-        after_w2 = ctx.enter_context(tc.tile_pool(name="after_w2", bufs=1))
-        after_s1 = ctx.enter_context(tc.tile_pool(name="after_s1", bufs=1))
-        after_unit3 = ctx.enter_context(tc.tile_pool(name="after_unit3", bufs=1))
         psum = ctx.enter_context(tc.psum_pool(name="psum", bufs=1))
 
-        w2_scale_raw = keep.tile([P, H], U8, name="w2_scale_raw")
+        def placed_pool(name):
+            pool = ctx.enter_context(tc.tile_pool(name=name, bufs=1))
+            return lambda shape, dtype, tile_name, offset: pool.tile(shape, dtype, name=tile_name, align_bytes=64, offset=offset)
+
+        after_scales1 = placed_pool("after_scales1")
+        after_scales2 = placed_pool("after_scales2")
+        after_squares0 = placed_pool("after_squares0")
+        after_roots0 = placed_pool("after_roots0")
+        after_roots1 = placed_pool("after_roots1")
+        after_roots3 = placed_pool("after_roots3")
+
+        def kept(shape, dtype, name):
+            return keep.tile(shape, dtype, name=name, align_bytes=64)
+
+        w2_scale_raw = kept([P, H], U8, "w2_scale_raw")
         nc.gpsimd.memset(w2_scale_raw[:].bitcast(I32), 0)
         list1 = keep.tile([P, S // 16], U16, name="list1")
         list2 = keep.tile([P, S // 16], U16, name="list2")
-        scale_win1 = after_s1.tile([P, T], U8, name="scale_win1", align_bytes=64, offset=16384)
-        scale_win2 = after_w2.tile([P, T], U8, name="scale_win2", align_bytes=64, offset=16320)
+        scale_win1 = after_scales1([P, T], U8, "scale_win1", 16384)
+        scale_win2 = after_scales2([P, T], U8, "scale_win2", 8192)
         nc.sync.dma_start(list1[:], offs)
-        nc.sync.dma_start(scale_win1[FIRST_ROW:P, :].bitcast(I32), tab_scales[0].bitcast(I32))
+        nc.sync.dma_start(scale_win1[ROWS1:P, :].bitcast(I32), tab_scales[0].bitcast(I32))
         nc.sync.dma_start(list2[:], offs2)
-        nc.sync.dma_start(scale_win2[FIRST_ROW2:64, :].bitcast(I32), tab2_scales[0].bitcast(I32))
-        nc.vector.memset(scale_win1[0:FIRST_ROW, :].bitcast(I32), 0)
-        plane1 = keep.tile([P, S], U8, name="plane1", align_bytes=64)
-        plane2 = keep.tile([P, S], U8, name="plane2", align_bytes=64)
-        nc.gpsimd.memset(scale_win2[0:FIRST_ROW2, :].bitcast(I32), 0)
-        nc.gpsimd.memset(scale_win2[64:P, :].bitcast(I32), 0)
+        nc.sync.dma_start(scale_win2[ROWS2 : P // 2, :].bitcast(I32), tab2_scales[0].bitcast(I32))
+        nc.vector.memset(scale_win1[0:ROWS1, :].bitcast(I32), 0)
+        nc.vector.memset(scale_win2[0:ROWS2, :].bitcast(I32), 0)
+        nc.gpsimd.memset(scale_win2[P // 2 : P, :].bitcast(I32), 0)
+        plane1 = kept([P, S], U8, "plane1")
+        plane2 = kept([P, S], U8, "plane2")
         nc.gpsimd.memset(plane1[:].bitcast(I32), 0)
 
         warm_in = keep.tile([P, 1], F32, name="warm_in")
@@ -75,48 +82,51 @@ def tile_list_flow_residual_refine_kernel(
         nc.vector.memset(warm_in[:], 1.0)
         nc.scalar.activation(warm_out[:], warm_in[:], ACT.Sqrt)
 
-        word_win1 = keep.tile([P, T], I32, name="word_win1", tag="words_then_w3")
         w1_rows = w1.rearrange("(p i) r -> p i r", i=PACK)
-        w1_raw0 = keep.tile([P, PACK, PASS], F32, name="w1_raw0")
-        gain_rows = keep.tile([P, PASS], F32, name="gain_rows")
+        w2_rows = w2_words[0].bitcast(I32)
+        gain_rows = kept([P, PASS], F32, "gain_rows")
         nc.sync.dma_start(gain_rows[P - HALVES : P, :], gain.rearrange("(b r) -> b r", b=HALVES))
         nc.gpsimd.memset(gain_rows[0 : P - HALVES, :], 0.0)
+        w1_raw0 = kept([P, PACK, PASS], F32, "w1_raw0")
         nc.sync.dma_start(w1_raw0[:], w1_rows[:, :, 0:PASS])
         for quad in range(QUADS):
             nc.sync.dma_start(
                 w2_scale_raw[32 * quad : 32 * quad + 4, :].bitcast(I32),
                 w2_scales[0, 4 * quad : 4 * quad + 4, :].bitcast(I32),
             )
+        word_win1 = keep.tile([P, T], I32, name="word_win1", tag="words_then_w3")
         nc.sync.dma_start(word_win1[:], tab_words[0].rearrange("p t i -> p (t i)").bitcast(I32))
+        w2_raw0 = kept([P, PASS // 2], I32, "w2_raw0")
+        nc.sync.dma_start(w2_raw0[:], w2_rows[:, 0 : PASS // 2])
 
-        identity = keep.tile([P, P], F32, name="identity")
+        identity = kept([P, P], F32, "identity")
         make_identity(nc, identity[:])
         nc.gpsimd.memset(plane2[:].bitcast(I32), 0)
-        gain_turned = psum.tile([P, CHUNK], F32, name="gain_turned", tag="bank", bufs=BANKS)
-        gain_dealt = keep.tile([P, PASS], F32, name="gain_dealt")
+
+        def turn(rows, name, tag, bufs):
+            turned = psum.tile([P, PACK, P], F32, name=name, tag=tag, bufs=bufs)
+            for t in range(PACK):
+                nc.tensor.transpose(turned[:, t, :], rows[:, t * P : (t + 1) * P], identity[:])
+            return turned
+
+        gain_dealt = kept([P, PASS], F32, "gain_dealt")
         nc.scalar.copy(
             gain_dealt[:].rearrange("p (t u e) -> p t u e", t=PACK, e=RUN),
             gain_rows[:].rearrange("p (u t e) -> p t u e", t=PACK, e=RUN),
         )
-        for t in range(PACK):
-            nc.tensor.transpose(gain_turned[:, t * P : (t + 1) * P], gain_dealt[:, t * P : (t + 1) * P], identity[:])
-        gain_cols = keep.tile([P, HALVES * PACK], F32, name="gain_cols")
-        gain_sq = keep.tile([P, HALVES * PACK], F32, name="gain_sq")
-        nc.scalar.copy(
-            gain_cols[:].rearrange("p (b t) -> p b t", t=PACK),
-            gain_turned[:].rearrange("p (t x) -> p x t", x=P)[:, P - HALVES : P, :],
-        )
+        gain_turned = turn(gain_dealt, "gain_turned", "bank", BANKS)
+        gain_cols = kept([P, HALVES, PACK], F32, "gain_cols")
+        gain_sq = kept([P, HALVES, PACK], F32, "gain_sq")
+        nc.scalar.copy(gain_cols[:], gain_turned[:].rearrange("p t x -> p x t")[:, P - HALVES : P, :])
         nc.gpsimd.tensor_tensor(gain_sq[:], gain_cols[:], gain_cols[:], ALU.mult)
-        sign_raw = keep.tile([P, PASS], F32, name="sign_raw")
-        sign_dealt = keep.tile([P, PASS], F32, name="sign_dealt")
+        sign_raw = kept([P, PASS], F32, "sign_raw")
+        sign_dealt = kept([P, PASS], F32, "sign_dealt")
         nc.scalar.activation(sign_raw[:], gain_dealt[:], ACT.Sign)
         nc.scalar.activation(sign_dealt[:], sign_raw[:], ACT.Sign, bias=0.5)
-        sign_turned = psum.tile([P, CHUNK], F32, name="sign_turned", tag="out_acc1")
-        for t in range(PACK):
-            nc.tensor.transpose(sign_turned[:, t * P : (t + 1) * P], sign_dealt[:, t * P : (t + 1) * P], identity[:])
+        sign_turned = turn(sign_dealt, "sign_turned", "out_acc1", 1)
 
-        picked1 = keep.tile([P, S], U8, name="picked1", align_bytes=64)
-        picked2 = keep.tile([P, S], U8, name="picked2", align_bytes=64)
+        picked1 = kept([P, S], U8, "picked1")
+        picked2 = kept([P, S], U8, "picked2")
         nc.vector.tensor_copy(picked1[:], scale_win1[:].indirect(list1[:]))
         nc.vector.tensor_copy(picked2[:], scale_win2[:].indirect(list2[:]))
 
@@ -126,45 +136,22 @@ def tile_list_flow_residual_refine_kernel(
                 to = 32 * quad + plane_row
                 nc.sync.dma_start(plane[to : to + 4, :].bitcast(I32), picked[row : row + 4, :].bitcast(I32))
 
-        def load_w2(b, pool, offset):
-            raw = pool.tile([P, PASS // 2], I32, name="w2_raw%d" % b, align_bytes=64, offset=offset)
-            nc.sync.dma_start(raw[:], w2_words[0].bitcast(I32)[:, b * PASS // 2 : (b + 1) * PASS // 2])
-            return raw
-
-        move_scale_rows(plane1, PLANE1_ROW, picked1, FIRST_ROW)
-        word_win2 = after_s1.tile([P, T], I32, name="word_win2", align_bytes=64, offset=64)
+        move_scale_rows(plane1, PLANE1_ROW, picked1, ROWS1)
+        word_win2 = after_scales1([P, T], I32, "word_win2", 64)
         nc.sync.dma_start(word_win2[:], tab2_words[0].rearrange("p t i -> p (t i)").bitcast(I32))
-        w2_raw0 = load_w2(0, after_s1, 16448 + 512)
-        move_scale_rows(plane2, 0, picked2, FIRST_ROW2)
-        w1_raw1 = after_w2.tile([P, PACK, PASS], F32, name="w1_raw1", align_bytes=64, offset=8192)
+        move_scale_rows(plane2, 0, picked2, ROWS2)
+        w1_raw1 = after_scales2([P, PACK, PASS], F32, "w1_raw1", 64)
         nc.sync.dma_start(w1_raw1[:], w1_rows[:, :, PASS:H])
-        w2_raw1 = load_w2(1, after_w2, 16384)
+        w2_raw1 = after_scales2([P, PASS // 2], I32, "w2_raw1", 8256)
+        nc.sync.dma_start(w2_raw1[:], w2_rows[:, PASS // 2 : PASS])
 
-        def table_plane(table, c):
-            cols = slice(c * CHUNK, (c + 1) * CHUNK)
-            return plane2[:, cols] if table == 1 else plane1[PLANE1_ROW:P, cols]
+        w1_codes = [kept([P, PASS], U32, "w1_codes0")]
+        w1_plane = kept([P, H], U8, "w1_plane")
+        w2_codes = [kept([P, 2 * PASS], U8, "w2_codes0")]
+        w2_plane = kept([P, H], U8, "w2_plane")
 
-        w1_codes = [keep.tile([P, PASS], U32, name="w1_codes0", align_bytes=64)]
-        w1_plane = keep.tile([P, H], U8, name="w1_plane", align_bytes=64)
-
-        def w1_cast_tile(name):
-            return after_s1.tile([P, PACK, PASS], BF16, name=name, tag="w1_cast", align_bytes=64, offset=7168)
-
-        def quantize_w1(cast, b):
-            cols = slice(b * PASS, (b + 1) * PASS)
-            nc.vector.quantize_mx(w1_codes[b][:].bitcast(FP8X4), w1_plane[:, cols], cast[:].rearrange("p t x -> p (t x)"))
-
-        w1_cast0 = keep.tile([P, PACK, PASS], BF16, name="w1_cast0", align_bytes=64)
-        for t in range(PACK):
-            nc.scalar.activation(
-                w1_cast0[:, t, :].rearrange("p (u e i) -> p u i e", e=RUN, i=PACK),
-                w1_raw0[:].rearrange("p i (u t e) -> p t u i e", t=PACK, e=RUN)[:, t],
-                ACT.Copy,
-                scale=-1.0,
-            )
-        quantize_w1(w1_cast0, 0)
-
-        w2_codes = [keep.tile([P, 2 * PASS], U8, name="w2_codes0", align_bytes=64)]
+        def quantize(codes, plane, values):
+            nc.vector.quantize_mx(codes.bitcast(FP8X4), plane, values.rearrange("p a x -> p (a x)"))
 
         def deal_w2(b, raw):
             nc.vector.tensor_copy(
@@ -172,155 +159,109 @@ def tile_list_flow_residual_refine_kernel(
                 raw[:].rearrange("p (u t w) -> p t u w", t=PACK, w=2),
             )
 
-        w2_plane = keep.tile([P, H], U8, name="w2_plane", align_bytes=64)
+        w1_cast0 = kept([P, PACK, PASS], BF16, "w1_cast0")
+        for t in range(PACK):
+            nc.scalar.activation(
+                w1_cast0[:, t, :].rearrange("p (u e i) -> p u i e", e=RUN, i=PACK),
+                w1_raw0[:].rearrange("p i (u t e) -> p t u i e", t=PACK, e=RUN)[:, t],
+                ACT.Copy,
+                scale=-1.0,
+            )
+        quantize(w1_codes[0][:], w1_plane[:, 0:PASS], w1_cast0[:])
         nc.vector.tensor_copy(
             w2_plane[:].bitcast(I32).rearrange("p (b t u) -> p b t u", b=HALVES, t=PACK),
             w2_scale_raw[:].bitcast(I32).rearrange("p (b u t) -> p b t u", b=HALVES, t=PACK),
         )
+        deal_w2(0, w2_raw0)
 
         def gather_words(picked, window, offsets, first, count):
             entries = offsets[:, first // 16 : (first + count) // 16]
-            nc.vector.tensor_copy(picked, window[:].bitcast(U32).indirect(entries))
+            nc.vector.tensor_copy(picked[:], window[:].bitcast(U32).indirect(entries))
             return picked
 
-        v_words = [
-            gather_words(keep.tile([P, CHUNK], U32, name="v_words%d" % c, align_bytes=64)[:], word_win1, list1, c * CHUNK, CHUNK)
-            for c in range(CHUNKS)
-        ]
-        HALF = CHUNK // 2
-        v2_first = [gather_words(keep.tile([P, HALF], U32, name="v2_first0", align_bytes=64)[:], word_win2, list2, 0, HALF)]
-        deal_w2(0, w2_raw0)
-        picked = after_s1.tile([P, HALF], U32, name="v2_first1", align_bytes=64, offset=16448)
-        v2_first.append(gather_words(picked[:], word_win2, list2, HALF, HALF))
-        picked = after_s1.tile([P, CHUNKS - 1, CHUNK], U32, name="v2_later", align_bytes=64, offset=16448 + 1024)
-        v2_words = [None] + [gather_words(picked[:, c - 1, :], word_win2, list2, c * CHUNK, CHUNK) for c in range(1, CHUNKS)]
+        words1 = [gather_words(kept([P, CHUNK], U32, "words1_%d" % c), word_win1, list1, c * CHUNK, CHUNK) for c in range(CHUNKS)]
+        first2 = [gather_words(kept([P, HALF], U32, "first2_%d" % half), word_win2, list2, half * HALF, HALF) for half in range(2)]
+        words2 = {c: gather_words(kept([P, CHUNK], U32, "words2_%d" % c), word_win2, list2, c * CHUNK, CHUNK) for c in range(1, CHUNKS)}
 
-        w3_codes = keep.tile([P, HALVES * N], U32, name="w3_codes", align_bytes=64)
-        w3_plane = keep.tile([P, HALVES * N], U8, name="w3_plane", align_bytes=64)
-        h_codes = [keep.tile([P, CHUNK], U32, name="h_codes%d" % u, align_bytes=64) for u in range(len(UNITS))]
-        h_plane = [keep.tile([P, CHUNK], U8, name="h_plane%d" % u, align_bytes=64) for u in range(len(UNITS))]
-        roots = [keep.tile([P, PACK, CHUNK], BF16, name="roots%d" % u, align_bytes=64) for u in range(len(UNITS))]
-        squares = {}
-        squares0 = after_w2.tile([P, PACK, CHUNK], F32, name="squares0", align_bytes=64, offset=0)
-
-        def load_w3():
-            raw = keep.tile([P, HALVES, PACK, N], F32, name="w3_raw", tag="words_then_w3")
-            rows = w3.rearrange("(b u t e) n -> b t u e n", b=HALVES, t=PACK, e=RUN)
-            for b in range(HALVES):
-                for t in range(PACK):
-                    nc.sync.dma_start(raw[:, b, t, :], rows[b, t])
-            return raw
-
-        def prepare_w1_second_half():
-            cast = w1_cast_tile("w1_cast1")
-            nc.gpsimd.tensor_scalar(
-                cast[:].rearrange("p t (u e i) -> p u t e i", e=RUN, i=PACK),
-                w1_raw1[:].rearrange("p i (u t e) -> p u t e i", t=PACK, e=RUN),
-                -1.0, 0.0, ALU.mult, ALU.add,
+        def pass1(acc, c, b, t, cols, start, stop):
+            entries = slice(c * CHUNK + cols.start, c * CHUNK + cols.stop)
+            nc.tensor.matmul_mx(
+                acc, w1_codes[b][:, t * P : (t + 1) * P].bitcast(FP8X4), w1_plane[:, b * PASS + t * P : b * PASS + (t + 1) * P],
+                words1[c][:, cols].bitcast(FP8X4), plane1[PLANE1_ROW:P, entries], start=start, stop=stop,
             )
-            w2_codes.append(after_w2.tile([P, 2 * PASS], U8, name="w2_codes1", align_bytes=64, offset=7680))
-            w1_codes.append(after_w2.tile([P, PASS], U32, name="w1_codes1", align_bytes=64, offset=0))
-            return cast
 
-        def cast_w3(raw):
-            cast = after_s1.tile([P, HALVES, N * PACK], BF16, name="w3_cast", align_bytes=64, offset=6208)
-            signs = sign_turned[:].rearrange("p (t x) -> p t x", x=P)
-            for b in range(HALVES):
-                column = P - HALVES + b
-                sign = signs[:, :, column : column + 1].unsqueeze(1).to_broadcast([P, N // 4, PACK, 4])
-                nc.vector.tensor_tensor(
-                    cast[:, b, :].rearrange("p (c i t) -> p c t i", i=4, t=PACK),
-                    raw[:, b].rearrange("p t (c i) -> p c t i", i=4),
-                    sign,
-                    ALU.mult,
-                )
-            return cast
+        def pass2(acc, c, b, t, cols, start, stop):
+            entries = slice(c * CHUNK + cols.start, c * CHUNK + cols.stop)
+            words = first2[cols.start // HALF] if c == 0 else words2[c]
+            nc.tensor.matmul_mx(
+                acc, w2_codes[b][:, 2 * t * P : 2 * (t + 1) * P].bitcast(FP4X4), w2_plane[:, b * PASS + t * P : b * PASS + (t + 1) * P],
+                words[:].bitcast(FP8X4), plane2[:, entries], start=start, stop=stop,
+            )
 
-        def quantize_w3(cast):
-            for b in range(HALVES):
-                cols = slice(b * N, (b + 1) * N)
-                nc.vector.quantize_mx(w3_codes[:, cols].bitcast(FP8X4), w3_plane[:, cols], cast[:, b, :])
+        halves = [slice(0, HALF), slice(HALF, CHUNK)]
 
-        def product_pair(acc, b, t, words1, plane1, words2, plane2, w1_first):
-            cols = slice((PACK * b + t) * P, (PACK * b + t + 1) * P)
-            passes = [
-                (w2_codes[b][:, 2 * t * P : 2 * (t + 1) * P].bitcast(FP4X4), w2_plane, words2, plane2),
-                (w1_codes[b][:, t * P : (t + 1) * P].bitcast(FP8X4), w1_plane, words1, plane1),
-            ]
-            if w1_first:
-                passes = passes[::-1]
-            for index, (codes, plane, words, moving_plane) in enumerate(passes):
-                nc.tensor.matmul_mx(
-                    acc, codes, plane[:, cols], words.bitcast(FP8X4), moving_plane, start=(index == 0), stop=(index == 1)
-                )
-
-        def first_products(u, t):
+        def products(u, t):
             c, b = UNITS[u]
             bank = psum.tile([P, CHUNK], F32, name="bank", tag="bank", bufs=BANKS)
-            if b == 0 and c == 0:
-                raise ValueError
-            words2 = v2_words[c] if c > 0 else None
-            if c > 0:
-                product_pair(bank[:], b, t, v_words[c], table_plane(0, c), words2, table_plane(1, c), False)
+            if c == 0:
+                pass1(bank[:], c, b, t, WHOLE, True, False)
+                for cols in halves:
+                    pass2(bank[:, cols], c, b, t, cols, False, cols.stop == CHUNK)
             else:
-                for half in range(2):
-                    cols = slice(half * HALF, (half + 1) * HALF)
-                    product_pair(bank[:, cols], b, t, v_words[0][:, cols], table_plane(0, 0)[:, cols], v2_first[half], table_plane(1, 0)[:, cols], False)
+                pass2(bank[:], c, b, t, WHOLE, True, False)
+                pass1(bank[:], c, b, t, WHOLE, False, True)
             return bank
 
-        def open_first_unit():
-            tile = squares0
-            for t in range(PACK):
-                squares[0, t] = tile[:, t, :]
-            banks = [psum.tile([P, 2, HALF], F32, name="bank", tag="bank", bufs=BANKS) for index in range(PACK)]
-            for table in range(2):
-                for half in range(2):
-                    cols = slice(half * HALF, (half + 1) * HALF)
-                    for t in range(PACK):
-                        w_cols = slice(t * P, (t + 1) * P)
-                        acc = banks[2 * half + t // 2][:, t % 2, :]
-                        if table == 0:
-                            nc.tensor.matmul_mx(acc, w1_codes[0][:, w_cols].bitcast(FP8X4), w1_plane[:, w_cols],
-                                                v_words[0][:, cols].bitcast(FP8X4), table_plane(0, 0)[:, cols],
-                                                start=(t % 2 == 0), stop=False)
-                        else:
-                            nc.tensor.matmul_mx(acc, w2_codes[0][:, 2 * t * P : 2 * (t + 1) * P].bitcast(FP4X4), w2_plane[:, w_cols],
-                                                v2_first[half].bitcast(FP8X4), table_plane(1, 0)[:, cols],
-                                                start=False, stop=(t % 2 == 1))
-                            if t % 2 == 1:
-                                nc.scalar.activation(tile[:, t - 1 : t + 1, cols], banks[2 * half + t // 2][:], ACT.Square)
-            return [0, 1, 2, 3]
+        squares = {}
+        roots = {}
 
         def square_tile():
-            return ring.tile([P, CHUNK], F32, name="square", tag="square", bufs=len(UNITS) * PACK)[:]
+            return ring.tile([P, CHUNK], F32, name="square", tag="square", bufs=16)[:]
 
-        def square_on_scalar(u, t):
-            bank = first_products(u, t)
+        def square_by_scalar(u, t):
+            bank = products(u, t)
             squares[u, t] = square_tile()
             nc.scalar.activation(squares[u, t], bank[:], ACT.Square)
 
-        def square_on_vector(u, t, square):
-            bank = first_products(u, t)
+        def square_by_vector(u, t, square, cols=WHOLE):
+            bank = products(u, t)
             squares[u, t] = square
-            nc.vector.tensor_reduce(square, bank[:].unsqueeze(2).to_broadcast([P, CHUNK, 2]), AXIS.X, ALU.mult)
+            width = cols.stop - cols.start
+            nc.vector.tensor_reduce(square[:, cols], bank[:, cols].unsqueeze(2).to_broadcast([P, width, 2]), AXIS.X, ALU.mult)
+            return bank
 
-        def root(u, t, cols):
-            column = PACK * UNITS[u][1] + t
-            g2 = gain_sq[:, column : column + 1]
+        def root(u, t, cols=WHOLE):
+            g2 = gain_sq[:, UNITS[u][1], t : t + 1]
             nc.scalar.activation(roots[u][:, t, cols], squares[u, t][:, cols], ACT.Sqrt, bias=g2, scale=g2)
 
-        def interleave_on_vector(words, u, cols):
+        def scalar_unit(u, take_roots=True):
+            done = [t for t in range(PACK) if (u, t) in squares]
+            behind = None
+            for t in range(PACK):
+                if t not in done:
+                    square_by_scalar(u, t)
+                    if behind is not None and take_roots:
+                        root(u, behind)
+                    behind = t
+            if take_roots:
+                for t in done[:1] + [behind] + done[1:]:
+                    root(u, t)
+
+        def interleave_by_vector(words, u, cols=WHOLE):
             nc.vector.tensor_copy(
                 words.rearrange("p (c i) t -> p c t i", i=4), roots[u][:, :, cols].rearrange("p t (c i) -> p c t i", i=4)
             )
 
-        def interleave_on_gpsimd(words, u, cols):
-            nc.gpsimd.tensor_scalar(words, roots[u][:, :, cols].rearrange("p t j -> p j t"), 1.0, 0.0, ALU.mult, ALU.add)
+        def interleave_by_gpsimd(words, u):
+            nc.gpsimd.tensor_scalar(words, roots[u][:].rearrange("p t j -> p j t"), 1.0, 0.0, ALU.mult, ALU.add)
 
-        def quantize_h(words, u, cols):
-            nc.vector.quantize_mx(h_codes[u][:, cols].bitcast(FP8X4), h_plane[u][:, cols], words.rearrange("p j t -> p (j t)"))
+        h_codes = [kept([P, CHUNK], U32, "h_codes%d" % u) for u in range(len(UNITS))]
+        h_plane = [kept([P, CHUNK], U8, "h_plane%d" % u) for u in range(len(UNITS))]
 
-        def last_product(acc, c, half, b, cols, start, stop):
+        def quantize_h(words, u, cols=WHOLE):
+            quantize(h_codes[u][:, cols], h_plane[u][:, cols], words)
+
+        def last_pass(acc, c, half, b, cols, start, stop):
             w_cols = slice(b * N + half * P, b * N + (half + 1) * P)
             u = UNITS.index((c, b))
             nc.tensor.matmul_mx(
@@ -328,14 +269,11 @@ def tile_list_flow_residual_refine_kernel(
                 h_codes[u][:, cols].bitcast(FP8X4), h_plane[u][:, cols], start=start, stop=stop,
             )
 
-        whole = slice(0, CHUNK)
-        halves_of_chunk = [slice(0, CHUNK // 2), slice(CHUNK // 2, CHUNK)]
-
         def multiply_chunk(c):
             accs = [psum.tile([P, CHUNK], F32, name="out_acc%d" % half, tag="out_acc%d" % half) for half in range(N // P)]
             for half in range(N // P):
                 for b in range(HALVES):
-                    last_product(accs[half][:], c, half, b, whole, b == 0, b == HALVES - 1)
+                    last_pass(accs[half][:], c, half, b, WHOLE, b == 0, b == HALVES - 1)
             return accs
 
         def result_tile(width):
@@ -346,91 +284,106 @@ def tile_list_flow_residual_refine_kernel(
             copy(result[:], accs[half][:])
             nc.sync.dma_start(out[half * P : (half + 1) * P, c * CHUNK : (c + 1) * CHUNK], result[:])
 
-        def open_unit(u):
-            by_vector = [t for t in range(PACK) if (u, t) in squares or (u, t) in SQUARES_BESIDE_CAST]
-            behind = None
+        roots[0] = after_roots0([P, PACK, CHUNK], BF16, "roots0", 4096)
+        roots[1] = after_roots1([P, PACK, CHUNK], BF16, "roots1", 4096)
+        roots[2] = kept([P, PACK, CHUNK], BF16, "roots2")
+        roots[3] = after_roots3([P, PACK, CHUNK], BF16, "roots3", 0)
+        roots[4] = kept([P, PACK, CHUNK], BF16, "roots4")
+        roots[5] = kept([P, PACK, CHUNK], BF16, "roots5")
+
+        squares0 = after_squares0([P, PACK, CHUNK], F32, "squares0", 0)
+        banks = [psum.tile([P, 2, HALF], F32, name="bank", tag="bank", bufs=BANKS) for index in range(PACK)]
+        for half, cols in enumerate(halves):
             for t in range(PACK):
-                if t not in by_vector:
-                    square_on_scalar(u, t)
-                    if behind is not None and u < LAST:
-                        root(u, behind, whole)
-                    behind = t
-                elif (u, t) not in squares:
-                    square_on_vector(u, t, square_tile())
-            return by_vector[:1] + [behind] + by_vector[1:]
+                pass1(banks[2 * half + t // 2][:, t % 2, :], 0, 0, t, cols, t % 2 == 0, False)
+        for half, cols in enumerate(halves):
+            for pair in range(2):
+                bank = banks[2 * half + pair]
+                for index in range(2):
+                    pass2(bank[:, index, :], 0, 0, 2 * pair + index, cols, False, index == 1)
+                nc.scalar.activation(squares0[:, 2 * pair : 2 * pair + 2, cols], bank[:], ACT.Square)
+        for t in range(PACK):
+            squares[0, t] = squares0[:, t, :]
 
-        def close_unit(u, waiting):
-            for t in waiting:
-                root(u, t, whole)
+        w3_raw = keep.tile([P, HALVES, PACK, N], F32, name="w3_raw", tag="words_then_w3")
+        w3_rows = w3.rearrange("(b u t e) n -> b t u e n", b=HALVES, t=PACK, e=RUN)
+        for b in range(HALVES):
+            for t in range(PACK):
+                nc.sync.dma_start(w3_raw[:, b, t, :], w3_rows[b, t])
 
-        def finish_on_vector(u, last_half=None):
-            words = [keep.tile([P, CHUNK // 2, PACK], BF16, name="words%d_0" % u, align_bytes=64)]
-            words.append(last_half or keep.tile([P, CHUNK // 2, PACK], BF16, name="words%d_1" % u, align_bytes=64))
-            for part, cols in zip(words, halves_of_chunk):
-                interleave_on_vector(part[:], u, cols)
-            for part, cols in zip(words, halves_of_chunk):
-                quantize_h(part[:], u, cols)
-
-        waiting = open_first_unit()
-        w3_raw = load_w3()
-        w1_cast1 = prepare_w1_second_half()
-        for u, t in SQUARES_BESIDE_CAST:
-            if u == 1:
-                square_on_vector(u, t, square_tile())
-        close_unit(0, waiting)
+        w1_cast1 = after_scales1([P, PACK, PASS], BF16, "w1_cast1", 12288)
+        nc.gpsimd.tensor_scalar(
+            w1_cast1[:].rearrange("p t (u e i) -> p u t e i", e=RUN, i=PACK),
+            w1_raw1[:].rearrange("p i (u t e) -> p u t e i", t=PACK, e=RUN),
+            -1.0, 0.0, ALU.mult, ALU.add,
+        )
+        for t in range(3):
+            square_by_vector(1, t, square_tile())
+        for t in range(PACK):
+            root(0, t)
+        w2_codes.append(after_squares0([P, 2 * PASS], U8, "w2_codes1", 0))
+        w1_codes.append(after_squares0([P, PASS], U32, "w1_codes1", 2048))
         deal_w2(1, w2_raw1)
-        quantize_w1(w1_cast1, 1)
+        quantize(w1_codes[1][:], w1_plane[:, PASS:H], w1_cast1[:])
 
-        waiting = open_unit(1)
-        words0 = after_s1.tile([P, CHUNK, PACK], BF16, name="words0", align_bytes=64, offset=4096)
-        interleave_on_gpsimd(words0[:], 0, whole)
-        held = after_s1.tile([P, len(SQUARES_BESIDE_INTERLEAVE), CHUNK], F32, name="held", align_bytes=64, offset=10304)
-        for index, (u, t) in enumerate(SQUARES_BESIDE_INTERLEAVE):
-            square_on_vector(u, t, held[:, index, :])
-        quantize_h(words0[:], 0, whole)
-        close_unit(1, waiting)
+        scalar_unit(1)
+        h_words0 = after_scales1([P, CHUNK, PACK], BF16, "h_words0", 8256)
+        interleave_by_gpsimd(h_words0[:], 0)
+        held = after_squares0([P, 3, CHUNK], F32, "held", 5120)
+        for t in range(3):
+            square_by_vector(4, t, held[:, t, :])
+        quantize_h(h_words0[:], 0)
 
-        waiting = open_unit(2)
-        words1 = after_s1.tile([P, CHUNK, PACK], BF16, name="words1", align_bytes=64, offset=64)
-        interleave_on_gpsimd(words1[:], 1, whole)
-        square30 = after_s1.tile([P, CHUNK], F32, name="square30", align_bytes=64, offset=4160)
-        bank30 = first_products(3, 0)
-        squares[3, 0] = square30[:]
-        nc.vector.tensor_reduce(square30[:, 0:HALF], bank30[:, 0:HALF].unsqueeze(2).to_broadcast([P, HALF, 2]), AXIS.X, ALU.mult)
-        w3_cast = cast_w3(w3_raw)
-        quantize_h(words1[:], 1, whole)
-        quantize_w3(w3_cast)
-        close_unit(2, waiting)
-        nc.scalar.activation(square30[:, HALF:CHUNK], bank30[:, HALF:CHUNK], ACT.Square)
-        close_unit(3, open_unit(3))
+        scalar_unit(2)
+        h_words1 = after_scales1([P, CHUNK, PACK], BF16, "h_words1", 4224)
+        interleave_by_gpsimd(h_words1[:], 1)
+        square_by_vector(3, 0, after_roots0([P, CHUNK], F32, "square30", 4160)[:])
+        w3_cast = after_roots0([P, HALVES, N * PACK], BF16, "w3_cast", 64)
+        for b in range(HALVES):
+            column = P - HALVES + b
+            nc.vector.tensor_tensor(
+                w3_cast[:, b, :].rearrange("p (c i t) -> p c t i", i=4, t=PACK),
+                w3_raw[:, b].rearrange("p t (c i) -> p c t i", i=4),
+                sign_turned[:, :, column : column + 1].unsqueeze(1).to_broadcast([P, N // 4, PACK, 4]),
+                ALU.mult,
+            )
+        quantize_h(h_words1[:], 1)
+        h_words2 = after_roots1([P, CHUNK, PACK], BF16, "h_words2", 64)
+        interleave_by_vector(h_words2[:], 2)
+        w3_codes = after_roots1([P, HALVES * N], U32, "w3_codes", 4160)
+        w3_plane = kept([P, HALVES * N], U8, "w3_plane")
+        quantize(w3_codes[:], w3_plane[:], w3_cast[:])
+        quantize_h(h_words2[:], 2)
 
-        waiting = open_unit(4)
-        finish_on_vector(3, after_unit3.tile([P, CHUNK // 2, PACK], BF16, name="words3_1", align_bytes=64, offset=3072))
-        words2 = after_unit3.tile([P, CHUNK, PACK], BF16, name="words2", align_bytes=64, offset=0)
-        interleave_on_gpsimd(words2[:, 0:GPSIMD_COLUMNS, :], 2, slice(0, GPSIMD_COLUMNS))
-        late_square = after_unit3.tile([P, CHUNK], F32, name="late_square", align_bytes=64, offset=4096)
-        square_on_vector(LAST, 0, late_square[:])
+        scalar_unit(3)
+        h_words3 = after_roots1([P, CHUNK, PACK], BF16, "h_words3", 0)
+        interleave_by_gpsimd(h_words3[:], 3)
+        scalar_unit(4)
+        late = after_roots0([P, 2, CHUNK], F32, "late_squares", 64)
+        square_by_vector(LAST, 0, late[:, 0, :])
+        shared_bank = square_by_vector(LAST, 1, late[:, 1, :], halves[0])
         accs = multiply_chunk(0)
         for half in reversed(range(N // P)):
             store_half(accs, 0, half, nc.vector.tensor_copy)
-        interleave_on_vector(words2[:, GPSIMD_COLUMNS:CHUNK, :], 2, slice(GPSIMD_COLUMNS, CHUNK))
-        quantize_h(words2[:], 2, whole)
-        close_unit(4, waiting)
-
-        open_unit(LAST)
-        finish_on_vector(4)
+        h_words4 = after_roots3([P, CHUNK, PACK], BF16, "h_words4", 0)
+        interleave_by_vector(h_words4[:], 4)
+        quantize_h(h_words3[:], 3)
         accs = multiply_chunk(1)
+        quantize_h(h_words4[:], 4)
+
+        nc.scalar.activation(late[:, 1, halves[1]], shared_bank[:, halves[1]], ACT.Square)
+        scalar_unit(LAST, take_roots=False)
         for piece in LAST_PIECES:
             for t in range(PACK):
                 root(LAST, t, piece)
-        interleaved = None
+        behind = None
         for index, piece in enumerate(LAST_PIECES):
-            words = keep.tile([P, piece.stop - piece.start, PACK], BF16, name="piece_words%d" % index, align_bytes=64)
-            interleave_on_vector(words[:], LAST, piece)
-            if interleaved is not None:
-                quantize_h(*interleaved)
-            interleaved = (words[:], LAST, piece)
-        quantize_h(*interleaved)
+            words = kept([P, piece.stop - piece.start, PACK], BF16, "piece_words%d" % index)
+            interleave_by_vector(words[:], LAST, piece)
+            if behind is not None:
+                quantize_h(*behind)
+            behind = (words[:], LAST, piece)
+        quantize_h(*behind)
         for half in range(N // P):
             store_half(accs, 1, half, nc.scalar.copy)
         out_halves = out.rearrange("(h p) j -> p h j", p=P)
@@ -441,7 +394,7 @@ def tile_list_flow_residual_refine_kernel(
             for b in range(HALVES):
                 for half in range(N // P):
                     first, final = (b, half) == (0, 0), (b, half) == (HALVES - 1, N // P - 1)
-                    last_product(bank[:, half * width : (half + 1) * width], CHUNKS - 1, half, b, piece, first, final)
+                    last_pass(bank[:, half * width : (half + 1) * width], CHUNKS - 1, half, b, piece, first, final)
             result = result_tile((N // P) * width)
             nc.scalar.copy(result[:], bank[:, 0 : (N // P) * width])
             queue = nc.scalar if piece.stop == CHUNK else nc.sync

@@ -56,6 +56,7 @@ def tile_list_flow_residual_refine_kernel(
         after_roots0 = placed_pool("after_roots0")
         after_roots1 = placed_pool("after_roots1")
         after_roots3 = placed_pool("after_roots3")
+        after_pieces = placed_pool("after_pieces")
 
         def kept(shape, dtype, name):
             return keep.tile(shape, dtype, name=name, align_bytes=64)
@@ -64,18 +65,16 @@ def tile_list_flow_residual_refine_kernel(
         nc.gpsimd.memset(w2_scale_raw[:].bitcast(I32), 0)
         list1 = keep.tile([P, S // 16], U16, name="list1")
         list2 = keep.tile([P, S // 16], U16, name="list2")
-        scale_win1 = after_scales1([P, T], U8, "scale_win1", 16384)
+        scale_win1 = kept([P, T], U8, "scale_win1")
         scale_win2 = after_scales2([P, T], U8, "scale_win2", 8192)
         nc.sync.dma_start(list1[:], offs)
         nc.sync.dma_start(scale_win1[ROWS1:P, :].bitcast(I32), tab_scales[0].bitcast(I32))
         nc.sync.dma_start(list2[:], offs2)
-        nc.sync.dma_start(scale_win2[ROWS2 : P // 2, :].bitcast(I32), tab2_scales[0].bitcast(I32))
+        nc.sync.dma_start(scale_win2[ROWS1:P, :].bitcast(I32), tab2_scales[0].bitcast(I32))
         nc.vector.memset(scale_win1[0:ROWS1, :].bitcast(I32), 0)
-        nc.vector.memset(scale_win2[0:ROWS2, :].bitcast(I32), 0)
-        nc.gpsimd.memset(scale_win2[P // 2 : P, :].bitcast(I32), 0)
-        plane1 = kept([P, S], U8, "plane1")
-        plane2 = kept([P, S], U8, "plane2")
-        nc.gpsimd.memset(plane1[:].bitcast(I32), 0)
+        nc.vector.memset(scale_win2[0:ROWS1, :].bitcast(I32), 0)
+        first_plane = kept([P, 2, S - CHUNK], U8, "first_plane")
+        later_plane = kept([P, 2, CHUNK], U8, "later_plane")
 
         warm_in = keep.tile([P, 1], F32, name="warm_in")
         warm_out = keep.tile([P, 1], F32, name="warm_out")
@@ -98,10 +97,13 @@ def tile_list_flow_residual_refine_kernel(
         nc.sync.dma_start(word_win1[:], tab_words[0].rearrange("p t i -> p (t i)").bitcast(I32))
         w2_raw0 = kept([P, PASS // 2], I32, "w2_raw0")
         nc.sync.dma_start(w2_raw0[:], w2_rows[:, 0 : PASS // 2])
+        word_win2 = after_scales1([P, T], I32, "word_win2", 64)
+        nc.sync.dma_start(word_win2[:], tab2_words[0].rearrange("p t i -> p (t i)").bitcast(I32))
 
         identity = kept([P, P], F32, "identity")
         make_identity(nc, identity[:])
-        nc.gpsimd.memset(plane2[:].bitcast(I32), 0)
+        for plane in (first_plane, later_plane):
+            nc.gpsimd.memset(plane[:].rearrange("p a x -> p (a x)").bitcast(I32), 0)
 
         def turn(rows, name, tag, bufs):
             turned = psum.tile([P, PACK, P], F32, name=name, tag=tag, bufs=bufs)
@@ -125,23 +127,26 @@ def tile_list_flow_residual_refine_kernel(
         nc.scalar.activation(sign_dealt[:], sign_raw[:], ACT.Sign, bias=0.5)
         sign_turned = turn(sign_dealt, "sign_turned", "out_acc1", 1)
 
-        picked1 = kept([P, S], U8, "picked1")
-        picked2 = kept([P, S], U8, "picked2")
-        nc.vector.tensor_copy(picked1[:], scale_win1[:].indirect(list1[:]))
-        nc.vector.tensor_copy(picked2[:], scale_win2[:].indirect(list2[:]))
+        picked = kept([P, 2 * S], U8, "picked")
+        nc.vector.tensor_copy(picked[:, 0:S], scale_win1[:].indirect(list1[:]))
+        nc.vector.tensor_copy(picked[:, S : 2 * S], scale_win2[:].indirect(list2[:]))
+        rows_by_table = picked[:].bitcast(I32).rearrange("p (a w) -> p a w", a=2)
 
-        def move_scale_rows(plane, plane_row, picked, first_row):
+        def move_scale_rows(plane, first, end):
+            to = plane[:].rearrange("p a w -> p (a w)").bitcast(I32).rearrange("p (a w) -> p a w", a=2)
             for quad in range(QUADS):
-                row = first_row + 4 * quad
-                to = 32 * quad + plane_row
-                nc.sync.dma_start(plane[to : to + 4, :].bitcast(I32), picked[row : row + 4, :].bitcast(I32))
+                row = ROWS1 + 4 * quad
+                nc.sync.dma_start(to[32 * quad : 32 * quad + 4], rows_by_table[row : row + 4, :, first // 4 : end // 4])
 
-        move_scale_rows(plane1, PLANE1_ROW, picked1, ROWS1)
-        word_win2 = after_scales1([P, T], I32, "word_win2", 64)
-        nc.sync.dma_start(word_win2[:], tab2_words[0].rearrange("p t i -> p (t i)").bitcast(I32))
-        move_scale_rows(plane2, 0, picked2, ROWS2)
+        def moving_plane(table, c, cols):
+            if c == CHUNKS - 1:
+                return later_plane[:, table, cols]
+            return first_plane[:, table, c * CHUNK + cols.start : c * CHUNK + cols.stop]
+
+        move_scale_rows(first_plane, 0, S - CHUNK)
         w1_raw1 = after_scales2([P, PACK, PASS], F32, "w1_raw1", 64)
         nc.sync.dma_start(w1_raw1[:], w1_rows[:, :, PASS:H])
+        move_scale_rows(later_plane, S - CHUNK, S)
         w2_raw1 = after_scales2([P, PASS // 2], I32, "w2_raw1", 8256)
         nc.sync.dma_start(w2_raw1[:], w2_rows[:, PASS // 2 : PASS])
 
@@ -184,18 +189,16 @@ def tile_list_flow_residual_refine_kernel(
         words2 = {c: gather_words(kept([P, CHUNK], U32, "words2_%d" % c), word_win2, list2, c * CHUNK, CHUNK) for c in range(1, CHUNKS)}
 
         def pass1(acc, c, b, t, cols, start, stop):
-            entries = slice(c * CHUNK + cols.start, c * CHUNK + cols.stop)
             nc.tensor.matmul_mx(
                 acc, w1_codes[b][:, t * P : (t + 1) * P].bitcast(FP8X4), w1_plane[:, b * PASS + t * P : b * PASS + (t + 1) * P],
-                words1[c][:, cols].bitcast(FP8X4), plane1[PLANE1_ROW:P, entries], start=start, stop=stop,
+                words1[c][:, cols].bitcast(FP8X4), moving_plane(0, c, cols), start=start, stop=stop,
             )
 
         def pass2(acc, c, b, t, cols, start, stop):
-            entries = slice(c * CHUNK + cols.start, c * CHUNK + cols.stop)
             words = first2[cols.start // HALF] if c == 0 else words2[c]
             nc.tensor.matmul_mx(
                 acc, w2_codes[b][:, 2 * t * P : 2 * (t + 1) * P].bitcast(FP4X4), w2_plane[:, b * PASS + t * P : b * PASS + (t + 1) * P],
-                words[:].bitcast(FP8X4), plane2[:, entries], start=start, stop=stop,
+                words[:].bitcast(FP8X4), moving_plane(1, c, cols), start=start, stop=stop,
             )
 
         halves = [slice(0, HALF), slice(HALF, CHUNK)]
@@ -293,12 +296,18 @@ def tile_list_flow_residual_refine_kernel(
 
         squares0 = after_squares0([P, PACK, CHUNK], F32, "squares0", 0)
         banks = [psum.tile([P, 2, HALF], F32, name="bank", tag="bank", bufs=BANKS) for index in range(PACK)]
-        for half, cols in enumerate(halves):
-            for t in range(PACK):
-                pass1(banks[2 * half + t // 2][:, t % 2, :], 0, 0, t, cols, t % 2 == 0, False)
+        warm_acc = psum.tile([P, CHUNK], F32, name="warm_acc", tag="out_acc0")
+        for index in range(5):
+            w_cols = slice((index % PACK) * P, (index % PACK + 1) * P)
+            nc.tensor.matmul_mx(
+                warm_acc[:], w1_codes[0][:, w_cols].bitcast(FP8X4), w1_plane[:, w_cols],
+                words1[0][:].bitcast(FP8X4), w1_plane[:, 0:CHUNK], start=True, stop=True,
+            )
         for half, cols in enumerate(halves):
             for pair in range(2):
                 bank = banks[2 * half + pair]
+                for index in range(2):
+                    pass1(bank[:, index, :], 0, 0, 2 * pair + index, cols, index == 0, False)
                 for index in range(2):
                     pass2(bank[:, index, :], 0, 0, 2 * pair + index, cols, False, index == 1)
                 nc.scalar.activation(squares0[:, 2 * pair : 2 * pair + 2, cols], bank[:], ACT.Square)
@@ -378,7 +387,7 @@ def tile_list_flow_residual_refine_kernel(
                 root(LAST, t, piece)
         behind = None
         for index, piece in enumerate(LAST_PIECES):
-            words = kept([P, piece.stop - piece.start, PACK], BF16, "piece_words%d" % index)
+            words = after_pieces([P, piece.stop - piece.start, PACK], BF16, "piece_words%d" % index, 8 * piece.start)
             interleave_by_vector(words[:], LAST, piece)
             if behind is not None:
                 quantize_h(*behind)
@@ -395,8 +404,12 @@ def tile_list_flow_residual_refine_kernel(
                 for half in range(N // P):
                     first, final = (b, half) == (0, 0), (b, half) == (HALVES - 1, N // P - 1)
                     last_pass(bank[:, half * width : (half + 1) * width], CHUNKS - 1, half, b, piece, first, final)
-            result = result_tile((N // P) * width)
-            nc.scalar.copy(result[:], bank[:, 0 : (N // P) * width])
+            if piece == LAST_PIECES[1]:
+                result = after_pieces([P, (N // P) * width], F32, "first_result", 8 * LAST_PIECES[-1].start)
+                nc.vector.tensor_copy(result[:], bank[:, 0 : (N // P) * width])
+            else:
+                result = result_tile((N // P) * width)
+                nc.scalar.copy(result[:], bank[:, 0 : (N // P) * width])
             queue = nc.scalar if piece.stop == CHUNK else nc.sync
             queue.dma_start(
                 out_halves[:, :, first_col + piece.start : first_col + piece.stop],

@@ -70,11 +70,12 @@ def tile_list_flow_residual_refine_kernel(
         nc.sync.dma_start(list1[:], offs)
         nc.sync.dma_start(scale_win1[ROWS1:P, :].bitcast(I32), tab_scales[0].bitcast(I32))
         nc.sync.dma_start(list2[:], offs2)
-        nc.sync.dma_start(scale_win2[ROWS1:P, :].bitcast(I32), tab2_scales[0].bitcast(I32))
+        nc.sync.dma_start(scale_win2[ROWS2 : P // 2, :].bitcast(I32), tab2_scales[0].bitcast(I32))
         nc.vector.memset(scale_win1[0:ROWS1, :].bitcast(I32), 0)
-        nc.vector.memset(scale_win2[0:ROWS1, :].bitcast(I32), 0)
-        first_plane = kept([P, 2, S - CHUNK], U8, "first_plane")
-        later_plane = kept([P, 2, CHUNK], U8, "later_plane")
+        nc.vector.memset(scale_win2[0:ROWS2, :].bitcast(I32), 0)
+        nc.gpsimd.memset(scale_win2[P // 2 : P, :].bitcast(I32), 0)
+        plane1 = kept([P, S], U8, "plane1")
+        plane2 = kept([P, S], U8, "plane2")
 
         warm_in = keep.tile([P, 1], F32, name="warm_in")
         warm_out = keep.tile([P, 1], F32, name="warm_out")
@@ -102,8 +103,8 @@ def tile_list_flow_residual_refine_kernel(
 
         identity = kept([P, P], F32, "identity")
         make_identity(nc, identity[:])
-        for plane in (first_plane, later_plane):
-            nc.gpsimd.memset(plane[:].rearrange("p a x -> p (a x)").bitcast(I32), 0)
+        for plane in (plane1, plane2):
+            nc.gpsimd.memset(plane[:].bitcast(I32), 0)
 
         def turn(rows, name, tag, bufs):
             turned = psum.tile([P, PACK, P], F32, name=name, tag=tag, bufs=bufs)
@@ -127,26 +128,25 @@ def tile_list_flow_residual_refine_kernel(
         nc.scalar.activation(sign_dealt[:], sign_raw[:], ACT.Sign, bias=0.5)
         sign_turned = turn(sign_dealt, "sign_turned", "out_acc1", 1)
 
-        picked = kept([P, 2 * S], U8, "picked")
-        nc.vector.tensor_copy(picked[:, 0:S], scale_win1[:].indirect(list1[:]))
-        nc.vector.tensor_copy(picked[:, S : 2 * S], scale_win2[:].indirect(list2[:]))
-        rows_by_table = picked[:].bitcast(I32).rearrange("p (a w) -> p a w", a=2)
+        picked1 = kept([P, S], U8, "picked1")
+        picked2 = kept([P, S], U8, "picked2")
+        nc.vector.tensor_copy(picked1[:], scale_win1[:].indirect(list1[:]))
+        nc.vector.tensor_copy(picked2[:], scale_win2[:].indirect(list2[:]))
 
-        def move_scale_rows(plane, first, end):
-            to = plane[:].rearrange("p a w -> p (a w)").bitcast(I32).rearrange("p (a w) -> p a w", a=2)
+        def move_scale_rows(plane, plane_row, picked, first_row):
             for quad in range(QUADS):
-                row = ROWS1 + 4 * quad
-                nc.sync.dma_start(to[32 * quad : 32 * quad + 4], rows_by_table[row : row + 4, :, first // 4 : end // 4])
+                row = first_row + 4 * quad
+                to = 32 * quad + plane_row
+                nc.sync.dma_start(plane[to : to + 4, :].bitcast(I32), picked[row : row + 4, :].bitcast(I32))
 
         def moving_plane(table, c, cols):
-            if c == CHUNKS - 1:
-                return later_plane[:, table, cols]
-            return first_plane[:, table, c * CHUNK + cols.start : c * CHUNK + cols.stop]
+            entries = slice(c * CHUNK + cols.start, c * CHUNK + cols.stop)
+            return plane2[:, entries] if table == 1 else plane1[PLANE1_ROW:P, entries]
 
-        move_scale_rows(first_plane, 0, S - CHUNK)
+        move_scale_rows(plane1, PLANE1_ROW, picked1, ROWS1)
+        move_scale_rows(plane2, 0, picked2, ROWS2)
         w1_raw1 = after_scales2([P, PACK, PASS], F32, "w1_raw1", 64)
         nc.sync.dma_start(w1_raw1[:], w1_rows[:, :, PASS:H])
-        move_scale_rows(later_plane, S - CHUNK, S)
         w2_raw1 = after_scales2([P, PASS // 2], I32, "w2_raw1", 8256)
         nc.sync.dma_start(w2_raw1[:], w2_rows[:, PASS // 2 : PASS])
 
@@ -304,10 +304,10 @@ def tile_list_flow_residual_refine_kernel(
                 words1[0][:].bitcast(FP8X4), w1_plane[:, 0:CHUNK], start=True, stop=True,
             )
         for half, cols in enumerate(halves):
+            for t in range(PACK):
+                pass1(banks[2 * half + t // 2][:, t % 2, :], 0, 0, t, cols, t % 2 == 0, False)
             for pair in range(2):
                 bank = banks[2 * half + pair]
-                for index in range(2):
-                    pass1(bank[:, index, :], 0, 0, 2 * pair + index, cols, index == 0, False)
                 for index in range(2):
                     pass2(bank[:, index, :], 0, 0, 2 * pair + index, cols, False, index == 1)
                 nc.scalar.activation(squares0[:, 2 * pair : 2 * pair + 2, cols], bank[:], ACT.Square)

from contextlib import ExitStack

import concourse.mybir as mybir
from concourse.masks import make_identity

K, H, N, T, S = 512, 1024, 256, 4096, 1536
FLOPS = 2 * (2 * K * H * S + H * N * S)

F32 = mybir.dt.float32
BF16 = mybir.dt.bfloat16
I32 = mybir.dt.int32
U32 = mybir.dt.uint32
U16 = mybir.dt.uint16
U8 = mybir.dt.uint8
FP8X4 = mybir.dt.float8_e4m3fn_x4
FP4X4 = mybir.dt.float4_e2m1fn_x4
ALU = mybir.AluOpType
ACT = mybir.ActivationFunctionType
AXIS = mybir.AxisListType

P = 128
PACK = 4
PASS = P * PACK
CHUNK = 512
HALF = CHUNK // 2
CHUNKS = S // CHUNK
HALVES = H // PASS
RUN = 4
QUADS = 4
ROWS1 = P - 4 * QUADS
ROWS2 = P // 2 - 4 * QUADS
PLANE1_ROW = 4
BANKS = 6
UNITS = [(0, 0), (1, 0), (0, 1), (1, 1), (2, 0), (2, 1)]
LAST = len(UNITS) - 1
LAST_PIECES = [slice(0, 256), slice(256, 384), slice(384, 512)]
WHOLE = slice(0, CHUNK)


def tile_list_flow_residual_refine_kernel(
    tc, tab_words, tab_scales, tab2_words, tab2_scales, offs, offs2, w1, w2_words, w2_scales, gain, w3, out
):
    nc = tc.nc
    with ExitStack() as ctx:
        keep = ctx.enter_context(tc.tile_pool(name="keep", bufs=1))
        ring = ctx.enter_context(tc.tile_pool(name="ring", bufs=2))
        psum = ctx.enter_context(tc.psum_pool(name="psum", bufs=1))

        def placed_pool(name):
            pool = ctx.enter_context(tc.tile_pool(name=name, bufs=1))
            return lambda shape, dtype, tile_name, offset: pool.tile(shape, dtype, name=tile_name, align_bytes=64, offset=offset)

        after_scales1 = placed_pool("after_scales1")
        after_scales2 = placed_pool("after_scales2")
        after_squares0 = placed_pool("after_squares0")
        after_roots0 = placed_pool("after_roots0")
        after_roots1 = placed_pool("after_roots1")
        after_roots3 = placed_pool("after_roots3")
        after_pieces = placed_pool("after_pieces")

        def kept(shape, dtype, name):
            return keep.tile(shape, dtype, name=name, align_bytes=64)

        w2_scale_raw = kept([P, H], U8, "w2_scale_raw")
        nc.gpsimd.memset(w2_scale_raw[:].bitcast(I32), 0)
        list1 = keep.tile([P, S // 16], U16, name="list1")
        list2 = keep.tile([P, S // 16], U16, name="list2")
        scale_win1 = kept([P, T], U8, "scale_win1")
        scale_win2 = after_scales2([P, T], U8, "scale_win2", 8192)
        nc.sync.dma_start(list1[:], offs)
        nc.sync.dma_start(scale_win1[ROWS1:P, :].bitcast(I32), tab_scales[0].bitcast(I32))
        nc.sync.dma_start(list2[:], offs2)
        nc.sync.dma_start(scale_win2[ROWS2 : P // 2, :].bitcast(I32), tab2_scales[0].bitcast(I32))
        nc.vector.memset(scale_win1[0:ROWS1, :].bitcast(I32), 0)
        nc.vector.memset(scale_win2[0:ROWS2, :].bitcast(I32), 0)
        nc.gpsimd.memset(scale_win2[P // 2 : P, :].bitcast(I32), 0)
        plane1 = kept([P, S], U8, "plane1")
        plane2 = kept([P, S], U8, "plane2")

        warm_in = keep.tile([P, 1], F32, name="warm_in")
        warm_out = keep.tile([P, 1], F32, name="warm_out")
        nc.vector.memset(warm_in[:], 1.0)
        nc.scalar.activation(warm_out[:], warm_in[:], ACT.Sqrt)

        w1_rows = w1.rearrange("(p i) r -> p i r", i=PACK)
        w2_rows = w2_words[0].bitcast(I32)
        gain_rows = kept([P, PASS], F32, "gain_rows")
        nc.sync.dma_start(gain_rows[P - HALVES : P, :], gain.rearrange("(b r) -> b r", b=HALVES))
        nc.gpsimd.memset(gain_rows[0 : P - HALVES, :], 0.0)
        w1_raw0 = kept([P, PACK, PASS], F32, "w1_raw0")
        nc.sync.dma_start(w1_raw0[:], w1_rows[:, :, 0:PASS])
        for quad in range(QUADS):
            nc.sync.dma_start(
                w2_scale_raw[32 * quad : 32 * quad + 4, :].bitcast(I32),
                w2_scales[0, 4 * quad : 4 * quad + 4, :].bitcast(I32),
            )
        word_win1 = keep.tile([P, T], I32, name="word_win1", tag="words_then_w3")
        nc.sync.dma_start(word_win1[:], tab_words[0].rearrange("p t i -> p (t i)").bitcast(I32))
        w2_raw0 = kept([P, PASS // 2], I32, "w2_raw0")
        nc.sync.dma_start(w2_raw0[:], w2_rows[:, 0 : PASS // 2])
        word_win2 = after_scales1([P, T], I32, "word_win2", 64)
        nc.sync.dma_start(word_win2[:], tab2_words[0].rearrange("p t i -> p (t i)").bitcast(I32))

        identity = kept([P, P], F32, "identity")
        make_identity(nc, identity[:])
        for plane in (plane1, plane2):
            nc.gpsimd.memset(plane[:].bitcast(I32), 0)

        def turn(rows, name, tag, bufs):
            turned = psum.tile([P, PACK, P], F32, name=name, tag=tag, bufs=bufs)
            for t in range(PACK):
                nc.tensor.transpose(turned[:, t, :], rows[:, t * P : (t + 1) * P], identity[:])
            return turned

        gain_dealt = kept([P, PASS], F32, "gain_dealt")
        nc.scalar.copy(
            gain_dealt[:].rearrange("p (t u e) -> p t u e", t=PACK, e=RUN),
            gain_rows[:].rearrange("p (u t e) -> p t u e", t=PACK, e=RUN),
        )
        gain_turned = turn(gain_dealt, "gain_turned", "bank", BANKS)
        gain_cols = kept([P, HALVES, PACK], F32, "gain_cols")
        gain_sq = kept([P, HALVES, PACK], F32, "gain_sq")
        nc.scalar.copy(gain_cols[:], gain_turned[:].rearrange("p t x -> p x t")[:, P - HALVES : P, :])
        nc.gpsimd.tensor_tensor(gain_sq[:], gain_cols[:], gain_cols[:], ALU.mult)
        sign_raw = kept([P, PASS], F32, "sign_raw")
        sign_dealt = kept([P, PASS], F32, "sign_dealt")
        nc.scalar.activation(sign_raw[:], gain_dealt[:], ACT.Sign)
        nc.scalar.activation(sign_dealt[:], sign_raw[:], ACT.Sign, bias=0.5)
        sign_turned = turn(sign_dealt, "sign_turned", "out_acc1", 1)

        picked1 = kept([P, S], U8, "picked1")
        picked2 = kept([P, S], U8, "picked2")
        nc.vector.tensor_copy(picked1[:], scale_win1[:].indirect(list1[:]))
        nc.vector.tensor_copy(picked2[:], scale_win2[:].indirect(list2[:]))

        def move_scale_rows(plane, plane_row, picked, first_row):
            for quad in range(QUADS):
                row = first_row + 4 * quad
                to = 32 * quad + plane_row
                nc.sync.dma_start(plane[to : to + 4, :].bitcast(I32), picked[row : row + 4, :].bitcast(I32))

        def moving_plane(table, c, cols):
            entries = slice(c * CHUNK + cols.start, c * CHUNK + cols.stop)
            return plane2[:, entries] if table == 1 else plane1[PLANE1_ROW:P, entries]

        move_scale_rows(plane1, PLANE1_ROW, picked1, ROWS1)
        move_scale_rows(plane2, 0, picked2, ROWS2)
        w1_raw1 = after_scales2([P, PACK, PASS], F32, "w1_raw1", 64)
        nc.sync.dma_start(w1_raw1[:], w1_rows[:, :, PASS:H])
        w2_raw1 = after_scales2([P, PASS // 2], I32, "w2_raw1", 8256)
        nc.sync.dma_start(w2_raw1[:], w2_rows[:, PASS // 2 : PASS])

        w1_codes = [kept([P, PASS], U32, "w1_codes0")]
        w1_plane = kept([P, H], U8, "w1_plane")
        w2_codes = [kept([P, 2 * PASS], U8, "w2_codes0")]
        w2_plane = kept([P, H], U8, "w2_plane")

        def quantize(codes, plane, values):
            nc.vector.quantize_mx(codes.bitcast(FP8X4), plane, values.rearrange("p a x -> p (a x)"))

        def deal_w2(b, raw):
            nc.vector.tensor_copy(
                w2_codes[b][:].bitcast(I32).rearrange("p (t u w) -> p t u w", t=PACK, w=2),
                raw[:].rearrange("p (u t w) -> p t u w", t=PACK, w=2),
            )

        w1_cast0 = kept([P, PACK, PASS], BF16, "w1_cast0")
        for t in range(PACK):
            nc.scalar.activation(
                w1_cast0[:, t, :].rearrange("p (u e i) -> p u i e", e=RUN, i=PACK),
                w1_raw0[:].rearrange("p i (u t e) -> p t u i e", t=PACK, e=RUN)[:, t],
                ACT.Copy,
                scale=-1.0,
            )
        quantize(w1_codes[0][:], w1_plane[:, 0:PASS], w1_cast0[:])
        nc.vector.tensor_copy(
            w2_plane[:].bitcast(I32).rearrange("p (b t u) -> p b t u", b=HALVES, t=PACK),
            w2_scale_raw[:].bitcast(I32).rearrange("p (b u t) -> p b t u", b=HALVES, t=PACK),
        )
        deal_w2(0, w2_raw0)

        def gather_words(picked, window, offsets, first, count):
            entries = offsets[:, first // 16 : (first + count) // 16]
            nc.vector.tensor_copy(picked[:], window[:].bitcast(U32).indirect(entries))
            return picked

        words1 = [gather_words(kept([P, CHUNK], U32, "words1_%d" % c), word_win1, list1, c * CHUNK, CHUNK) for c in range(CHUNKS)]
        first2 = [gather_words(kept([P, HALF], U32, "first2_%d" % half), word_win2, list2, half * HALF, HALF) for half in range(2)]
        words2 = {c: gather_words(kept([P, CHUNK], U32, "words2_%d" % c), word_win2, list2, c * CHUNK, CHUNK) for c in range(1, CHUNKS)}

        def pass1(acc, c, b, t, cols, start, stop):
            nc.tensor.matmul_mx(
                acc, w1_codes[b][:, t * P : (t + 1) * P].bitcast(FP8X4), w1_plane[:, b * PASS + t * P : b * PASS + (t + 1) * P],
                words1[c][:, cols].bitcast(FP8X4), moving_plane(0, c, cols), start=start, stop=stop,
            )

        def pass2(acc, c, b, t, cols, start, stop):
            words = first2[cols.start // HALF] if c == 0 else words2[c]
            nc.tensor.matmul_mx(
                acc, w2_codes[b][:, 2 * t * P : 2 * (t + 1) * P].bitcast(FP4X4), w2_plane[:, b * PASS + t * P : b * PASS + (t + 1) * P],
                words[:].bitcast(FP8X4), moving_plane(1, c, cols), start=start, stop=stop,
            )

        halves = [slice(0, HALF), slice(HALF, CHUNK)]

        def products(u, t):
            c, b = UNITS[u]
            bank = psum.tile([P, CHUNK], F32, name="bank", tag="bank", bufs=BANKS)
            if c == 0:
                pass1(bank[:], c, b, t, WHOLE, True, False)
                for cols in halves:
                    pass2(bank[:, cols], c, b, t, cols, False, cols.stop == CHUNK)
            else:
                pass2(bank[:], c, b, t, WHOLE, True, False)
                pass1(bank[:], c, b, t, WHOLE, False, True)
            return bank

        squares = {}
        roots = {}

        def square_tile():
            return ring.tile([P, CHUNK], F32, name="square", tag="square", bufs=16)[:]

        def square_by_scalar(u, t):
            bank = products(u, t)
            squares[u, t] = square_tile()
            nc.scalar.activation(squares[u, t], bank[:], ACT.Square)

        def square_by_vector(u, t, square, cols=WHOLE):
            bank = products(u, t)
            squares[u, t] = square
            width = cols.stop - cols.start
            nc.vector.tensor_reduce(square[:, cols], bank[:, cols].unsqueeze(2).to_broadcast([P, width, 2]), AXIS.X, ALU.mult)
            return bank

        def root(u, t, cols=WHOLE):
            g2 = gain_sq[:, UNITS[u][1], t : t + 1]
            nc.scalar.activation(roots[u][:, t, cols], squares[u, t][:, cols], ACT.Sqrt, bias=g2, scale=g2)

        def scalar_unit(u, take_roots=True):
            done = [t for t in range(PACK) if (u, t) in squares]
            behind = None
            for t in range(PACK):
                if t not in done:
                    square_by_scalar(u, t)
                    if behind is not None and take_roots:
                        root(u, behind)
                    behind = t
            if take_roots:
                for t in done[:1] + [behind] + done[1:]:
                    root(u, t)

        def interleave_by_vector(words, u, cols=WHOLE):
            nc.vector.tensor_copy(
                words.rearrange("p (c i) t -> p c t i", i=4), roots[u][:, :, cols].rearrange("p t (c i) -> p c t i", i=4)
            )

        def interleave_by_gpsimd(words, u):
            nc.gpsimd.tensor_scalar(words, roots[u][:].rearrange("p t j -> p j t"), 1.0, 0.0, ALU.mult, ALU.add)

        h_codes = [kept([P, CHUNK], U32, "h_codes%d" % u) for u in range(len(UNITS))]
        h_plane = [kept([P, CHUNK], U8, "h_plane%d" % u) for u in range(len(UNITS))]

        def quantize_h(words, u, cols=WHOLE):
            quantize(h_codes[u][:, cols], h_plane[u][:, cols], words)

        def last_pass(acc, c, half, b, cols, start, stop):
            w_cols = slice(b * N + half * P, b * N + (half + 1) * P)
            u = UNITS.index((c, b))
            nc.tensor.matmul_mx(
                acc, w3_codes[:, w_cols].bitcast(FP8X4), w3_plane[:, w_cols],
                h_codes[u][:, cols].bitcast(FP8X4), h_plane[u][:, cols], start=start, stop=stop,
            )

        def multiply_chunk(c):
            accs = [psum.tile([P, CHUNK], F32, name="out_acc%d" % half, tag="out_acc%d" % half) for half in range(N // P)]
            for half in range(N // P):
                for b in range(HALVES):
                    last_pass(accs[half][:], c, half, b, WHOLE, b == 0, b == HALVES - 1)
            return accs

        def result_tile(width):
            return ring.tile([P, width], F32, name="result", tag="result", bufs=7)

        def store_half(accs, c, half, copy):
            result = result_tile(CHUNK)
            copy(result[:], accs[half][:])
            nc.sync.dma_start(out[half * P : (half + 1) * P, c * CHUNK : (c + 1) * CHUNK], result[:])

        roots[0] = after_roots0([P, PACK, CHUNK], BF16, "roots0", 4096)
        roots[1] = after_roots1([P, PACK, CHUNK], BF16, "roots1", 4096)
        roots[2] = kept([P, PACK, CHUNK], BF16, "roots2")
        roots[3] = after_roots3([P, PACK, CHUNK], BF16, "roots3", 0)
        roots[4] = kept([P, PACK, CHUNK], BF16, "roots4")
        roots[5] = kept([P, PACK, CHUNK], BF16, "roots5")

        squares0 = after_squares0([P, PACK, CHUNK], F32, "squares0", 0)
        banks = [psum.tile([P, 2, HALF], F32, name="bank", tag="bank", bufs=BANKS) for index in range(PACK)]
        warm_acc = psum.tile([P, CHUNK], F32, name="warm_acc", tag="out_acc0")
        for index in range(5):
            w_cols = slice((index % PACK) * P, (index % PACK + 1) * P)
            nc.tensor.matmul_mx(
                warm_acc[:], w1_codes[0][:, w_cols].bitcast(FP8X4), w1_plane[:, w_cols],
                words1[0][:].bitcast(FP8X4), w1_plane[:, 0:CHUNK], start=True, stop=True,
            )
        for half, cols in enumerate(halves):
            for t in range(PACK):
                pass1(banks[2 * half + t // 2][:, t % 2, :], 0, 0, t, cols, t % 2 == 0, False)
            for pair in range(2):
                bank = banks[2 * half + pair]
                for index in range(2):
                    pass2(bank[:, index, :], 0, 0, 2 * pair + index, cols, False, index == 1)
                nc.scalar.activation(squares0[:, 2 * pair : 2 * pair + 2, cols], bank[:], ACT.Square)
        for t in range(PACK):
            squares[0, t] = squares0[:, t, :]

        w3_raw = keep.tile([P, HALVES, PACK, N], F32, name="w3_raw", tag="words_then_w3")
        w3_rows = w3.rearrange("(b u t e) n -> b t u e n", b=HALVES, t=PACK, e=RUN)
        for b in range(HALVES):
            for t in range(PACK):
                nc.sync.dma_start(w3_raw[:, b, t, :], w3_rows[b, t])

        w1_cast1 = after_scales1([P, PACK, PASS], BF16, "w1_cast1", 12288)
        nc.gpsimd.tensor_scalar(
            w1_cast1[:].rearrange("p t (u e i) -> p u t e i", e=RUN, i=PACK),
            w1_raw1[:].rearrange("p i (u t e) -> p u t e i", t=PACK, e=RUN),
            -1.0, 0.0, ALU.mult, ALU.add,
        )
        for t in range(3):
            square_by_vector(1, t, square_tile())
        for t in range(PACK):
            root(0, t)
        w2_codes.append(after_squares0([P, 2 * PASS], U8, "w2_codes1", 0))
        w1_codes.append(after_squares0([P, PASS], U32, "w1_codes1", 2048))
        deal_w2(1, w2_raw1)
        quantize(w1_codes[1][:], w1_plane[:, PASS:H], w1_cast1[:])

        scalar_unit(1)
        h_words0 = after_scales1([P, CHUNK, PACK], BF16, "h_words0", 8256)
        interleave_by_gpsimd(h_words0[:], 0)
        held = after_squares0([P, 3, CHUNK], F32, "held", 5120)
        for t in range(3):
            square_by_vector(4, t, held[:, t, :])
        quantize_h(h_words0[:], 0)

        scalar_unit(2)
        h_words1 = after_scales1([P, CHUNK, PACK], BF16, "h_words1", 4224)
        interleave_by_gpsimd(h_words1[:], 1)
        square_by_vector(3, 0, after_roots0([P, CHUNK], F32, "square30", 4160)[:])
        w3_cast = after_roots0([P, HALVES, N * PACK], BF16, "w3_cast", 64)
        for b in range(HALVES):
            column = P - HALVES + b
            nc.vector.tensor_tensor(
                w3_cast[:, b, :].rearrange("p (c i t) -> p c t i", i=4, t=PACK),
                w3_raw[:, b].rearrange("p t (c i) -> p c t i", i=4),
                sign_turned[:, :, column : column + 1].unsqueeze(1).to_broadcast([P, N // 4, PACK, 4]),
                ALU.mult,
            )
        quantize_h(h_words1[:], 1)
        h_words2 = after_roots1([P, CHUNK, PACK], BF16, "h_words2", 64)
        interleave_by_vector(h_words2[:], 2)
        w3_codes = after_roots1([P, HALVES * N], U32, "w3_codes", 4160)
        w3_plane = kept([P, HALVES * N], U8, "w3_plane")
        quantize(w3_codes[:], w3_plane[:], w3_cast[:])
        quantize_h(h_words2[:], 2)

        scalar_unit(3)
        h_words3 = after_roots1([P, CHUNK, PACK], BF16, "h_words3", 0)
        interleave_by_gpsimd(h_words3[:], 3)
        scalar_unit(4)
        late = after_roots0([P, 2, CHUNK], F32, "late_squares", 64)
        square_by_vector(LAST, 0, late[:, 0, :])
        shared_bank = square_by_vector(LAST, 1, late[:, 1, :], halves[0])
        accs = multiply_chunk(0)
        for half in reversed(range(N // P)):
            store_half(accs, 0, half, nc.vector.tensor_copy)
        h_words4 = after_roots3([P, CHUNK, PACK], BF16, "h_words4", 0)
        interleave_by_vector(h_words4[:], 4)
        quantize_h(h_words3[:], 3)
        accs = multiply_chunk(1)
        quantize_h(h_words4[:], 4)

        nc.scalar.activation(late[:, 1, halves[1]], shared_bank[:, halves[1]], ACT.Square)
        scalar_unit(LAST, take_roots=False)
        for piece in LAST_PIECES:
            for t in range(PACK):
                root(LAST, t, piece)
        behind = None
        for index, piece in enumerate(LAST_PIECES):
            words = after_pieces([P, piece.stop - piece.start, PACK], BF16, "piece_words%d" % index, 8 * piece.start)
            interleave_by_vector(words[:], LAST, piece)
            if behind is not None:
                quantize_h(*behind)
            behind = (words[:], LAST, piece)
        quantize_h(*behind)
        for half in range(N // P):
            store_half(accs, 1, half, nc.scalar.copy)
        out_halves = out.rearrange("(h p) j -> p h j", p=P)
        first_col = (CHUNKS - 1) * CHUNK
        for piece in LAST_PIECES:
            width = piece.stop - piece.start
            bank = psum.tile([P, CHUNK], F32, name="piece_bank", tag="bank", bufs=BANKS)
            for b in range(HALVES):
                for half in range(N // P):
                    first, final = (b, half) == (0, 0), (b, half) == (HALVES - 1, N // P - 1)
                    last_pass(bank[:, half * width : (half + 1) * width], CHUNKS - 1, half, b, piece, first, final)
            if piece == LAST_PIECES[1]:
                result = after_pieces([P, (N // P) * width], F32, "first_result", 8 * LAST_PIECES[-1].start)
                nc.vector.tensor_copy(result[:], bank[:, 0 : (N // P) * width])
            else:
                result = result_tile((N // P) * width)
                nc.scalar.copy(result[:], bank[:, 0 : (N // P) * width])
            queue = nc.scalar if piece.stop == CHUNK else nc.sync
            queue.dma_start(
                out_halves[:, :, first_col + piece.start : first_col + piece.stop],
                result[:].rearrange("p (h j) -> p h j", j=width),
            )
